import numpy as np, ml_dtypes
CORES = [1,5,17,21,33,37,49,53]
N = 8
BF = ml_dtypes.bfloat16
def f(rng, *shape):
    return (rng.standard_normal(shape, dtype=np.float32) * np.exp2(rng.integers(-2, 3, shape[:-1] + (1,)))).astype(BF)
def wide(rng, *shape):
    v = f(rng, *shape).astype(np.float32); k = shape[:-2] + (1, shape[-1])
    return (v * np.exp2(rng.integers(-6, 7, k)) * (rng.random(k) > 0.0625)).astype(BF)
W, L, T, C, TH, SH = 4096, 192, 3, 5, 12, 12
def at(tab, a):
    return np.take_along_axis(tab, a.reshape(tab.shape[:-1] + (-1,)), -1).reshape(a.shape)
def tax(rng, key):
    term = np.argsort(key, axis=-1); gap = W - 1 - np.argsort(term, axis=-1)
    def up(lo, hi):
        v = np.where(rng.random((N, 8, W)) < 0.75, rng.random((1, 8, W)), rng.random((N, 8, W)))
        return np.take_along_axis(np.broadcast_to(term, (N, 8, W)), W - 1 - (gap * (lo + (hi - lo) * v)).astype(np.int64), 2)
    return term, gap, up(0.3, 0.7), up(0.05, 0.4)
def heights(rng, gap):
    h = (1.5 * (SH - np.log2(gap + 1.0))).astype(np.float32)[None, :, None, :]
    e = (h + rng.standard_normal((N, 8, 16, W), dtype=np.float32)) * np.exp2(rng.integers(-2, 3, (N, 8, 16, 1))).astype(np.float32)
    return e.reshape(N, 128, W).astype(BF)
def low(rng, term, n, top):
    return np.take_along_axis(np.broadcast_to(term, (N, 8, W)), rng.integers(0, top, (N, 8, n)), 2)
def lanes(rng, term, p0, p1):
    s = low(rng, term, 16 * L, W // 2).reshape(N, 8, 16, L)
    z = np.where(rng.random((N, 8, 16 * T * L)) < 0.1, low(rng, term, 16 * T * L, W), low(rng, term, 16 * T * L, W // 2)).reshape(N, 8, 16, T, L)
    kind = rng.integers(0, 8, (N, 8, 1, L))
    d = np.where(kind < 4, rng.integers(2, C + 1, s.shape), rng.integers(1, C + 1, s.shape)); d = np.where((kind < 3) & (rng.random(s.shape) < 0.1), 1, d)
    a = s
    for i in range(C):
        nx = at(p0, a)
        if i == 0: nx = np.where(rng.random(s.shape) < 0.4, at(p1, a), nx)
        a = np.where(d > i, nx, a)
    g = np.where(kind == 7, low(rng, term, 16 * L, W).reshape(s.shape), a)
    return s, g, z, (rng.random((N, 8, T, L)) < 0.4).astype(np.int64)
def pack(e, pa, s, g, z, sg):
    i4 = lambda v, *sh: np.ascontiguousarray(np.reshape(v, (N,) + sh)).astype(np.int32)
    return {"ev": np.reshape(e, (N, 128, W)).astype(BF), "par": i4(pa, 8, W), "s0": i4(s, 128, L), "g0": i4(g, 128, L), "z": i4(z, 128, T * L), "sg": i4(sg, 8, T * L)}
def setup_inputs(rng):
    term, gap, p0, p1 = tax(rng, rng.random((8, W)))
    return pack(heights(rng, gap), p0 + W * p1, *lanes(rng, term, p0, p1))
def setup_inputs_corners(rng):
    term, gap, p0, p1 = tax(rng, rng.random((8, W))); own = np.arange(W); c = rng.integers(0, 7, (1, 8, W))
    p0 = np.where(c == 0, own, np.where((c == 1) | (c == 4), W - 1, np.where((c == 2) | (c == 3), 0, p0)))
    p1 = np.where((c == 0) | (c == 3), own, np.where(c == 1, W - 1, np.where((c == 2) | (c == 4), 0, p1)))
    b = np.where(np.arange(N)[:, None, None] == 0, own, W - 1); p0 = np.where(c == 6, b, p0); p1 = np.where(c == 6, b, p1)
    for p in (p0, p1): p[:, ::2, W - 1] = W - 1; p[:, 1::2, W - 1] = 0
    e = heights(rng, gap).astype(np.float32); e[:, :, 0] = -256.0; e[:, :, W - 1] = 256.0
    s, g, z, sg = lanes(rng, term, p0, p1); one = (N, 8, 1, L)
    n = rng.choice(np.array([0, 0, 1, 4, 5, 16]), one); k = np.argsort(rng.random(s.shape), axis=2)
    g = np.where(rng.random(one) < 0.8, np.where(k < n, 0, W - 1), g)
    same = rng.random(one) < 0.2; s = np.where(same, s[:, :, :1], s); z = np.where(same[:, :, :, None], z[:, :, :1], z)
    g = np.where(rng.random(one) < 0.08, s, g); m = rng.integers(0, 8, (N, 8, 1, T, L))
    z = np.where(m == 0, s[:, :, :, None], np.where((m == 1) & (rng.random(z.shape) < 0.5), W - 1, np.where((m == 2) & (rng.random(z.shape) < 0.3), 0, z)))
    sg[0, :, 0] = 0; sg[1, :, 0] = 1; sg[2, :, 0] = 1; g[0] = W - 1
    for h in range(8):
        o = np.nonzero(c[0, h, 1:W - 1] == 0)[0] + 1; v = np.nonzero(c[0, h, 1:W - 1] == 6)[0] + 1
        s[0, h] = np.where(rng.random((1, L)) < 0.4, rng.choice(o, (16, L)), rng.choice(v, (16, L)))
        a, u = rng.permutation(v)[:2]; w = e[:, 16 * h:16 * h + 16]
        w[1:, :, a] = w[1:, :, u]; w[1, rng.permutation(16)[TH:], a] = -256.0
        j = np.append(rng.permutation(L - 1)[:L // 8], L - 1); i = rng.integers(0, 16, j.size)
        s[0, h, :, j] = rng.choice(o, (j.size, 16)); s[0, h, i, j] = a; z[0, h, i, 0, j] = u
    s[2, 7, :, L - 1] = rng.choice(o, 16); g[2, 7, :, L - 1] = W - 1; sg[2, 7, 0, L - 1] = 0
    for h in range(8):
        o = np.nonzero(c[0, h, 1:W - 1] == 0)[0] + 1; j = L if h < 7 else 1
        s[N - 1, h, :, :j] = rng.choice(o, (16, j)); g[N - 1, h, :, :j] = W - 1; sg[N - 1, h, 0] = 1; sg[N - 1, h, 0, :j] = 0
    return pack(e, p0 + W * p1, s, g, z, sg)
def setup_inputs_ends(rng):
    term, gap, p0, p1 = tax(rng, rng.random((8, W))); e = heights(rng, gap).astype(np.float32).reshape(N, 8, 16, W)
    cnt = rng.choice(np.array([0, 16, 8, 7, TH, TH - 1]), (N, 8, 1)); cnt[:, 0] = 16; cnt[:, 7] = 0
    v = np.where(np.argsort(rng.random((N, 8, 16)), axis=2) < cnt, 32.0, -32.0); v[:, 3] = 0.0
    e[..., 0] = v; e[..., W - 1] = -v
    pa = np.where(rng.random((N, 8, W)) < 0.85, (W * W - 1) * rng.integers(0, 2, (N, 8, W)), p0 + W * p1)
    kind = rng.integers(0, 5, (N, 8)); kind[:, 0] = 0; kind[:, 7] = 0; kind[N - 1] = 2
    pa[:, :, 0] = np.array([W * W - 1, 0, W * W - 1, 0, W - 1])[kind]; pa[:, :, W - 1] = np.array([0, W * W - 1, W * W - 1, 0, W * (W - 1)])[kind]
    def ends(*t):
        sh = (N, 8, 16) + t + (L,); one = (N, 8, 1) + t + (L,)
        x = np.where(rng.random(one) < 0.5, (W - 1) * rng.integers(0, 2, one), (W - 1) * rng.integers(0, 2, sh))
        return np.where((rng.random(one) < 0.25) & (rng.random(sh) < 0.5), rng.integers(0, W, sh), x)
    s = ends(); g = ends(); z = ends(T); sg = rng.integers(0, 2, (N, 8, T, L))
    x = (W - 1) * rng.integers(0, 2, (8, 16, L)); s[N - 1] = x; g[N - 1] = x; z[N - 1, :, :, 0] = x; sg[N - 1, :, 0] = 0; sg[1, :, 0] = 1
    s[:N - 1, 7, :, L - 3:] = 0; g[:N - 1, 7, :, L - 2:] = W - 1; g[:N - 1, 7, :, L - 3] = 0
    z[:N - 1, 7, :, 0, L - 3:] = W - 1; z[:N - 1, 7, :15, 0, L - 1] = 0; sg[:N - 1, 7, 0, L - 3:] = np.array([1, 0, 0])
    return pack(e, pa, s, g, z, sg)
def setup_inputs_spread(rng):
    c = rng.integers(-6, 7, (8, W)); term, gap, p0, p1 = tax(rng, c + rng.random((8, W)))
    w = np.abs(wide(rng, N, 128, W).astype(np.float32)).reshape(N, 8, 16, W) * np.exp2(2.0 * c).astype(np.float32)[None, :, None, :]
    w = np.where(rng.random((N, 8, 16, 1)) < 0.06, -w, w)
    return pack(w, p0 + W * p1, *lanes(rng, term, p0, p1))
def setup_inputs_ties(rng):
    term, gap, p0, p1 = tax(rng, rng.random((8, W))); q = W // 8; top = gap < q
    x = rng.integers(0, 4, (N, 8, 16, W)); x = np.where(top[None, :, None, :] & (rng.random(x.shape) < 0.75), 3, x)
    x[:, 5] = x[:, 5] // 2; x[:, 2] = 1
    u = np.take_along_axis(term[:, W - q:], rng.integers(0, q, (8, W)), 1)[None]
    p0 = np.where(rng.random((N, 8, W)) < 0.9, u, p0); p1 = np.where(rng.random((1, 8, W)) < 0.6, p0, p1)
    s, g, z, sg = lanes(rng, term, p0, p1); g = np.where(rng.random((N, 8, 1, L)) < 0.7, at(p0, s), g)
    return pack(x.astype(np.float32), p0 + W * p1, s, g, z, sg)
def check_inputs(d):
    bad = []
    for k, hi in (("par", W * W - 1), ("s0", W - 1), ("g0", W - 1), ("z", W - 1), ("sg", 1)):
        if np.min(d[k]) < 0 or np.max(d[k]) > hi: bad.append("range of " + k)
    e = d["ev"].astype(np.float32)
    if not np.all(np.isfinite(e)): bad.append("ev is not finite")
    if np.any((e != 0) & (np.abs(e) < np.float32(2.0 ** -126))): bad.append("ev holds subnormal numbers")
    return bad
def wits(tab, a):
    return np.take_along_axis(tab, a.reshape(8, 1, -1), 2).reshape(8, 16, 16, L)
def reference(ev, par, s0, g0, z, sg):
    e = ev.astype(np.float32).reshape(N, 8, 16, W); pa = par.astype(np.int64); p0 = pa & (W - 1); p1 = pa >> SH
    zs = z.astype(np.int64).reshape(N, 8, 16, T, L); plus = sg.reshape(N, 8, T, L) == 1
    S = s0.astype(np.int64).reshape(N, 8, 16, L); G = g0.astype(np.int64).reshape(N, 8, 16, L)
    ride = np.zeros((N, 8, L), bool); rz = np.zeros((N, 8, 16, L), np.int64)
    for t in range(T):
        for r in range(N):
            q = (r + t) % N; th = TH + (int(np.sum(ride[r])) & 1)
            x = np.where(ride[r][:, None], rz[r], zs[q, :, :, t]); pos = (plus[q, :, t] & ~ride[r])[:, None]
            ex = wits(e[q], x); g = G[r]; a = S[r]
            miss = np.sum(np.sum(wits(e[q], g) >= ex, axis=1) < th, axis=1)[:, None]
            for i in range(C):
                cov = np.sum(wits(e[q], a) >= ex, axis=1)
                nx = np.where(cov >= 8, at(p0[q], a), at(p1[q], a))
                stop = np.where(pos, cov >= th, nx == g)
                a = np.where(stop, a, nx)
            full = ~pos & (miss == 0); can = full & stop & (cov < th)
            win = np.argmin(np.where(can, cov, 99), axis=1)
            hit = can & (np.arange(16)[None, :, None] == win[:, None])
            S[r] = np.where(pos, a, S[r]); G[r] = np.where((pos & (miss > 4)) | hit, a, g)
            ride[r] = full[:, 0] & ~np.any(can, axis=1); rz[r] = x
    return {"ys": S.reshape(N, 128, L).astype(np.float32), "yg": G.reshape(N, 128, L).astype(np.float32)}

@@ -1,0 +1,552 @@
+import math
+from concourse.mybir import AluOpType, AxisListType, ActivationFunctionType
+
+A = AluOpType
+F = ActivationFunctionType
+NR, W, L, VIS, CL = 8, 4096, 192, 3, 5
+NCH = 3
+NL = L // NCH
+J = 16 * NL
+BIG = float(2 ** 22)
+LN2 = math.log(2.0)
+MIX = {"es": 0, "ecv": 2, "gat0": 4, "gat1": 4, "gat2": 5, "P": 38.0, "w": 2.0, "skew": 0.5, "slack": 0.02, "g": 1.5, "pe": 0.42, "hop": 0.08, "remote": 3.0, "noise": 0.0, "seed": 1,
+       "top": 60.0, "zero": 30.0, "th": 40.0, "gcov0": -5.0, "gcov1": -10.0, "gcov2": -20.0, "ch": -3.0, "tr0": 15.0, "tr1": 15.0, "tr2": 10.0, "tr3": 10.0, "tr4": 0.0, "nr": 3.0}
+
+ZM = ["PO", "TT", "MS", "G1", "G2", "CF", "NC", "W2", "UU", "SQ"] + ["E%d" % i for i in range(CL)] + ["F%d" % i for i in range(CL)]
+ZI_ = ["MI", "XI", "CI"]
+SCALED = {"IB": 1.0, "NIB": -1.0, "HA": 2.0 ** 97, "HB": -(2.0 ** 98), "I8K": 8192.0, "NHB": -BIG / 2, "NB": -BIG, "I16K": 16384.0, "I32B": 32.0}
+SEL = ["BOA", "BOF", "E8A", "E8F", "NIF"]
+
+SCRATCH = {
+    "EVB": ("sbuf", [128, W], "bfloat16"), "EC": ("sbuf", [128, 2 * W], "bfloat16"), "DT": ("sbuf", [128, 2 * W], "bfloat16"),
+    "PN": ("sbuf", [128, 256], "int32"), "PT": ("sbuf", [128, 16, 16], "int32"), "PF": ("sbuf", [128, 256], "float32"),
+    "TR": ("sbuf", [128, 256], "float32"), "TI": ("sbuf", [128, 256], "int32"), "TA": ("sbuf", [128, 512], "int32"),
+    "PL": ("sbuf", [128, 512], "uint16"),
+    "DGI": ("sbuf", [128, 1024], "int32"), "DGB": ("sbuf", [128, 1024], "bfloat16"),
+    "S0I": ("sbuf", [128, L], "int32"), "G0I": ("sbuf", [128, L], "int32"), "ZI": ("sbuf", [128, VIS * L], "int32"),
+    "SG8": ("sbuf", [128, VIS * L], "int32"), "SG8B": ("sbuf", [128, VIS * L], "bfloat16"), "SGB": ("sbuf", [128, VIS * L], "bfloat16"),
+    "ONE": ("sbuf", [128, 128], "float32"), "I32": ("sbuf", [128, 128], "float32"),
+    "ON16": ("sbuf", [128, 128], "float32"), "SEL": ("sbuf", [128, 128 * len(SEL)], "float32"), "SCN": ("sbuf", [128, 128 * len(SCALED)], "bfloat16"),
+    "BO": ("sbuf", [128, 128], "bfloat16"), "BOH": ("sbuf", [128, 128], "bfloat16"), "E8": ("sbuf", [128, 128], "bfloat16"),
+    "WK": ("sbuf", [128, 2048], "bfloat16"), "GC": ("sbuf", [128, NL], "bfloat16"),
+    "KI": ("sbuf", [128, 2], "int32"), "KB": ("sbuf", [128, 2], "float32"), "RS": ("sbuf", [128, 2], "float32"), "THI": ("sbuf", [128, 4], "int32"),
+    "VB": ("psum", [128, 512], "float32"), "PB": ("psum", [128, 512], "float32"),
+}
+for _t in range(VIS):
+    SCRATCH["ZU%d" % _t] = ("sbuf", [128, L], "uint16")
+    SCRATCH["TH%d" % _t] = ("sbuf", [128, 2], "float32")
+    if _t:
+        for _n, _d in (("ZR", "uint16"), ("ZF", "float32"), ("DZ", "float32"), ("NRL", "bfloat16"), ("NRS", "bfloat16")):
+            SCRATCH["%s%d" % (_n, _t)] = ("sbuf", [128, L], _d)
+SEMAPHORES = ["qV", "qS", "qT", "qG", "lsend", "zr1", "zr2"]
+for _c in range(NCH):
+    for _n, _k, _d in (("US", 2 * NL, "uint16"), ("IDX", NL, "uint16"), ("EX", J, "bfloat16"), ("CG", J, "bfloat16"), ("CM", J, "bfloat16"), ("DG", J, "bfloat16"),
+                       ("IH", 6 * NL, "float32"), ("SH", 6 * NL, "bfloat16"), ("CH", 6 * NL, "bfloat16"), ("MM", NL, "float32"),
+                       ("SM", NL * len(ZM), "bfloat16"), ("SI", NL * len(ZI_), "int32")):
+        SCRATCH["%s%d" % (_n, _c)] = ("sbuf", [128, _k], _d)
+    for _n in ("BC", "BM"):
+        SCRATCH["%s%d" % (_n, _c)] = ("psum", [128, 512], "float32")
+    for _t in range(VIS + 1):
+        SCRATCH["L%d_%d" % (_t, _c)] = ("sbuf", [128, 2 * NL], "float32")
+        if _t:
+            SCRATCH["X%d_%d" % (_t, _c)] = ("sbuf", [128, 2 * NL], "float32")
+            SEMAPHORES.append("aL%d_%d" % (_t, _c))
+            if _t < VIS:
+                SEMAPHORES.append("aN%d_%d" % (_t, _c))
+DMAS = ["PTa", "PTb", "PN", "EV", "Z0", "Z1", "S0", "G0", "SG", "D0", "D1", "D2", "D3"] + ["o%s%d" % (x, c) for x in "sg" for c in range(NCH)]
+SEMAPHORES += ["d_" + n for n in DMAS]
+PSUM = {n for n in SCRATCH if SCRATCH[n][0] == "psum" and n != "VB"}
+ACOL = 256
+CY = 0.00083
+
+
+def vc(n):
+    return max(64, n) * CY + 0.02
+
+
+def sc(n):
+    return max(64, n) * CY + 0.04
+
+
+def ga(n):
+    return 0.055 + n * CY * MIX["g"]
+
+
+def pc(cycles):
+    return cycles * MIX["pe"] * 1e-3 + 0.03
+
+
+def al(n, lo=0, hi=None):
+    if n in SCALED:
+        i = list(SCALED).index(n)
+        return ("SCN", i * 128, i * 128 + 128)
+    if n in SEL:
+        i = SEL.index(n)
+        return ("SEL", i * 128, i * 128 + 128)
+    return (n, lo, SCRATCH[n][1][-1] if hi is None else hi)
+
+
+def cst(T, n):
+    b, lo, hi = al(n)
+    return T[b][:, lo:hi]
+
+
+def zr(n, c):
+    b, l = ("SM", ZM) if n in ZM else ("SI", ZI_)
+    i = l.index(n)
+    return ("%s%d" % (b, c), i * NL, i * NL + NL)
+
+
+def z(T, n, c):
+    b, lo, hi = zr(n, c)
+    return T[b][:, lo:hi]
+
+
+def build():
+    ops = []
+
+    def op(q, cost, R, Wr, f, key, done=None, frm=None, bonus=""):
+        ops.append({"q": q, "cost": cost, "R": R, "W": Wr, "f": f, "key": key, "done": done, "frm": frm, "bonus": bonus})
+
+    def V(n, R, Wr, f, key, bonus=""):
+        op("V", vc(n), R, Wr, f, key, bonus=bonus)
+
+    def S(n, R, Wr, f, key, bonus=""):
+        op("S", sc(n), R, Wr, f, key, bonus=bonus)
+
+    def load(q, sem, R, Wr, f, cost, key=(-1, 0)):
+        op(q, cost, R, Wr, f, key, done="d_" + sem)
+
+    K0 = (-1, 0)
+    for y in range(2):
+        load("Y", "PT" + "ab"[y], [], [("PT", y, y + 1)], lambda g, T, x, y=y: g.sync.dma_start(T.PT[:, y:16:2, :], T.par[y:8:2, :]), 3.0)
+    load("S", "S0", [], [al("S0I")], lambda g, T, x: g.scalar.dma_start(T.S0I[:], T.s0[:]), 2.4)
+    load("S", "Z0", [], [al("ZI", 0, L)], lambda g, T, x: g.scalar.dma_start(T.ZI[:, 0:L], T.z[:, 0:L]), 2.4)
+    load("S", "G0", [], [al("G0I")], lambda g, T, x: g.scalar.dma_start(T.G0I[:], T.g0[:]), 2.6)
+    load("Y", "PN", [], [al("PN")], lambda g, T, x: g.sync.dma_start(T.PN[:], T.par[:]), 3.2)
+    load("Y", "EV", [], [al("EVB")], lambda g, T, x: g.sync.dma_start(T.EVB[:], T.ev[:]), 8.0)
+    load("S", "SG", [], [al("SG8")], lambda g, T, x: g.scalar.dma_start(T.SG8[0:8, :], T.sg[:]), 3.0)
+    load("Y", "Z1", [], [al("ZI", L, VIS * L)], lambda g, T, x: g.sync.dma_start(T.ZI[:, L:VIS * L], T.z[:, L:VIS * L]), 10.0, (0, 9))
+
+    V(128, [], [al("ONE")], lambda g, T, x: g.vector.memset(T.ONE[:], 1.0), K0, bonus="top")
+
+    def asel(o, i, pat, cmp, base, ch):
+        oa = lambda T: T.I32[:] if o == "I32" else cst(T, o)
+        ia = lambda T: T.ONE[:] if i == "ONE" else cst(T, i)
+        op("G", 0.4, [al(i)], [al(o)], lambda g, T, x: g.affine_select(oa(T), ia(T), pat, cmp, 0.0, base, ch), K0, bonus="top")
+    asel("I32", "ONE", [[-1, 128]], A.is_equal, 0, 1)
+    asel("BOA", "ONE", [[-16, 8], [0, 16]], A.is_ge, 0, 1)
+    asel("BOF", "BOA", [[16, 8], [0, 16]], A.is_ge, 15, -1)
+    asel("E8A", "ONE", [[1, 128]], A.is_ge, 0, -16)
+    asel("E8F", "E8A", [[-1, 128]], A.is_ge, 15, 16)
+    op("G", 7.0, [al("E8F"), al("BOF"), al("I32")], [al("DT", 0, W)], lambda g, T, x: g.iota(T.DT[:, 0:W], [[0, W]], 0, 0, allow_small_or_imprecise_dtypes=True), K0, bonus="zero")
+    op("G", 0.15, [], [al("KI", 0, 1)], lambda g, T, x: g.iota(T.KI[:, 0:1], [[0, 1]], 0, 1), K0)
+    V(1, [al("KI", 0, 1)], [al("KI", 1, 2)], lambda g, T, x: g.vector.tensor_scalar(T.KI[:, 1:2], T.KI[:, 0:1], 15, None, A.bitwise_and), (0, 8))
+    V(1, [al("KI", 1, 2)], [al("KB", 0, 1)], lambda g, T, x: g.vector.tensor_scalar(T.KB[:, 0:1], T.KI[:, 1:2], -LN2, 94.0 * LN2, A.mult, A.add), (0, 8))
+    V(2048, [], [al("DT", W, 2 * W)], lambda g, T, x: g.vector.memset(T.DT[:, W:2 * W], 0.0), K0)
+    for k in range(16):
+        S(128, [al("I32")], [al("WK", k * 128, k * 128 + 128)], lambda g, T, x, k=k: g.scalar.activation(T.WK[:, k * 128:k * 128 + 128], T.I32[:], F.Copy, scale=0.0), K0)
+    for k in range(16):
+        S(8, [al("BOF")], [al("WK", k * 128, k * 128 + 128)], lambda g, T, x, k=k: g.scalar.activation(
+            T.WK[:, k * 128 + k:k * 128 + 128:16], T.SEL[:, 128 + k:256:16], F.Copy), K0)
+    for n in SCALED:
+        S(128, [al("I32")], [al(n)], lambda g, T, x, n=n: g.scalar.activation(cst(T, n), T.I32[:], F.Copy, scale=SCALED[n]), K0)
+    S(128, [al("I32")], [al("NIF")], lambda g, T, x: g.scalar.activation(cst(T, "NIF"), T.I32[:], F.Copy, scale=-1.0), K0)
+    V(NL, [], [al("GC")], lambda g, T, x: g.vector.memset(T.GC[:], -(2.0 ** 97)), (0, 8))
+    S(128, [al("E8F")], [al("E8")], lambda g, T, x: g.scalar.activation(T.E8[:], cst(T, "E8F"), F.Copy), K0)
+    S(128, [al("BOF")], [al("BO")], lambda g, T, x: g.scalar.activation(T.BO[:], cst(T, "BOF"), F.Copy), K0)
+    S(128, [al("BOF")], [al("BOH")], lambda g, T, x: g.scalar.activation(T.BOH[:], cst(T, "BOF"), F.Copy, scale=0.5), K0)
+    V(128, [], [al("ON16")], lambda g, T, x: g.vector.memset(T.ON16[:], 0.0625), (0, 8))
+    V(1, [], [al("TH0", 0, 1)], lambda g, T, x: g.vector.memset(T.TH0[:, 0:1], 12.0), (0, 8))
+    V(1, [], [al("TH0", 1, 2)], lambda g, T, x: g.vector.memset(T.TH0[:, 1:2], -87.0), (0, 8))
+    for c in range(NCH):
+        V(NL, [], [al("CH%d" % c, 5 * NL)], lambda g, T, x, c=c: g.vector.memset(T["CH%d" % c][:, 5 * NL:6 * NL], 191.0), (0, 8))
+
+    V(L, [al("ZI", 0, L)], [al("ZU0")], lambda g, T, x: g.vector.tensor_copy(T.ZU0[:], T.ZI[:, 0:L]), K0)
+    V(256, [("PT", 0, 16)], [al("PF")], lambda g, T, x: g.vector.tensor_copy(T.PF[:], T.PT[:]), K0)
+    V(256, [al("PF")], [al("TR")], lambda g, T, x: g.vector.transpose(T.TR[:], T.PF[:]), K0)
+    for q3 in range(8):
+        V(32, [al("TR")], [("TI", q3, q3 + 1)], lambda g, T, x, q3=q3: g.vector.tensor_copy(T.TI[:, q3:256:8], T.TR[:, q3 * 32:q3 * 32 + 32]), K0)
+    V(256, [al("TI")], [al("TA", 0, 256)], lambda g, T, x: g.vector.tensor_scalar(T.TA[:, 0:256], T.TI[:], 4095, None, A.bitwise_and), K0)
+    V(256, [al("TI")], [al("TA", 256, 512)], lambda g, T, x: g.vector.tensor_scalar(T.TA[:, 256:512], T.TI[:], 12, None, A.logical_shift_right), K0)
+    for h in range(2):
+        V(256, [al("TA", h * 256, h * 256 + 256)], [al("PL", h * 256, h * 256 + 256)], lambda g, T, x, h=h: g.vector.tensor_copy(
+            T.PL[:, h * 256:h * 256 + 256], T.TA[:, h * 256:h * 256 + 256]), K0)
+    for b, (sh, m) in enumerate(((0, 4032), (0, 63), (12, 4032), (12, 63))):
+        lo, hi = b * 256, b * 256 + 256
+        if sh:
+            V(256, [al("PN")], [al("DGI", lo, hi)], lambda g, T, x, lo=lo, hi=hi, sh=sh, m=m: g.vector.tensor_scalar(
+                T.DGI[:, lo:hi], T.PN[:], sh, m, A.logical_shift_right, A.bitwise_and), (0, 5))
+        else:
+            V(256, [al("PN")], [al("DGI", lo, hi)], lambda g, T, x, lo=lo, hi=hi, m=m: g.vector.tensor_scalar(
+                T.DGI[:, lo:hi], T.PN[:], m, None, A.bitwise_and), (0, 5))
+    V(1024, [al("DGI")], [al("DGB")], lambda g, T, x: g.vector.tensor_copy(T.DGB[:], T.DGI[:]), (0, 5))
+    for b in range(4):
+        load("Y", "D%d" % b, [al("DGB", b * 256, b * 256 + 256)], [("DT", (b // 2) * W, (b // 2) * W + W)], lambda g, T, x, b=b: g.sync.dma_start(
+            T.DT[b % 2:128:16, (b // 2) * W:(b // 2) * W + W], T.DGB[:, b * 256:b * 256 + 256]), 2.5, (0, 5))
+    V(576, [al("SG8")], [al("SG8B")], lambda g, T, x: g.vector.tensor_copy(T.SG8B[0:8, :], T.SG8[0:8, :]), (0, 6))
+    for t in range(VIS):
+        op("T", 0.1, [al("E8"), al("SG8B")], [al("PB", 0, L)], lambda g, T, x, t=t: g.tensor.matmul(T.PB[:, 0:L], T.E8[0:8, :], T.SG8B[0:8, t * L:t * L + L], True, True), (t, 6))
+        S(L, [al("PB", 0, L)], [al("SGB", t * L, t * L + L)], lambda g, T, x, t=t: g.scalar.activation(T.SGB[:, t * L:t * L + L], T.PB[:, 0:L], F.Copy), (t, 6))
+    for b in range(4):
+        R = [al("EVB"), al("PL", b * 128, b * 128 + 128)]
+        Wr = [al("EC", b * 2048, b * 2048 + 2048)]
+        if b < MIX["ecv"]:
+            op("V", ga(2048), R, Wr, lambda g, T, x, b=b: g.vector.tensor_copy(
+                T.EC[:, b * 2048:b * 2048 + 2048], T.EVB[:, 0:W].indirect(T.PL[:, b * 128:b * 128 + 128])), (0, 4))
+        else:
+            op("S", ga(2048), R, Wr, lambda g, T, x, b=b: g.scalar.activation(
+                T.EC[:, b * 2048:b * 2048 + 2048], T.EVB[:, 0:W].indirect(T.PL[:, b * 128:b * 128 + 128]), F.Copy), (0, 4))
+
+    def fold16(bank, col, src):
+        def f(g, T, x):
+            for r in range(16):
+                y = g.tensor.matmul(T[bank][:, col:col + NL], T.WK[:, r * 128:r * 128 + 128], T[src][:, r:J:16], r == 0, r == 15)
+            return y
+        return f
+
+    def walk(t, c):
+        k = (t, c)
+        o, e = c * NL, "%d" % c
+        Ln, Un, ex, cm, cg, bank, dg, ix, zu = "L%d_%d" % (t, c), "US" + e, "EX" + e, "CM" + e, "CG" + e, "BC" + e, "DG" + e, "IDX" + e, "ZU%d" % t
+        vb = c * 2 * NL
+        if t == 0:
+            for h, n in enumerate(("S0I", "G0I")):
+                V(NL, [al(n, o, o + NL)], [al(Ln, h * NL, h * NL + NL)], lambda g, T, x, h=h, n=n: g.vector.tensor_copy(T[Ln][:, h * NL:h * NL + NL], T[n][:, o:o + NL]), k)
+            V(NL, [al("SGB", o, o + NL)], [zr("PO", c)], lambda g, T, x: g.vector.tensor_copy(z(T, "PO", c), T.SGB[:, o:o + NL]), k)
+        else:
+            nr, zf, dz = "NRL%d" % t, "ZF%d" % t, "DZ%d" % t
+            V(2 * NL, [al(nr, o, o + NL), al(dz, o, o + NL)], [al("VB", vb, vb + NL)], lambda g, T, x: g.vector.tensor_tensor(
+                T.VB[:, vb:vb + NL], T[dz][:, o:o + NL], T[nr][:, o:o + NL], A.mult), k)
+            V(NL, [al("VB", vb, vb + NL), al(zf, o, o + NL)], [al("VB", vb + NL, vb + 2 * NL)], lambda g, T, x: g.vector.tensor_tensor(
+                T.VB[:, vb + NL:vb + 2 * NL], T.VB[:, vb:vb + NL], T[zf][:, o:o + NL], A.add), k)
+            V(NL, [al("VB", vb + NL, vb + 2 * NL)], [al(zu, o, o + NL)], lambda g, T, x: g.vector.tensor_copy(T[zu][:, o:o + NL], T.VB[:, vb + NL:vb + 2 * NL]), k)
+            op("R", MIX["remote"], [al("X%d_%d" % (t, c))], [al(Ln)], None, k, done="aL%d_%d" % (t, c), frm=-1)
+            V(2 * NL, [al("SGB", t * L + o, t * L + o + NL), al(nr, o, o + NL)], [zr("PO", c)], lambda g, T, x: g.vector.tensor_tensor(
+                z(T, "PO", c), T.SGB[:, t * L + o:t * L + o + NL], T[nr][:, o:o + NL], A.mult), k)
+        V(2 * NL, [al(Ln)], [al(Un)], lambda g, T, x: g.vector.tensor_copy(T[Un][:], T[Ln][:]), k)
+        op("S", ga(J), [al("EVB"), al(zu, o, o + NL)], [al(ex)], lambda g, T, x: g.scalar.activation(T[ex][:], T.EVB[:, 0:W].indirect(T[zu][:, o:o + NL]), F.Copy), k)
+        op("V", ga(J), [al("EVB"), al(Un), al(ex)], [al(cm)], lambda g, T, x: g.vector.tensor_tensor(
+            T[cm][:], T.EVB[:, 0:W].indirect(T[Un][:, 0:NL]), T[ex][:], A.is_ge), k)
+        ih, ch, sh = "IH" + e, "CH" + e, "SH" + e
+        aw = (bank, ACOL, ACOL + NL)
+        for i in range(CL + 1):
+            lo, hi = i * NL, i * NL + NL
+            if i:
+                if i < CL:
+                    op("V", ga(J), [al("EC"), al(ix), al(ex)], [al(cm)], lambda g, T, x: g.vector.tensor_tensor(
+                        T[cm][:], T.EC[:, 0:2 * W].indirect(T[ix][:]), T[ex][:], A.is_ge), k)
+                op("S", ga(J), [al("DT"), al(ix)], [al(dg)], lambda g, T, x: g.scalar.activation(T[dg][:], T.DT[:, 0:2 * W].indirect(T[ix][:]), F.Copy), k)
+            if i < CL:
+                op("T", pc(J), [al("WK"), al(cm)], [al(bank, 0, NL)], fold16(bank, 0, cm), k)
+            if i:
+                op("T", pc(J), [al("WK"), al(dg)], [aw], fold16(bank, ACOL, dg), k)
+            if i == CL:
+                S(NL, [aw], [al(ih, lo, hi)], lambda g, T, x, lo=lo, hi=hi: g.scalar.activation(T[ih][:, lo:hi], T[bank][:, ACOL:ACOL + NL], F.Copy), k)
+                break
+            if i:
+                V(NL, [al(bank, 0, NL)], [al(sh, lo, hi)], lambda g, T, x, lo=lo, hi=hi: g.vector.tensor_scalar(T[sh][:, lo:hi], T[bank][:, 0:NL], 7.5, 4096.0, A.is_lt, A.mult), k)
+                V(NL, [aw, al(sh, lo, hi)], [al(ih, lo, hi)], lambda g, T, x, lo=lo, hi=hi: g.vector.tensor_tensor(
+                    T[ih][:, lo:hi], T[bank][:, ACOL:ACOL + NL], T[sh][:, lo:hi], A.add), k)
+            else:
+                V(NL, [al(bank, 0, NL)], [al("VB", vb, vb + NL)], lambda g, T, x: g.vector.tensor_scalar(T.VB[:, vb:vb + NL], T[bank][:, 0:NL], 7.5, 4096.0, A.is_lt, A.mult), k)
+                V(NL, [al("VB", vb, vb + NL), al(Ln, 0, NL)], [al(ih, lo, hi)], lambda g, T, x, lo=lo, hi=hi: g.vector.tensor_tensor(
+                    T[ih][:, lo:hi], T.VB[:, vb:vb + NL], T[Ln][:, 0:NL], A.add), k)
+            V(NL, [al(ih, lo, hi)], [al(ix)], lambda g, T, x, lo=lo, hi=hi: g.vector.tensor_copy(T[ix][:], T[ih][:, lo:hi]), k)
+            S(NL, [al(bank, 0, NL)], [al(ch, lo, hi)], lambda g, T, x, lo=lo, hi=hi, i=i: g.scalar.activation(
+                T[ch][:, lo:hi], T[bank][:, 0:NL], F.Identity, bias=32.0 * i), k, bonus="ch")
+
+    def epilogue(t, c):
+        k = (t, c)
+        e = "%d" % c
+        bm, th, Ln, ih, ch, mmn, sh = "BM" + e, "TH%d" % t, "L%d_%d" % (t, c), "IH" + e, "CH" + e, "MM" + e, "SH" + e
+        Un, ex, cg = "US" + e, "EX" + e, "CG" + e
+
+        def Z(n):
+            return zr(n, c)
+        bk = al(bm, 0, NL)
+        S(NL, [Z("PO"), al(th)], [Z("TT")], lambda g, T, x: g.scalar.activation(z(T, "TT", c), z(T, "PO", c), F.Identity, bias=99.0, scale=T[th][:, 1:2]), k)
+
+        def gates():
+            op("V", ga(J), [al("EVB"), al(Un), al(ex)], [al(cg)], lambda g, T, x: g.vector.tensor_tensor(
+                T[cg][:], T.EVB[:, 0:W].indirect(T[Un][:, NL:2 * NL]), T[ex][:], A.is_ge), k, bonus="gcov%d" % c)
+            op("T", pc(J), [al("WK"), al(cg)], [bk], fold16(bm, 0, cg), k)
+            V(NL, [bk, al(th)], [Z("MS")], lambda g, T, x: g.vector.tensor_scalar(z(T, "MS", c), T[bm][:, 0:NL], T[th][:, 0:1], None, A.is_lt), k)
+
+            def fr(g, T, x):
+                g.tensor.matmul(T[bm][:, 0:NL], T.BO[:], z(T, "MS", c), True, False)
+                return g.tensor.matmul(T[bm][:, 0:NL], cst(T, "I32B"), z(T, "PO", c), False, True)
+            op("T", pc(2 * NL), [al("BO"), al("I32B"), Z("MS"), Z("PO")], [bk], fr, k)
+            S(NL, [bk], [Z("G1")], lambda g, T, x: g.scalar.activation(z(T, "G1", c), T[bm][:, 0:NL], F.Sign, bias=-0.5), k)
+            S(NL, [bk], [Z("G2")], lambda g, T, x: g.scalar.activation(z(T, "G2", c), T[bm][:, 0:NL], F.Sign, bias=-36.5), k)
+        for i in range(CL):
+            if i == MIX["gat%d" % c]:
+                gates()
+            s0, s1 = slice(i * NL, i * NL + NL), slice((i + 1) * NL, (i + 2) * NL)
+            En, Fn, tb = "E%d" % i, "F%d" % i, "tr%d" % i
+
+            def fy(g, T, x, s0=s0, s1=s1, es=i < MIX["es"]):
+                g.tensor.matmul(T[bm][:, NL:2 * NL], cst(T, "IB"), T[ch][:, s0], True, False)
+                g.tensor.matmul(T[bm][:, NL:2 * NL], cst(T, "NIB"), z(T, "TT", c), False, True)
+                g.tensor.matmul(T[bm][:, 0:NL], T.I32[:], T[ih][:, s1], True, False)
+                if s1.start < CL * NL:
+                    g.tensor.matmul(T[bm][:, 0:NL], cst(T, "NIB"), T[sh][:, s1], False, False)
+                if es:
+                    g.tensor.matmul(T[bm][:, 0:NL], cst(T, "NIF"), T[Ln][:, NL:2 * NL], False, False)
+                return g.tensor.matmul(T[bm][:, 0:NL], cst(T, "I16K"), z(T, "PO", c), False, True)
+            last = i == CL - 1
+            es = i < MIX["es"]
+            op("T", pc((7 if last else 8) * NL + (4 * NL if es else 0)), [al("I32"), al("I16K"), al("IB"), al("NIB"), al(ih, s1.start, s1.stop), Z("PO"), al(ch, s0.start, s0.stop), Z("TT")]
+               + ([] if last else [al(sh, s1.start, s1.stop)]) + ([al("NIF"), al(Ln, NL, 2 * NL)] if es else []), [al(bm, 0, 2 * NL)], fy, k, bonus=tb)
+            if es:
+                S(NL, [bk], [Z("SQ")], lambda g, T, x: g.scalar.activation(z(T, "SQ", c), T[bm][:, 0:NL], F.Square), k, bonus=tb)
+                S(NL, [al(bm, NL, 2 * NL)], [Z(Fn)], lambda g, T, x, Fn=Fn, i=i: g.scalar.activation(z(T, Fn, c), T[bm][:, NL:2 * NL], F.Sign, bias=0.5 - 32.0 * i), k, bonus=tb)
+                S(NL, [Z("SQ")], [Z(En)], lambda g, T, x, En=En: g.scalar.activation(z(T, En, c), z(T, "SQ", c), F.Relu, bias=1.0, scale=-1.0), k, bonus=tb)
+            else:
+                V(NL, [bk, al(Ln, NL, 2 * NL)], [Z(En)], lambda g, T, x, En=En: g.vector.tensor_tensor(z(T, En, c), T[bm][:, 0:NL], T[Ln][:, NL:2 * NL], A.is_equal), k, bonus=tb)
+                S(NL, [al(bm, NL, 2 * NL)], [Z(Fn)], lambda g, T, x, Fn=Fn, i=i: g.scalar.activation(z(T, Fn, c), T[bm][:, NL:2 * NL], F.Sign, bias=0.5 - 32.0 * i), k, bonus=tb)
+
+            def fw(g, T, x, s0=s0, s1=s1, En=En, Fn=Fn, last=last):
+                if last:
+                    g.tensor.matmul(T[bm][:, NL:2 * NL], T.I32[:], T[ih][:, s1], True, False)
+                    g.tensor.matmul(T[bm][:, NL:2 * NL], cst(T, "I8K"), T[ch][:, s1], False, True)
+                g.tensor.matmul(T[bm][:, 0:NL], T.I32[:], T[ih][:, s0], True, False)
+                g.tensor.matmul(T[bm][:, 0:NL], cst(T, "I8K"), T[ch][:, s0], False, False)
+                g.tensor.matmul(T[bm][:, 0:NL], cst(T, "NHB"), z(T, Fn, c), False, False)
+                return g.tensor.matmul(T[bm][:, 0:NL], cst(T, "NB"), z(T, En, c), False, True)
+            op("T", pc((12 if last else 7) * NL), [al("I32"), al("I8K"), al("NHB"), al("NB"), al(ih, s0.start, s1.stop), al(ch, s0.start, s1.stop if last else s0.stop), Z(En), Z(Fn)],
+               [al(bm, 0, 2 * NL)], fw, k, bonus=tb)
+            if i == 0:
+                V(NL, [bk], [al(mmn)], lambda g, T, x: g.vector.tensor_copy(T[mmn][:], T[bm][:, 0:NL]), k, bonus=tb)
+            else:
+                for j in range(2 if last else 1):
+                    V(NL, [al(bm, j * NL, j * NL + NL), al(mmn)], [al(mmn)], lambda g, T, x, j=j: g.vector.tensor_tensor(
+                        T[mmn][:], T[bm][:, j * NL:j * NL + NL], T[mmn][:], A.min), k, bonus=tb)
+        if MIX["gat%d" % c] == CL:
+            gates()
+        V(NL, [al(mmn)], [Z("MI")], lambda g, T, x: g.vector.tensor_copy(z(T, "MI", c), T[mmn][:]), k)
+        V(NL, [Z("MI")], [Z("CI")], lambda g, T, x: g.vector.tensor_scalar(z(T, "CI", c), z(T, "MI", c), 13, 31, A.arith_shift_right, A.bitwise_and), k)
+        V(NL, [Z("CI"), al(th)], [Z("NC")], lambda g, T, x: g.vector.tensor_scalar(z(T, "NC", c), z(T, "CI", c), T[th][:, 0:1], 64.0, A.is_ge, A.mult), k)
+        V(NL, [Z("CI")], [Z("CF")], lambda g, T, x: g.vector.tensor_copy(z(T, "CF", c), z(T, "CI", c)), k)
+        V(NL, [Z("MI")], [Z("XI")], lambda g, T, x: g.vector.tensor_scalar(z(T, "XI", c), z(T, "MI", c), 4095, None, A.bitwise_and), k)
+
+        def fc(g, T, x):
+            if t + 1 < VIS:
+                bq = T[bm][:, NL:2 * NL]
+                g.tensor.matmul(bq, cst(T, "IB"), T.GC[:], True, False)
+                g.tensor.matmul(bq, cst(T, "HA"), z(T, "G1", c), False, False)
+                g.tensor.matmul(bq, cst(T, "HB"), z(T, "G2", c), False, False)
+                g.tensor.matmul(bq, T.BO[:], z(T, "NC", c), False, True)
+            g.tensor.matmul(T[bm][:, 0:NL], cst(T, "IB"), z(T, "NC", c), True, False)
+            return g.tensor.matmul(T[bm][:, 0:NL], cst(T, "IB"), z(T, "CF", c), False, True)
+        op("T", pc((2 if t + 1 == VIS else 6) * NL), [al("IB"), al("BO"), al("GC"), al("HA"), al("HB"), Z("G1"), Z("G2"), Z("CF"), Z("NC")], [al(bm, 0, 2 * NL)], fc, k)
+        o = c * NL
+        if t + 1 < VIS:
+            ns, nl = "NRS%d" % (t + 1), "NRL%d" % (t + 1)
+            V(NL, [al(bm, NL, 2 * NL)], [al(ns, o, o + NL)], lambda g, T, x: g.vector.tensor_scalar(T[ns][:, o:o + NL], T[bm][:, NL:2 * NL], 1024.0, None, A.not_equal), k, bonus="nr")
+            op("G", 0.1, [al(ns, o, o + NL)], [], lambda g, T, x: x["send"](T[nl][:, o:o + NL], T[ns][:, o:o + NL], "aN%d_%d" % (t + 1, c), "next"), k)
+            op("R", MIX["remote"], [al(ns, o, o + NL)], [al(nl, o, o + NL)], None, k, done="aN%d_%d" % (t + 1, c), frm=-1)
+        S(NL, [bk, al("KB", 0, 1)], [Z("W2")], lambda g, T, x: g.scalar.activation(z(T, "W2", c), T[bm][:, 0:NL], F.Exp, bias=T.KB[:, 0:1], scale=-16.0 * LN2), k)
+
+        def fs(g, T, x):
+            g.tensor.matmul(T[bm][:, 0:NL], cst(T, "IB"), T.GC[:], True, False)
+            g.tensor.matmul(T[bm][:, 0:NL], cst(T, "HA"), z(T, "G1", c), False, False)
+            g.tensor.matmul(T[bm][:, 0:NL], cst(T, "HB"), z(T, "G2", c), False, False)
+            return g.tensor.matmul(T[bm][:, 0:NL], T.BOH[:], z(T, "W2", c), False, True)
+        op("T", pc(4 * NL), [al("IB"), al("GC"), al("HA"), al("HB"), al("BOH"), Z("G1"), Z("G2"), Z("W2")], [bk], fs, k)
+        vb = c * 2 * NL
+        r0, r1 = (vb, vb + NL), (vb + NL, vb + 2 * NL)
+        Xn = "X%d_%d" % (t + 1, c)
+
+        def vt(in0, in1, out, alu, R, Wr):
+            V(NL, R, Wr, lambda g, T, x: g.vector.tensor_tensor(out(T), in0(T), in1(T), alu), k)
+
+        def vbs(r):
+            return lambda T: T.VB[:, r[0]:r[1]]
+        V(NL, [Z("XI")], [al("VB", *r0)], lambda g, T, x: g.vector.tensor_copy(T.VB[:, r0[0]:r0[1]], z(T, "XI", c)), k)
+        lS, lG = (lambda T: T[Ln][:, 0:NL]), (lambda T: T[Ln][:, NL:2 * NL])
+        vt(vbs(r0), lS, vbs(r1), A.subtract, [al("VB", *r0), al(Ln, 0, NL)], [al("VB", *r1)])
+        vt(vbs(r0), lG, vbs(r0), A.subtract, [al("VB", *r0), al(Ln, NL, 2 * NL)], [al("VB", *r0)])
+        vt(vbs(r1), lambda T: z(T, "PO", c), vbs(r1), A.mult, [al("VB", *r1), Z("PO")], [al("VB", *r1)])
+        vt(vbs(r1), lS, lambda T: T[Xn][:, 0:NL], A.add, [al("VB", *r1), al(Ln, 0, NL)], [al(Xn, 0, NL)])
+        V(NL, [bk, Z("W2")], [Z("UU")], lambda g, T, x: g.vector.tensor_tensor(z(T, "UU", c), T[bm][:, 0:NL], z(T, "W2", c), A.is_lt), k)
+        vt(vbs(r0), lambda T: z(T, "UU", c), vbs(r0), A.mult, [al("VB", *r0), Z("UU")], [al("VB", *r0)])
+        vt(vbs(r0), lG, lambda T: T[Xn][:, NL:2 * NL], A.add, [al("VB", *r0), al(Ln, NL, 2 * NL)], [al(Xn, NL, 2 * NL)])
+        if t + 1 < VIS:
+            op("G", 0.1, [al(Xn)], [], lambda g, T, x: x["send"](T["L%d_%d" % (t + 1, c)][:], T[Xn][:], "aL%d_%d" % (t + 1, c), "next"), k)
+        else:
+            H = "L%d_%d" % (VIS, c)
+            op("G", 0.1, [al(Xn)], [], lambda g, T, x: x["send"](T[H][:], T[Xn][:], "aL%d_%d" % (VIS, c), "home"), k)
+            op("R", MIX["remote"], [al(Xn)], [al(H)], None, k, done="aL%d_%d" % (VIS, c), frm=2)
+            load("Y", "os%d" % c, [al(H)], [], lambda g, T, x: g.sync.dma_start(T.ys[:, o:o + NL], T[H][:, 0:NL]), 2.0, k)
+            load("S", "og%d" % c, [al(H)], [], lambda g, T, x: g.scalar.dma_start(T.yg[:, o:o + NL], T[H][:, NL:2 * NL]), 2.0, k)
+
+    def zsend(t):
+        u = t + 1
+        op("G", 0.1, [al("ZU%d" % t)], [], lambda g, T, x: x["send"](T["ZR%d" % u][:], T["ZU%d" % t][:], "zr%d" % u, "next"), (t, 5))
+        op("R", MIX["remote"], [al("ZU%d" % t)], [al("ZR%d" % u)], None, (t, 5), done="zr%d" % u, frm=-1)
+        V(L, [al("ZR%d" % u)], [al("ZF%d" % u)], lambda g, T, x: g.vector.tensor_copy(T["ZF%d" % u][:], T["ZR%d" % u][:]), (t, 5))
+        V(2 * L, [al("ZF%d" % u), al("ZI", u * L, u * L + L)], [al("DZ%d" % u)], lambda g, T, x: g.vector.tensor_tensor(
+            T["DZ%d" % u][:], T.ZI[:, u * L:u * L + L], T["ZF%d" % u][:], A.subtract), (t, 5))
+
+    def thresh(t):
+        n, th = "NRL%d" % t, "TH%d" % t
+        b = "th"
+        V(L, [al(n)], [al("RS", 0, 1)], lambda g, T, x: g.vector.tensor_reduce(T.RS[:, 0:1], T[n][:], AxisListType.X, A.add), (t, 0), bonus=b)
+        op("T", 0.15, [al("ON16"), al("RS", 0, 1)], [al("PB", 0, 1)], lambda g, T, x: g.tensor.matmul(T.PB[:, 0:1], T.ON16[:], T.RS[:, 0:1], True, True), (t, 0), bonus=b)
+        V(1, [al("PB", 0, 1)], [al("THI", 0, 1)], lambda g, T, x: g.vector.tensor_copy(T.THI[:, 0:1], T.PB[:, 0:1]), (t, 0), bonus=b)
+        V(1, [al("THI", 0, 1)], [al("THI", 1, 2)], lambda g, T, x: g.vector.tensor_scalar(T.THI[:, 1:2], T.THI[:, 0:1], 1, None, A.bitwise_and), (t, 0), bonus=b)
+        for j, v in ((0, 12.0), (1, -87.0)):
+            V(1, [al("THI", 1, 2)], [al(th, j, j + 1)], lambda g, T, x, j=j, v=v: g.vector.tensor_scalar(T[th][:, j:j + 1], T.THI[:, 1:2], v, None, A.add), (t, 0), bonus=b)
+
+    zsend(0)
+    for t in range(VIS):
+        for c in range(NCH):
+            walk(t, c)
+        if t:
+            if t + 1 < VIS:
+                zsend(t)
+            thresh(t)
+        for c in range(NCH):
+            epilogue(t, c)
+    return ops
+
+
+def depend(ops):
+    acc, bank = {}, {}
+    for n, o in enumerate(ops):
+        o["hard"], o["soft"] = set(), set()
+        for wr, regs in ((0, o["R"]), (1, o["W"])):
+            for b, lo, hi in regs:
+                for (m, w2, l2, h2) in acc.get(b, ()):
+                    if m != n and (wr or w2) and lo < h2 and l2 < hi:
+                        if wr and not w2 and ops[m]["q"] == o["q"] and not ops[m]["done"]:
+                            o["soft"].add(m)
+                        else:
+                            o["hard"].add(m)
+                if b in PSUM:
+                    for q, m in bank.get(b, {}).items():
+                        if m != n:
+                            (o["soft"] if q == o["q"] else o["hard"]).add(m)
+        for wr, regs in ((0, o["R"]), (1, o["W"])):
+            for b, lo, hi in regs:
+                if wr:
+                    acc[b] = [a for a in acc.get(b, []) if not (lo <= a[2] and a[3] <= hi and a[0] != n)] + [(n, 1, lo, hi)]
+                else:
+                    acc.setdefault(b, []).append((n, 0, lo, hi))
+                if b in PSUM:
+                    bank.setdefault(b, {})[o["q"]] = n
+    return ops
+
+
+def schedule(ops):
+    n = len(ops)
+    succ = [[] for _ in range(n)]
+    for i, o in enumerate(ops):
+        for m in o["hard"] | o["soft"]:
+            succ[m].append(i)
+    bot = [0.0] * n
+    hop = MIX["hop"]
+    for i in range(n - 1, -1, -1):
+        bot[i] = ops[i]["cost"] + max([bot[s] + hop for s in succ[i]], default=0.0)
+    own = [0.0] * n
+    for i in range(n - 1, -1, -1):
+        own[i] = ops[i]["cost"] + max([own[s] + hop for s in succ[i] if ops[s]["key"] == ops[i]["key"]], default=0.0)
+    pri = []
+    for i in range(n):
+        b, (t, c) = ops[i]["bonus"], ops[i]["key"]
+        if c >= NCH or t < 0:
+            due = MIX["P"] * (t + 1) - bot[i]
+        else:
+            due = MIX["P"] * (t + 1) + MIX["skew"] * c - MIX["w"] * own[i]
+        pri.append((MIX.get(b, 0.0) if b else 0.0) - due + MIX["noise"] * ((i * 7919 + MIX["seed"] * 104729) % 1009) / 1009.0)
+    need = [len(o["hard"] | o["soft"]) for o in ops]
+    ready = [0.0] * n
+    cand = {}
+    for i in range(n):
+        if not need[i]:
+            cand.setdefault(ops[i]["q"], []).append(i)
+    free, order, end = {}, [], [0.0] * n
+    start = [0.0] * n
+    while True:
+        best = None
+        for q, l in cand.items():
+            if not l:
+                continue
+            f = free.get(q, 0.0) if q != "R" else 0.0
+            lo = min(max(f, ready[i]) for i in l)
+            i = max((j for j in l if max(f, ready[j]) <= lo + MIX["slack"]), key=lambda j: (pri[j], -j))
+            s = max(f, ready[i])
+            if best is None or s < best[0]:
+                best = (s, i, q)
+        if best is None:
+            break
+        s, i, q = best
+        o = ops[i]
+        cand[q].remove(i)
+        order.append(i)
+        start[i] = s
+        end[i] = s + o["cost"]
+        free[q] = s + (0.1 if o["done"] else o["cost"])
+        for j in succ[i]:
+            need[j] -= 1
+            ready[j] = max(ready[j], end[i] + (hop if ops[j]["q"] != q else hop / 2) if i in ops[j]["hard"] else s)
+            if not need[j]:
+                cand.setdefault(ops[j]["q"], []).append(j)
+    return order, start, end
+
+
+def rank_program(g, core, T, topo):
+    rank = T.rank_of(core)
+    if rank is None:
+        return
+    ops = depend(build())
+    order, _, _ = schedule(ops)
+    place = {i: n for n, i in enumerate(order)}
+    cores = T.cores
+    to = {"next": cores[(rank + 1) % NR], "home": cores[(rank - 2) % NR]}
+    sent = [0]
+
+    def send(out, src, sem, where):
+        dst = to[where]
+        rid, pid, _ = topo.addr(dst)
+        sent[0] += len(topo.engines(core, dst))
+        return g.remote_dma(out_ap=out, in_ap=src, remote_sem=T.sem[sem], local_sem=T.sem["lsend"], pid=pid, routing_id=rid, dma_engine_mask=topo.mask(core, dst))
+
+    x = {"send": send}
+    eng = {"V": g.vector, "S": g.scalar, "T": g.tensor, "G": g, "Y": g.sync}
+    count = {q: 0 for q in eng}
+    know = {q: {} for q in eng}
+    tok, clock, sems = {}, {}, {}
+    for i in order:
+        o = ops[i]
+        q = o["q"]
+        if q == "R":
+            src = cores[(rank + o["frm"]) % NR]
+            tok[i] = (o["done"], len(topo.engines(src, core)))
+            clock[i] = {}
+            sems[o["done"]] = tok[i][1]
+            continue
+        for m in sorted((m for m in o["hard"] if m in tok), key=lambda m: -place[m]):
+            s, v = tok[m]
+            if know[q].get(s, 0) < v:
+                eng[q].wait_ge(T.sem[s], v)
+                know[q][s] = v
+                for a, b in clock[m].items():
+                    if know[q].get(a, 0) < b:
+                        know[q][a] = b
+        ins = o["f"](g, T, x)
+        clock[i] = dict(know[q])
+        if o["done"]:
+            ins.then_inc(T.sem[o["done"]], 16)
+            tok[i] = (o["done"], 16)
+            sems[o["done"]] = 16
+        elif o["W"]:
+            count[q] += 1
+            ins.then_inc(T.sem["q" + q], 1)
+            tok[i] = ("q" + q, count[q])
+            sems["q" + q] = count[q]
+    for s, v in sems.items():
+        if know["G"].get(s, 0) < v:
+            g.wait_ge(T.sem[s], v)
+    g.wait_ge(T.sem["lsend"], sent[0])

@@ -1,5 +1,5 @@
 import math
-from concourse.mybir import AluOpType, AxisListType, ActivationFunctionType
+from concourse.mybir import AluOpType, ActivationFunctionType
 
 A = AluOpType
 F = ActivationFunctionType
@@ -7,61 +7,69 @@ NR, W, L, VIS, CL = 8, 4096, 192, 3, 5
 NCH = 3
 NL = L // NCH
 J = 16 * NL
-BIG = float(2 ** 22)
 LN2 = math.log(2.0)
-MIX = {"es": 0, "ecv": 2, "gat0": 4, "gat1": 4, "gat2": 5, "P": 38.0, "w": 2.0, "skew": 0.5, "slack": 0.02, "g": 1.5, "pe": 0.42, "hop": 0.08, "remote": 3.0, "noise": 0.0, "seed": 1,
-       "top": 60.0, "zero": 30.0, "th": 40.0, "gcov0": -5.0, "gcov1": -10.0, "gcov2": -20.0, "ch": -3.0, "tr0": 15.0, "tr1": 15.0, "tr2": 10.0, "tr3": 10.0, "tr4": 0.0, "nr": 3.0}
+H = 16384.0
+KG = 2.0 ** 104
+U = 2.0 ** -20
+MAGIC = 768.0
+TAU = (1.5 * 2.0 ** -104, 1.5 * 2.0 ** -121)
+MIX = {'ecv': 2, 'gat': (4, 2, 2), 'g': 1.5, 'pe': 0.42, 'hop': 0.2, 'same': 0.15, 'remote': 3.0, 'slack': 0.2, 'skew': (1.0, 1.0, 1.0), 'small': 4.0, 'gcov': (0.0, -10.0, -20.0), 'top': 60.0, 'th': 10.0, 'idx': 5.0, 'ge': 0.0, 'slackV': 0.1, 'slackS': 0.1}
 
-ZM = ["PO", "TT", "MS", "G1", "G2", "CF", "NC", "W2", "UU", "SQ"] + ["E%d" % i for i in range(CL)] + ["F%d" % i for i in range(CL)]
-ZI_ = ["MI", "XI", "CI"]
-SCALED = {"IB": 1.0, "NIB": -1.0, "HA": 2.0 ** 97, "HB": -(2.0 ** 98), "I8K": 8192.0, "NHB": -BIG / 2, "NB": -BIG, "I16K": 16384.0, "I32B": 32.0}
-SEL = ["BOA", "BOF", "E8A", "E8F", "NIF"]
+ZB = ["PO", "SR", "MS", "Q2", "SC", "W2", "SU"]
+ZF = ["RR", "T1", "T2"]
+ZI_ = ["MI", "AI"]
+SCALED = {"IB": 1.0, "IH": 0.5, "IU": U, "N64": -64.0, "N128": -128.0, "HI": H, "NHI": -H, "HH": H / 2, "NHH": -H / 2, "H32": 32 * H}
+BLOCK = {"BO": 1.0, "NBH": -H / 2}
+MATS = list(SCALED) + list(BLOCK) + ["KK", "TB", "E8"]
+SEL = ["I32", "BOA", "BOF", "E8A", "E8F", "NIF", "I14", "I52"]
+CONST = {"C1": 1.0, "C37": -37.0, "C45": -45.0, "CM": MAGIC}
+CONST.update({"O%d" % i: -0.75 * i for i in range(1, CL + 1)})
 
 SCRATCH = {
-    "EVB": ("sbuf", [128, W], "bfloat16"), "EC": ("sbuf", [128, 2 * W], "bfloat16"), "DT": ("sbuf", [128, 2 * W], "bfloat16"),
+    "EVB": ("sbuf", [128, VIS * W], "bfloat16"), "EC": ("sbuf", [128, 2 * W], "bfloat16"), "DT": ("sbuf", [128, 2 * W], "bfloat16"),
     "PN": ("sbuf", [128, 256], "int32"), "PT": ("sbuf", [128, 16, 16], "int32"), "PF": ("sbuf", [128, 256], "float32"),
     "TR": ("sbuf", [128, 256], "float32"), "TI": ("sbuf", [128, 256], "int32"), "TA": ("sbuf", [128, 512], "int32"),
     "PL": ("sbuf", [128, 512], "uint16"),
     "DGI": ("sbuf", [128, 1024], "int32"), "DGB": ("sbuf", [128, 1024], "bfloat16"),
-    "S0I": ("sbuf", [128, L], "int32"), "G0I": ("sbuf", [128, L], "int32"), "ZI": ("sbuf", [128, VIS * L], "int32"),
-    "SG8": ("sbuf", [128, VIS * L], "int32"), "SG8B": ("sbuf", [128, VIS * L], "bfloat16"), "SGB": ("sbuf", [128, VIS * L], "bfloat16"),
-    "ONE": ("sbuf", [128, 128], "float32"), "I32": ("sbuf", [128, 128], "float32"),
-    "ON16": ("sbuf", [128, 128], "float32"), "SEL": ("sbuf", [128, 128 * len(SEL)], "float32"), "SCN": ("sbuf", [128, 128 * len(SCALED)], "bfloat16"),
-    "BO": ("sbuf", [128, 128], "bfloat16"), "BOH": ("sbuf", [128, 128], "bfloat16"), "E8": ("sbuf", [128, 128], "bfloat16"),
-    "WK": ("sbuf", [128, 2048], "bfloat16"), "GC": ("sbuf", [128, NL], "bfloat16"),
-    "KI": ("sbuf", [128, 2], "int32"), "KB": ("sbuf", [128, 2], "float32"), "RS": ("sbuf", [128, 2], "float32"), "THI": ("sbuf", [128, 4], "int32"),
-    "VB": ("psum", [128, 512], "float32"), "PB": ("psum", [128, 512], "float32"),
+    "SGI": ("sbuf", [128, NCH, 2, NL], "int32"), "ZI": ("sbuf", [128, VIS * L], "int32"), "ZO": ("sbuf", [128, VIS * L], "float32"),
+    "SG8": ("sbuf", [128, VIS * L], "int32"), "SG8B": ("sbuf", [128, VIS * L], "bfloat16"),
+    "ONE": ("sbuf", [128, 128], "float32"), "ON32": ("sbuf", [128, 128], "float32"),
+    "SEL": ("sbuf", [128, 128 * len(SEL)], "float32"), "SCN": ("sbuf", [128, 128 * len(MATS)], "bfloat16"),
+    "ZK": ("sbuf", [128, 144], "bfloat16"), "CT": ("sbuf", [128, NL * len(CONST)], "bfloat16"),
+    "KI": ("sbuf", [128, 2], "int32"), "KB": ("sbuf", [128, 2], "float32"), "THI": ("sbuf", [128, 2], "int32"), "NP": ("sbuf", [128, 2], "float32"),
+    "US": ("sbuf", [128, 2 * L], "uint16"), "ZU": ("sbuf", [128, L], "uint16"),
+    "PB": ("psum", [128, 512], "float32"),
 }
-for _t in range(VIS):
-    SCRATCH["ZU%d" % _t] = ("sbuf", [128, L], "uint16")
-    SCRATCH["TH%d" % _t] = ("sbuf", [128, 2], "float32")
+for _t in range(VIS + 1):
+    SCRATCH["L%d" % _t] = ("sbuf", [128, 2 * L], "float32")
     if _t:
-        for _n, _d in (("ZR", "uint16"), ("ZF", "float32"), ("DZ", "float32"), ("NRL", "bfloat16"), ("NRS", "bfloat16")):
-            SCRATCH["%s%d" % (_n, _t)] = ("sbuf", [128, L], _d)
-SEMAPHORES = ["qV", "qS", "qT", "qG", "lsend", "zr1", "zr2"]
+        SCRATCH["X%d" % _t] = ("sbuf", [128, 2 * L], "float32")
+    if _t < VIS:
+        SCRATCH["TH%d" % _t] = ("sbuf", [128, 4], "float32")
+    if 0 < _t < VIS:
+        for _n in ("ZX", "ZS", "ZF"):
+            SCRATCH["%s%d" % (_n, _t)] = ("sbuf", [128, L], "float32")
+        SCRATCH["RS%d" % _t] = ("sbuf", [128, 4], "float32")
+SEMAPHORES = ["qV", "qS", "qT", "qG", "lsend"]
 for _c in range(NCH):
-    for _n, _k, _d in (("US", 2 * NL, "uint16"), ("IDX", NL, "uint16"), ("EX", J, "bfloat16"), ("CG", J, "bfloat16"), ("CM", J, "bfloat16"), ("DG", J, "bfloat16"),
-                       ("IH", 6 * NL, "float32"), ("SH", 6 * NL, "bfloat16"), ("CH", 6 * NL, "bfloat16"), ("MM", NL, "float32"),
-                       ("SM", NL * len(ZM), "bfloat16"), ("SI", NL * len(ZI_), "int32")):
+    for _n, _k, _d in (("IDX", NL, "uint16"), ("EX", J, "bfloat16"), ("CG", J, "bfloat16"), ("CM", J, "bfloat16"), ("DG", J, "bfloat16"),
+                       ("FF", 6 * NL, "bfloat16"), ("EE", 6 * NL, "bfloat16"), ("D0", 6 * NL, "bfloat16"), ("MM", 6 * NL, "float32"), ("GE", 6 * NL, "float32"),
+                       ("SB", NL * len(ZB), "bfloat16"), ("SF", NL * len(ZF), "float32"), ("SI", NL * len(ZI_), "int32")):
         SCRATCH["%s%d" % (_n, _c)] = ("sbuf", [128, _k], _d)
-    for _n in ("BC", "BM"):
+    for _n in ("XB", "CB"):
         SCRATCH["%s%d" % (_n, _c)] = ("psum", [128, 512], "float32")
-    for _t in range(VIS + 1):
-        SCRATCH["L%d_%d" % (_t, _c)] = ("sbuf", [128, 2 * NL], "float32")
-        if _t:
-            SCRATCH["X%d_%d" % (_t, _c)] = ("sbuf", [128, 2 * NL], "float32")
-            SEMAPHORES.append("aL%d_%d" % (_t, _c))
-            if _t < VIS:
-                SEMAPHORES.append("aN%d_%d" % (_t, _c))
-DMAS = ["PTa", "PTb", "PN", "EV", "Z0", "Z1", "S0", "G0", "SG", "D0", "D1", "D2", "D3"] + ["o%s%d" % (x, c) for x in "sg" for c in range(NCH)]
+    for _t in range(1, VIS + 1):
+        SEMAPHORES.append("aL%d_%d" % (_t, _c))
+        if _t < VIS:
+            SEMAPHORES.append("aZ%d_%d" % (_t, _c))
+DMAS = ["PTa", "PTb", "PN", "EV0", "EV1", "EV2", "Z0", "Z1", "S0", "G0", "SG", "D0", "D1"] + ["o%s%d" % (x, c) for x in "sg" for c in range(NCH)]
 SEMAPHORES += ["d_" + n for n in DMAS]
-PSUM = {n for n in SCRATCH if SCRATCH[n][0] == "psum" and n != "VB"}
-ACOL = 256
+PSUM = {n for n in SCRATCH if SCRATCH[n][0] == "psum"}
 CY = 0.00083
 
 
 def vc(n):
-    return max(64, n) * CY + 0.02
+    return max(64, n) * CY + 0.03
 
 
 def sc(n):
@@ -76,337 +84,315 @@ def pc(cycles):
     return cycles * MIX["pe"] * 1e-3 + 0.03
 
 
+def named(n):
+    for b, l, k in (("SCN", MATS, 128), ("SEL", SEL, 128), ("CT", list(CONST), NL)):
+        if n in l:
+            return (b, l.index(n) * k, l.index(n) * k + k)
+    return None
+
+
 def al(n, lo=0, hi=None):
-    if n in SCALED:
-        i = list(SCALED).index(n)
-        return ("SCN", i * 128, i * 128 + 128)
-    if n in SEL:
-        i = SEL.index(n)
-        return ("SEL", i * 128, i * 128 + 128)
-    return (n, lo, SCRATCH[n][1][-1] if hi is None else hi)
-
-
-def cst(T, n):
-    b, lo, hi = al(n)
-    return T[b][:, lo:hi]
+    if lo == 0 and hi is None and named(n) and n not in SCRATCH:
+        return named(n)
+    return (n, lo, math.prod(SCRATCH[n][1][1:]) if hi is None else hi)
 
 
 def zr(n, c):
-    b, l = ("SM", ZM) if n in ZM else ("SI", ZI_)
-    i = l.index(n)
-    return ("%s%d" % (b, c), i * NL, i * NL + NL)
+    for b, l in (("SB", ZB), ("SF", ZF), ("SI", ZI_)):
+        if n in l:
+            return ("%s%d" % (b, c), l.index(n) * NL, l.index(n) * NL + NL)
 
 
-def z(T, n, c):
-    b, lo, hi = zr(n, c)
-    return T[b][:, lo:hi]
+def ap(T, r):
+    return T[r[0]][:, r[1]:r[2]] if len(r) == 3 else T[r[0]][:, r[1]:r[2]:r[3]]
 
 
 def build():
     ops = []
 
-    def op(q, cost, R, Wr, f, key, done=None, frm=None, bonus=""):
-        ops.append({"q": q, "cost": cost, "R": R, "W": Wr, "f": f, "key": key, "done": done, "frm": frm, "bonus": bonus})
+    def op(q, cost, R, Wr, f, key, done=None, frm=None, bonus="", n=0):
+        ops.append({"q": q, "cost": cost, "R": [r[:3] for r in R], "W": [r[:3] for r in Wr], "f": f, "key": key, "done": done, "frm": frm, "bonus": bonus, "n": n})
 
     def V(n, R, Wr, f, key, bonus=""):
-        op("V", vc(n), R, Wr, f, key, bonus=bonus)
+        op("V", vc(n), R, Wr, f, key, bonus=bonus, n=n)
 
     def S(n, R, Wr, f, key, bonus=""):
-        op("S", sc(n), R, Wr, f, key, bonus=bonus)
+        op("S", sc(n), R, Wr, f, key, bonus=bonus, n=n)
 
     def load(q, sem, R, Wr, f, cost, key=(-1, 0)):
         op(q, cost, R, Wr, f, key, done="d_" + sem)
 
+    def size(r):
+        return len(range(*r[1:]))
+
+    def tt(out, a, b, alu, key, bonus=""):
+        n = size(out) * (1 if a[0] in PSUM or b[0] in PSUM else 2)
+        V(n, [a, b], [out], lambda g, T, x: g.vector.tensor_tensor(ap(T, out), ap(T, a), ap(T, b), alu), key, bonus)
+
+    def ts(out, a, s1, s2, o0, o1, key, bonus=""):
+        R = [a] + [s for s in (s1, s2) if isinstance(s, tuple)]
+
+        def f(g, T, x):
+            v1, v2 = [ap(T, s) if isinstance(s, tuple) else s for s in (s1, s2)]
+            if o1 is None:
+                return g.vector.tensor_scalar(ap(T, out), ap(T, a), v1, None, o0)
+            return g.vector.tensor_scalar(ap(T, out), ap(T, a), v1, v2, o0, o1)
+        V(size(out), R, [out], f, key, bonus)
+
+    def cp(out, a, key, bonus=""):
+        V(size(out), [a], [out], lambda g, T, x: g.vector.tensor_copy(ap(T, out), ap(T, a)), key, bonus)
+
+    def fill(out, v, key, bonus=""):
+        V(size(out) // 2, [], [out], lambda g, T, x: g.vector.memset(ap(T, out), v), key, bonus)
+
+    def act(out, a, fn, key, bias=0.0, scale=1.0, acc=None, bonus=""):
+        R = [a] + [s for s in (bias,) if isinstance(s, tuple)]
+
+        def f(g, T, x):
+            b = ap(T, bias) if isinstance(bias, tuple) else bias
+            if acc:
+                return g.scalar.activation(ap(T, out), ap(T, a), fn, bias=b, scale=scale, accum_out=ap(T, acc))
+            return g.scalar.activation(ap(T, out), ap(T, a), fn, bias=b, scale=scale)
+        S(size(out), R, [out] + ([acc] if acc else []), f, key, bonus)
+
+    def mm(groups, key, bonus="", close=True):
+        R, Wr, cyc = [], [], 0
+        for out, terms, first in groups:
+            Wr.append(out)
+            for t in terms:
+                R += [al(t[0]), t[1]]
+                cyc += max(64, size(t[1])) * (4 if t[0] in SEL else 1)
+
+        def f(g, T, x):
+            for out, terms, first in groups:
+                for n, t in enumerate(terms):
+                    y = g.tensor.matmul(ap(T, t[2] if len(t) > 2 else out), ap(T, al(t[0])), ap(T, t[1]), first and n == 0, close and n == len(terms) - 1)
+            return y
+        op("T", pc(cyc), R, Wr, f, key, bonus=bonus, n=cyc)
+
+    def gather(q, out, win, off, key, in1=None, bonus=""):
+        def f(g, T, x):
+            src = ap(T, win).indirect(ap(T, off))
+            if in1:
+                return g.vector.tensor_tensor(ap(T, out), src, ap(T, in1), A.is_ge)
+            if q == "V":
+                return g.vector.tensor_copy(ap(T, out), src)
+            return g.scalar.activation(ap(T, out), src, F.Copy)
+        op(q, ga(size(out)), [win, off] + ([in1] if in1 else []), [out], f, key, bonus=bonus, n=-size(out))
+
+    def fold(out, src, key, close=True):
+        def f(g, T, x):
+            for r in range(16):
+                y = g.tensor.matmul(ap(T, out), T.ZK[:, 15 - r:143 - r], T[src][:, r:J:16], r == 0, close and r == 15)
+            return y
+        op("T", pc(J), [al("ZK"), al(src)], [out], f, key, n=J)
+
     K0 = (-1, 0)
     for y in range(2):
         load("Y", "PT" + "ab"[y], [], [("PT", y, y + 1)], lambda g, T, x, y=y: g.sync.dma_start(T.PT[:, y:16:2, :], T.par[y:8:2, :]), 3.0)
-    load("S", "S0", [], [al("S0I")], lambda g, T, x: g.scalar.dma_start(T.S0I[:], T.s0[:]), 2.4)
     load("S", "Z0", [], [al("ZI", 0, L)], lambda g, T, x: g.scalar.dma_start(T.ZI[:, 0:L], T.z[:, 0:L]), 2.4)
-    load("S", "G0", [], [al("G0I")], lambda g, T, x: g.scalar.dma_start(T.G0I[:], T.g0[:]), 2.6)
+    load("S", "S0", [], [("SGI", 0, 1)], lambda g, T, x: g.scalar.dma_start(T.SGI[:, :, 0, :], T.s0[:]), 2.4)
+    load("S", "G0", [], [("SGI", 1, 2)], lambda g, T, x: g.scalar.dma_start(T.SGI[:, :, 1, :], T.g0[:]), 2.6)
     load("Y", "PN", [], [al("PN")], lambda g, T, x: g.sync.dma_start(T.PN[:], T.par[:]), 3.2)
-    load("Y", "EV", [], [al("EVB")], lambda g, T, x: g.sync.dma_start(T.EVB[:], T.ev[:]), 8.0)
+    load("Y", "EV0", [], [al("EVB", 0, W)], lambda g, T, x: g.sync.dma_start(T.EVB[:, 0:W], T.ev[:]), 8.0)
     load("S", "SG", [], [al("SG8")], lambda g, T, x: g.scalar.dma_start(T.SG8[0:8, :], T.sg[:]), 3.0)
-    load("Y", "Z1", [], [al("ZI", L, VIS * L)], lambda g, T, x: g.sync.dma_start(T.ZI[:, L:VIS * L], T.z[:, L:VIS * L]), 10.0, (0, 9))
 
     V(128, [], [al("ONE")], lambda g, T, x: g.vector.memset(T.ONE[:], 1.0), K0, bonus="top")
 
     def asel(o, i, pat, cmp, base, ch):
-        oa = lambda T: T.I32[:] if o == "I32" else cst(T, o)
-        ia = lambda T: T.ONE[:] if i == "ONE" else cst(T, i)
-        op("G", 0.4, [al(i)], [al(o)], lambda g, T, x: g.affine_select(oa(T), ia(T), pat, cmp, 0.0, base, ch), K0, bonus="top")
-    asel("I32", "ONE", [[-1, 128]], A.is_equal, 0, 1)
+        op("G", 0.4, [al(i)], [al(o)], lambda g, T, x: g.affine_select(ap(T, al(o)), ap(T, al(i)), pat, cmp, 0.0, base, ch), K0, bonus="top")
     asel("BOA", "ONE", [[-16, 8], [0, 16]], A.is_ge, 0, 1)
     asel("BOF", "BOA", [[16, 8], [0, 16]], A.is_ge, 15, -1)
+    asel("I32", "ONE", [[-1, 128]], A.is_equal, 0, 1)
     asel("E8A", "ONE", [[1, 128]], A.is_ge, 0, -16)
     asel("E8F", "E8A", [[-1, 128]], A.is_ge, 15, 16)
-    op("G", 7.0, [al("E8F"), al("BOF"), al("I32")], [al("DT", 0, W)], lambda g, T, x: g.iota(T.DT[:, 0:W], [[0, W]], 0, 0, allow_small_or_imprecise_dtypes=True), K0, bonus="zero")
-    op("G", 0.15, [], [al("KI", 0, 1)], lambda g, T, x: g.iota(T.KI[:, 0:1], [[0, 1]], 0, 1), K0)
-    V(1, [al("KI", 0, 1)], [al("KI", 1, 2)], lambda g, T, x: g.vector.tensor_scalar(T.KI[:, 1:2], T.KI[:, 0:1], 15, None, A.bitwise_and), (0, 8))
-    V(1, [al("KI", 1, 2)], [al("KB", 0, 1)], lambda g, T, x: g.vector.tensor_scalar(T.KB[:, 0:1], T.KI[:, 1:2], -LN2, 94.0 * LN2, A.mult, A.add), (0, 8))
-    V(2048, [], [al("DT", W, 2 * W)], lambda g, T, x: g.vector.memset(T.DT[:, W:2 * W], 0.0), K0)
-    for k in range(16):
-        S(128, [al("I32")], [al("WK", k * 128, k * 128 + 128)], lambda g, T, x, k=k: g.scalar.activation(T.WK[:, k * 128:k * 128 + 128], T.I32[:], F.Copy, scale=0.0), K0)
-    for k in range(16):
-        S(8, [al("BOF")], [al("WK", k * 128, k * 128 + 128)], lambda g, T, x, k=k: g.scalar.activation(
-            T.WK[:, k * 128 + k:k * 128 + 128:16], T.SEL[:, 128 + k:256:16], F.Copy), K0)
+    op("G", 0.15, [], [("KI", 0, 1)], lambda g, T, x: g.iota(T.KI[:, 0:1], [[0, 1]], 0, 1), K0)
+    op("G", 3.6, [al("E8F"), al("BOF"), al("I32"), ("KI", 0, 1)], [al("DT", 0, W // 2)], lambda g, T, x: g.iota(
+        T.DT[:, 0:W // 2], [[0, W // 2]], 0, 0, allow_small_or_imprecise_dtypes=True), K0, bonus="top")
+    fill(al("DT", W // 2, 2 * W), 0.0, K0, bonus="top")
+    ts(("KI", 1, 2), ("KI", 0, 1), 15, None, A.bitwise_and, None, (0, 8))
+    ts(("KB", 0, 1), ("KI", 1, 2), -LN2, -172.0 * LN2, A.mult, A.add, (0, 8))
+    fill(al("ZK"), 0.0, K0)
+    b0 = al("BOF")[1]
+    act(("ZK", 15, 143, 16), ("SEL", b0, b0 + 128, 16), F.Copy, K0)
     for n in SCALED:
-        S(128, [al("I32")], [al(n)], lambda g, T, x, n=n: g.scalar.activation(cst(T, n), T.I32[:], F.Copy, scale=SCALED[n]), K0)
-    S(128, [al("I32")], [al("NIF")], lambda g, T, x: g.scalar.activation(cst(T, "NIF"), T.I32[:], F.Copy, scale=-1.0), K0)
-    V(NL, [], [al("GC")], lambda g, T, x: g.vector.memset(T.GC[:], -(2.0 ** 97)), (0, 8))
-    S(128, [al("E8F")], [al("E8")], lambda g, T, x: g.scalar.activation(T.E8[:], cst(T, "E8F"), F.Copy), K0)
-    S(128, [al("BOF")], [al("BO")], lambda g, T, x: g.scalar.activation(T.BO[:], cst(T, "BOF"), F.Copy), K0)
-    S(128, [al("BOF")], [al("BOH")], lambda g, T, x: g.scalar.activation(T.BOH[:], cst(T, "BOF"), F.Copy, scale=0.5), K0)
-    V(128, [], [al("ON16")], lambda g, T, x: g.vector.memset(T.ON16[:], 0.0625), (0, 8))
-    V(1, [], [al("TH0", 0, 1)], lambda g, T, x: g.vector.memset(T.TH0[:, 0:1], 12.0), (0, 8))
-    V(1, [], [al("TH0", 1, 2)], lambda g, T, x: g.vector.memset(T.TH0[:, 1:2], -87.0), (0, 8))
+        act(al(n), al("I32"), F.Copy, K0, scale=SCALED[n])
+    for n in BLOCK:
+        act(al(n), al("BOF"), F.Copy, K0, scale=BLOCK[n])
+    for n, v in (("NIF", -1.0), ("I14", 64 * U), ("I52", 2.0 ** 52)):
+        act(al(n), al("I32"), F.Copy, K0, scale=v)
+    act(al("KK"), al("I52"), F.Copy, K0, scale=2.0 ** 52)
+    act(al("E8"), al("E8F"), F.Copy, K0)
+    act(al("BOA"), al("I32"), F.Copy, K0, scale=2.0)
+    tt(al("TB"), al("BOA"), al("BOF"), A.subtract, (0, 8))
+    for n in CONST:
+        fill(al(n), CONST[n], (0, 8))
+    V(128, [], [al("ON32")], lambda g, T, x: g.vector.memset(T.ON32[:], -1.0 / 32), (0, 8))
+    for j, v in enumerate((-11.5, -59.5, 4.5, -TAU[0])):
+        fill(("TH0", j, j + 1), v, (0, 8))
     for c in range(NCH):
-        V(NL, [], [al("CH%d" % c, 5 * NL)], lambda g, T, x, c=c: g.vector.memset(T["CH%d" % c][:, 5 * NL:6 * NL], 191.0), (0, 8))
+        fill(("D0%d" % c, 0, 6 * NL, 6), -64.0, (0, 8))
 
-    V(L, [al("ZI", 0, L)], [al("ZU0")], lambda g, T, x: g.vector.tensor_copy(T.ZU0[:], T.ZI[:, 0:L]), K0)
+    cp(al("ZU"), al("ZI", 0, L), K0)
+    V(2 * L, [("SGI", 0, 2)], [al("US")], lambda g, T, x: g.vector.tensor_copy(T.US[:], T.SGI[:]), K0)
+    V(2 * L, [("SGI", 0, 2)], [al("L0")], lambda g, T, x: g.vector.tensor_copy(T.L0[:], T.SGI[:]), K0)
     V(256, [("PT", 0, 16)], [al("PF")], lambda g, T, x: g.vector.tensor_copy(T.PF[:], T.PT[:]), K0)
     V(256, [al("PF")], [al("TR")], lambda g, T, x: g.vector.transpose(T.TR[:], T.PF[:]), K0)
     for q3 in range(8):
         V(32, [al("TR")], [("TI", q3, q3 + 1)], lambda g, T, x, q3=q3: g.vector.tensor_copy(T.TI[:, q3:256:8], T.TR[:, q3 * 32:q3 * 32 + 32]), K0)
-    V(256, [al("TI")], [al("TA", 0, 256)], lambda g, T, x: g.vector.tensor_scalar(T.TA[:, 0:256], T.TI[:], 4095, None, A.bitwise_and), K0)
-    V(256, [al("TI")], [al("TA", 256, 512)], lambda g, T, x: g.vector.tensor_scalar(T.TA[:, 256:512], T.TI[:], 12, None, A.logical_shift_right), K0)
-    for h in range(2):
-        V(256, [al("TA", h * 256, h * 256 + 256)], [al("PL", h * 256, h * 256 + 256)], lambda g, T, x, h=h: g.vector.tensor_copy(
-            T.PL[:, h * 256:h * 256 + 256], T.TA[:, h * 256:h * 256 + 256]), K0)
-    for b, (sh, m) in enumerate(((0, 4032), (0, 63), (12, 4032), (12, 63))):
-        lo, hi = b * 256, b * 256 + 256
-        if sh:
-            V(256, [al("PN")], [al("DGI", lo, hi)], lambda g, T, x, lo=lo, hi=hi, sh=sh, m=m: g.vector.tensor_scalar(
-                T.DGI[:, lo:hi], T.PN[:], sh, m, A.logical_shift_right, A.bitwise_and), (0, 5))
-        else:
-            V(256, [al("PN")], [al("DGI", lo, hi)], lambda g, T, x, lo=lo, hi=hi, m=m: g.vector.tensor_scalar(
-                T.DGI[:, lo:hi], T.PN[:], m, None, A.bitwise_and), (0, 5))
-    V(1024, [al("DGI")], [al("DGB")], lambda g, T, x: g.vector.tensor_copy(T.DGB[:], T.DGI[:]), (0, 5))
-    for b in range(4):
-        load("Y", "D%d" % b, [al("DGB", b * 256, b * 256 + 256)], [("DT", (b // 2) * W, (b // 2) * W + W)], lambda g, T, x, b=b: g.sync.dma_start(
-            T.DT[b % 2:128:16, (b // 2) * W:(b // 2) * W + W], T.DGB[:, b * 256:b * 256 + 256]), 2.5, (0, 5))
+    ts(al("TA", 0, 256), al("TI"), 4095, None, A.bitwise_and, None, K0)
+    ts(al("TA", 256, 512), al("TI"), 12, None, A.logical_shift_right, None, K0)
+    cp(al("PL"), al("TA"), K0)
+    for d, m in enumerate((4032, 63)):
+        ts(("DGI", d * 512, d * 512 + 512, 2), al("PN"), m, None, A.bitwise_and, None, (0, 5))
+        ts(("DGI", d * 512 + 1, d * 512 + 512, 2), al("PN"), 12, m, A.logical_shift_right, A.bitwise_and, (0, 5))
+        ts(al("DGB", d * 512, d * 512 + 512), al("DGI", d * 512, d * 512 + 512), 64 * U, None, A.mult, None, (0, 5))
+        load("Y", "D%d" % d, [al("DGB", d * 512, d * 512 + 512)], [al("DT")], lambda g, T, x, d=d: g.sync.dma_start(
+            T.DT[d:128:16, :], T.DGB[:, d * 512:d * 512 + 512]), 2.5, (0, 5))
     V(576, [al("SG8")], [al("SG8B")], lambda g, T, x: g.vector.tensor_copy(T.SG8B[0:8, :], T.SG8[0:8, :]), (0, 6))
-    for t in range(VIS):
-        op("T", 0.1, [al("E8"), al("SG8B")], [al("PB", 0, L)], lambda g, T, x, t=t: g.tensor.matmul(T.PB[:, 0:L], T.E8[0:8, :], T.SG8B[0:8, t * L:t * L + L], True, True), (t, 6))
-        S(L, [al("PB", 0, L)], [al("SGB", t * L, t * L + L)], lambda g, T, x, t=t: g.scalar.activation(T.SGB[:, t * L:t * L + L], T.PB[:, 0:L], F.Copy), (t, 6))
     for b in range(4):
-        R = [al("EVB"), al("PL", b * 128, b * 128 + 128)]
-        Wr = [al("EC", b * 2048, b * 2048 + 2048)]
-        if b < MIX["ecv"]:
-            op("V", ga(2048), R, Wr, lambda g, T, x, b=b: g.vector.tensor_copy(
-                T.EC[:, b * 2048:b * 2048 + 2048], T.EVB[:, 0:W].indirect(T.PL[:, b * 128:b * 128 + 128])), (0, 4))
-        else:
-            op("S", ga(2048), R, Wr, lambda g, T, x, b=b: g.scalar.activation(
-                T.EC[:, b * 2048:b * 2048 + 2048], T.EVB[:, 0:W].indirect(T.PL[:, b * 128:b * 128 + 128]), F.Copy), (0, 4))
+        hf, s = b // 2, b % 2
+        gather("V" if b < MIX["ecv"] else "S", ("EC", hf * W + s, hf * W + W, 2), al("EVB", 0, W), al("PL", s * 256 + hf * 128, s * 256 + hf * 128 + 128), (0, 4))
+    load("Y", "Z1", [al("EC")], [al("ZI", L, VIS * L)], lambda g, T, x: g.sync.dma_start(T.ZI[:, L:VIS * L], T.z[:, L:VIS * L]), 3.0, (0, 9))
+    for t in range(1, VIS):
+        load("Y", "EV%d" % t, [al("EC")], [al("EVB", t * W, t * W + W)], lambda g, T, x, t=t: g.sync.dma_start(T.EVB[:, t * W:t * W + W], T.ev[:]), 8.0, (0, 9))
+        ts(al("ZO", t * L, t * L + L), al("ZI", t * L, t * L + L), float(t * W), None, A.add, None, (t - 1, 9))
 
-    def fold16(bank, col, src):
-        def f(g, T, x):
-            for r in range(16):
-                y = g.tensor.matmul(T[bank][:, col:col + NL], T.WK[:, r * 128:r * 128 + 128], T[src][:, r:J:16], r == 0, r == 15)
-            return y
-        return f
+    def stays(t, c, first, step):
+        e, n = "%d" % c, 6 // step
+        vv = ("CB" + e, NL, NL + n * NL)
+        tt(("EE" + e, first, 6 * NL, step), ("XB" + e, first, 6 * NL, step), ("GE" + e, first, 6 * NL, step), A.is_equal, (t, c))
+        mm([(vv, [("IB", ("FF" + e, first, 6 * NL, step))] + [("N64", zr("PO", c), (vv[0], NL + j, vv[2], n)) for j in range(n)]
+             + [("N128", ("EE" + e, first, 6 * NL, step))], True)], (t, c))
+        act(("D0" + e, first, 6 * NL, step), vv, F.Sign, (t, c), bias=("TH%d" % t, 1, 2), scale=-1.0)
 
     def walk(t, c):
         k = (t, c)
         o, e = c * NL, "%d" % c
-        Ln, Un, ex, cm, cg, bank, dg, ix, zu = "L%d_%d" % (t, c), "US" + e, "EX" + e, "CM" + e, "CG" + e, "BC" + e, "DG" + e, "IDX" + e, "ZU%d" % t
-        vb = c * 2 * NL
-        if t == 0:
-            for h, n in enumerate(("S0I", "G0I")):
-                V(NL, [al(n, o, o + NL)], [al(Ln, h * NL, h * NL + NL)], lambda g, T, x, h=h, n=n: g.vector.tensor_copy(T[Ln][:, h * NL:h * NL + NL], T[n][:, o:o + NL]), k)
-            V(NL, [al("SGB", o, o + NL)], [zr("PO", c)], lambda g, T, x: g.vector.tensor_copy(z(T, "PO", c), T.SGB[:, o:o + NL]), k)
-        else:
-            nr, zf, dz = "NRL%d" % t, "ZF%d" % t, "DZ%d" % t
-            V(2 * NL, [al(nr, o, o + NL), al(dz, o, o + NL)], [al("VB", vb, vb + NL)], lambda g, T, x: g.vector.tensor_tensor(
-                T.VB[:, vb:vb + NL], T[dz][:, o:o + NL], T[nr][:, o:o + NL], A.mult), k)
-            V(NL, [al("VB", vb, vb + NL), al(zf, o, o + NL)], [al("VB", vb + NL, vb + 2 * NL)], lambda g, T, x: g.vector.tensor_tensor(
-                T.VB[:, vb + NL:vb + 2 * NL], T.VB[:, vb:vb + NL], T[zf][:, o:o + NL], A.add), k)
-            V(NL, [al("VB", vb + NL, vb + 2 * NL)], [al(zu, o, o + NL)], lambda g, T, x: g.vector.tensor_copy(T[zu][:, o:o + NL], T.VB[:, vb + NL:vb + 2 * NL]), k)
-            op("R", MIX["remote"], [al("X%d_%d" % (t, c))], [al(Ln)], None, k, done="aL%d_%d" % (t, c), frm=-1)
-            V(2 * NL, [al("SGB", t * L + o, t * L + o + NL), al(nr, o, o + NL)], [zr("PO", c)], lambda g, T, x: g.vector.tensor_tensor(
-                z(T, "PO", c), T.SGB[:, t * L + o:t * L + o + NL], T[nr][:, o:o + NL], A.mult), k)
-        V(2 * NL, [al(Ln)], [al(Un)], lambda g, T, x: g.vector.tensor_copy(T[Un][:], T[Ln][:]), k)
-        op("S", ga(J), [al("EVB"), al(zu, o, o + NL)], [al(ex)], lambda g, T, x: g.scalar.activation(T[ex][:], T.EVB[:, 0:W].indirect(T[zu][:, o:o + NL]), F.Copy), k)
-        op("V", ga(J), [al("EVB"), al(Un), al(ex)], [al(cm)], lambda g, T, x: g.vector.tensor_tensor(
-            T[cm][:], T.EVB[:, 0:W].indirect(T[Un][:, 0:NL]), T[ex][:], A.is_ge), k)
-        ih, ch, sh = "IH" + e, "CH" + e, "SH" + e
-        aw = (bank, ACOL, ACOL + NL)
+        ex, cm, dg, ix, xb, cb, ff, ee = "EX" + e, "CM" + e, "DG" + e, "IDX" + e, "XB" + e, "CB" + e, "FF" + e, "EE" + e
+        lS, lG = ("L%d" % t, 2 * o, 2 * o + NL), ("L%d" % t, 2 * o + NL, 2 * o + 2 * NL)
+        th = "TH%d" % t
+        m1, m2 = (cb, 6 * NL, 7 * NL), (cb, 7 * NL, 8 * NL)
+        PO, g5 = zr("PO", c), ("GE" + e, CL, 6 * NL, 6)
+        e8 = al("E8")
+        if t:
+            zx, zf = ("ZX%d" % t, o, o + NL), ("ZF%d" % t, o, o + NL)
+            op("R", MIX["remote"], [("ZS%d" % t, o, o + NL)], [zx], None, k, done="aZ%d_%d" % (t, c), frm=-1)
+            tt(zf, zx, ("ZO", t * L + o, t * L + o + NL), A.min, k)
+            cp(("ZU", o, o + NL), zf, k)
+            act(zr("SR", c), zx, F.Sign, k, bias=-0.875 * H, acc=("RS%d" % t, c, c + 1))
+            lo = ("L%d" % t, 2 * o, 2 * o + 2 * NL)
+            op("R", MIX["remote"], [("X%d" % t, 2 * o, 2 * o + 2 * NL)], [lo], None, k, done="aL%d_%d" % (t, c), frm=-1)
+            cp(("US", 2 * o, 2 * o + 2 * NL), lo, k)
+
+        def fp(g, T, x):
+            y = g.tensor.matmul(ap(T, m1), T.SCN[0:8, e8[1]:e8[2]], T.SG8B[0:8, t * L + o:t * L + o + NL], True, not t)
+            return g.tensor.matmul(ap(T, m1), ap(T, al("IH")), ap(T, zr("SR", c)), False, True) if t else y
+        op("T", pc(2 * NL), [e8, al("SG8B")] + ([al("IH"), zr("SR", c)] if t else []), [m1], fp, k, n=2 * NL)
+        act(PO, m1, F.Relu, k, bias=-0.5 if t else 0.0)
+        gather("S", al(ex), al("EVB", 0, (t + 1) * W), ("ZU", o, o + NL), k)
+        gather("V", al(cm), al("EVB", 0, W), ("US", 2 * o, 2 * o + NL), k, in1=al(ex))
+
+        def gates():
+            gather("V", al("CG" + e), al("EVB", 0, W), ("US", 2 * o + NL, 2 * o + 2 * NL), k, in1=al(ex), bonus="gcov")
+            fold(m1, "CG" + e, k)
+            act(zr("MS", c), m1, F.Sign, k, bias=(th, 0, 1))
+            mm([(m1, [("BO", zr("MS", c)), ("N64", PO)], True)], k)
+            act(zr("Q2", c), m1, F.Abs, k, bias=21.0)
+
         for i in range(CL + 1):
-            lo, hi = i * NL, i * NL + NL
+            xi, fi = (xb, i, 6 * NL, 6), (ff, i + 1, 6 * NL, 6)
+            if i == MIX["gat"][c]:
+                gates()
             if i:
                 if i < CL:
-                    op("V", ga(J), [al("EC"), al(ix), al(ex)], [al(cm)], lambda g, T, x: g.vector.tensor_tensor(
-                        T[cm][:], T.EC[:, 0:2 * W].indirect(T[ix][:]), T[ex][:], A.is_ge), k)
-                op("S", ga(J), [al("DT"), al(ix)], [al(dg)], lambda g, T, x: g.scalar.activation(T[dg][:], T.DT[:, 0:2 * W].indirect(T[ix][:]), F.Copy), k)
+                    gather("V", al(cm), al("EC"), al(ix), k, in1=al(ex))
+                gather("S", al(dg), al("DT"), al(ix), k)
             if i < CL:
-                op("T", pc(J), [al("WK"), al(cm)], [al(bank, 0, NL)], fold16(bank, 0, cm), k)
+                fold((cb, 0, NL), cm, k)
+                act(fi, (cb, 0, NL), F.Identity, k, bias=16.0, scale=-1.0)
             if i:
-                op("T", pc(J), [al("WK"), al(dg)], [aw], fold16(bank, ACOL, dg), k)
-            if i == CL:
-                S(NL, [aw], [al(ih, lo, hi)], lambda g, T, x, lo=lo, hi=hi: g.scalar.activation(T[ih][:, lo:hi], T[bank][:, ACOL:ACOL + NL], F.Copy), k)
-                break
-            if i:
-                V(NL, [al(bank, 0, NL)], [al(sh, lo, hi)], lambda g, T, x, lo=lo, hi=hi: g.vector.tensor_scalar(T[sh][:, lo:hi], T[bank][:, 0:NL], 7.5, 4096.0, A.is_lt, A.mult), k)
-                V(NL, [aw, al(sh, lo, hi)], [al(ih, lo, hi)], lambda g, T, x, lo=lo, hi=hi: g.vector.tensor_tensor(
-                    T[ih][:, lo:hi], T[bank][:, ACOL:ACOL + NL], T[sh][:, lo:hi], A.add), k)
+                fold(xi, dg, k, close=False)
+                mm([(xi, [("IB", al("O%d" % i))] + ([("IU", fi)] if i < CL else []), False)], k)
             else:
-                V(NL, [al(bank, 0, NL)], [al("VB", vb, vb + NL)], lambda g, T, x: g.vector.tensor_scalar(T.VB[:, vb:vb + NL], T[bank][:, 0:NL], 7.5, 4096.0, A.is_lt, A.mult), k)
-                V(NL, [al("VB", vb, vb + NL), al(Ln, 0, NL)], [al(ih, lo, hi)], lambda g, T, x, lo=lo, hi=hi: g.vector.tensor_tensor(
-                    T[ih][:, lo:hi], T.VB[:, vb:vb + NL], T[Ln][:, 0:NL], A.add), k)
-            V(NL, [al(ih, lo, hi)], [al(ix)], lambda g, T, x, lo=lo, hi=hi: g.vector.tensor_copy(T[ix][:], T[ih][:, lo:hi]), k)
-            S(NL, [al(bank, 0, NL)], [al(ch, lo, hi)], lambda g, T, x, lo=lo, hi=hi, i=i: g.scalar.activation(
-                T[ch][:, lo:hi], T[bank][:, 0:NL], F.Identity, bias=32.0 * i), k, bonus="ch")
+                mm([(xi, [("I14", lS), ("IU", fi)], True)], k)
+            if i < CL:
+                ts(al(ix), xi, 2.0 ** 15, 7.5 / 32 + 0.75 * i * 2.0 ** 15, A.mult, A.add, k, bonus="idx")
+            if i == 0:
+                mm([(m2, [("I14", lG), ("IB", PO)], True), ((xb, 6 * NL, 7 * NL), [("I32", lS), ("HI", PO)], True)], k)
+                act(g5, m2, F.Identity, k, bias=-0.75 * CL)
+            elif i < CL:
+                mm([(m2, [("I32", g5), ("IU", fi)], True)], k, bonus="ge")
+                act(("GE" + e, i, 6 * NL, 6), m2, F.Identity, k, bias=0.75 * (CL - i), bonus="ge")
+            if i == CL - 1:
+                stays(t, c, 1, 3)
+                stays(t, c, 3, 6)
 
     def epilogue(t, c):
         k = (t, c)
-        e = "%d" % c
-        bm, th, Ln, ih, ch, mmn, sh = "BM" + e, "TH%d" % t, "L%d_%d" % (t, c), "IH" + e, "CH" + e, "MM" + e, "SH" + e
-        Un, ex, cg = "US" + e, "EX" + e, "CG" + e
+        o, e = c * NL, "%d" % c
+        xb, cb, ff, ee, mmn, th = "XB" + e, "CB" + e, "FF" + e, "EE" + e, "MM" + e, "TH%d" % t
+        lG = ("L%d" % t, 2 * o + NL, 2 * o + 2 * NL)
+        m1, m2, vv = (cb, 6 * NL, 7 * NL), (cb, 7 * NL, 8 * NL), (cb, NL, 6 * NL)
+        PO, M6 = zr("PO", c), (mmn, 5, 6 * NL, 6)
 
         def Z(n):
             return zr(n, c)
-        bk = al(bm, 0, NL)
-        S(NL, [Z("PO"), al(th)], [Z("TT")], lambda g, T, x: g.scalar.activation(z(T, "TT", c), z(T, "PO", c), F.Identity, bias=99.0, scale=T[th][:, 1:2]), k)
-
-        def gates():
-            op("V", ga(J), [al("EVB"), al(Un), al(ex)], [al(cg)], lambda g, T, x: g.vector.tensor_tensor(
-                T[cg][:], T.EVB[:, 0:W].indirect(T[Un][:, NL:2 * NL]), T[ex][:], A.is_ge), k, bonus="gcov%d" % c)
-            op("T", pc(J), [al("WK"), al(cg)], [bk], fold16(bm, 0, cg), k)
-            V(NL, [bk, al(th)], [Z("MS")], lambda g, T, x: g.vector.tensor_scalar(z(T, "MS", c), T[bm][:, 0:NL], T[th][:, 0:1], None, A.is_lt), k)
-
-            def fr(g, T, x):
-                g.tensor.matmul(T[bm][:, 0:NL], T.BO[:], z(T, "MS", c), True, False)
-                return g.tensor.matmul(T[bm][:, 0:NL], cst(T, "I32B"), z(T, "PO", c), False, True)
-            op("T", pc(2 * NL), [al("BO"), al("I32B"), Z("MS"), Z("PO")], [bk], fr, k)
-            S(NL, [bk], [Z("G1")], lambda g, T, x: g.scalar.activation(z(T, "G1", c), T[bm][:, 0:NL], F.Sign, bias=-0.5), k)
-            S(NL, [bk], [Z("G2")], lambda g, T, x: g.scalar.activation(z(T, "G2", c), T[bm][:, 0:NL], F.Sign, bias=-36.5), k)
-        for i in range(CL):
-            if i == MIX["gat%d" % c]:
-                gates()
-            s0, s1 = slice(i * NL, i * NL + NL), slice((i + 1) * NL, (i + 2) * NL)
-            En, Fn, tb = "E%d" % i, "F%d" % i, "tr%d" % i
-
-            def fy(g, T, x, s0=s0, s1=s1, es=i < MIX["es"]):
-                g.tensor.matmul(T[bm][:, NL:2 * NL], cst(T, "IB"), T[ch][:, s0], True, False)
-                g.tensor.matmul(T[bm][:, NL:2 * NL], cst(T, "NIB"), z(T, "TT", c), False, True)
-                g.tensor.matmul(T[bm][:, 0:NL], T.I32[:], T[ih][:, s1], True, False)
-                if s1.start < CL * NL:
-                    g.tensor.matmul(T[bm][:, 0:NL], cst(T, "NIB"), T[sh][:, s1], False, False)
-                if es:
-                    g.tensor.matmul(T[bm][:, 0:NL], cst(T, "NIF"), T[Ln][:, NL:2 * NL], False, False)
-                return g.tensor.matmul(T[bm][:, 0:NL], cst(T, "I16K"), z(T, "PO", c), False, True)
-            last = i == CL - 1
-            es = i < MIX["es"]
-            op("T", pc((7 if last else 8) * NL + (4 * NL if es else 0)), [al("I32"), al("I16K"), al("IB"), al("NIB"), al(ih, s1.start, s1.stop), Z("PO"), al(ch, s0.start, s0.stop), Z("TT")]
-               + ([] if last else [al(sh, s1.start, s1.stop)]) + ([al("NIF"), al(Ln, NL, 2 * NL)] if es else []), [al(bm, 0, 2 * NL)], fy, k, bonus=tb)
-            if es:
-                S(NL, [bk], [Z("SQ")], lambda g, T, x: g.scalar.activation(z(T, "SQ", c), T[bm][:, 0:NL], F.Square), k, bonus=tb)
-                S(NL, [al(bm, NL, 2 * NL)], [Z(Fn)], lambda g, T, x, Fn=Fn, i=i: g.scalar.activation(z(T, Fn, c), T[bm][:, NL:2 * NL], F.Sign, bias=0.5 - 32.0 * i), k, bonus=tb)
-                S(NL, [Z("SQ")], [Z(En)], lambda g, T, x, En=En: g.scalar.activation(z(T, En, c), z(T, "SQ", c), F.Relu, bias=1.0, scale=-1.0), k, bonus=tb)
-            else:
-                V(NL, [bk, al(Ln, NL, 2 * NL)], [Z(En)], lambda g, T, x, En=En: g.vector.tensor_tensor(z(T, En, c), T[bm][:, 0:NL], T[Ln][:, NL:2 * NL], A.is_equal), k, bonus=tb)
-                S(NL, [al(bm, NL, 2 * NL)], [Z(Fn)], lambda g, T, x, Fn=Fn, i=i: g.scalar.activation(z(T, Fn, c), T[bm][:, NL:2 * NL], F.Sign, bias=0.5 - 32.0 * i), k, bonus=tb)
-
-            def fw(g, T, x, s0=s0, s1=s1, En=En, Fn=Fn, last=last):
-                if last:
-                    g.tensor.matmul(T[bm][:, NL:2 * NL], T.I32[:], T[ih][:, s1], True, False)
-                    g.tensor.matmul(T[bm][:, NL:2 * NL], cst(T, "I8K"), T[ch][:, s1], False, True)
-                g.tensor.matmul(T[bm][:, 0:NL], T.I32[:], T[ih][:, s0], True, False)
-                g.tensor.matmul(T[bm][:, 0:NL], cst(T, "I8K"), T[ch][:, s0], False, False)
-                g.tensor.matmul(T[bm][:, 0:NL], cst(T, "NHB"), z(T, Fn, c), False, False)
-                return g.tensor.matmul(T[bm][:, 0:NL], cst(T, "NB"), z(T, En, c), False, True)
-            op("T", pc((12 if last else 7) * NL), [al("I32"), al("I8K"), al("NHB"), al("NB"), al(ih, s0.start, s1.stop), al(ch, s0.start, s1.stop if last else s0.stop), Z(En), Z(Fn)],
-               [al(bm, 0, 2 * NL)], fw, k, bonus=tb)
-            if i == 0:
-                V(NL, [bk], [al(mmn)], lambda g, T, x: g.vector.tensor_copy(T[mmn][:], T[bm][:, 0:NL]), k, bonus=tb)
-            else:
-                for j in range(2 if last else 1):
-                    V(NL, [al(bm, j * NL, j * NL + NL), al(mmn)], [al(mmn)], lambda g, T, x, j=j: g.vector.tensor_tensor(
-                        T[mmn][:], T[bm][:, j * NL:j * NL + NL], T[mmn][:], A.min), k, bonus=tb)
-        if MIX["gat%d" % c] == CL:
-            gates()
-        V(NL, [al(mmn)], [Z("MI")], lambda g, T, x: g.vector.tensor_copy(z(T, "MI", c), T[mmn][:]), k)
-        V(NL, [Z("MI")], [Z("CI")], lambda g, T, x: g.vector.tensor_scalar(z(T, "CI", c), z(T, "MI", c), 13, 31, A.arith_shift_right, A.bitwise_and), k)
-        V(NL, [Z("CI"), al(th)], [Z("NC")], lambda g, T, x: g.vector.tensor_scalar(z(T, "NC", c), z(T, "CI", c), T[th][:, 0:1], 64.0, A.is_ge, A.mult), k)
-        V(NL, [Z("CI")], [Z("CF")], lambda g, T, x: g.vector.tensor_copy(z(T, "CF", c), z(T, "CI", c)), k)
-        V(NL, [Z("MI")], [Z("XI")], lambda g, T, x: g.vector.tensor_scalar(z(T, "XI", c), z(T, "MI", c), 4095, None, A.bitwise_and), k)
-
-        def fc(g, T, x):
-            if t + 1 < VIS:
-                bq = T[bm][:, NL:2 * NL]
-                g.tensor.matmul(bq, cst(T, "IB"), T.GC[:], True, False)
-                g.tensor.matmul(bq, cst(T, "HA"), z(T, "G1", c), False, False)
-                g.tensor.matmul(bq, cst(T, "HB"), z(T, "G2", c), False, False)
-                g.tensor.matmul(bq, T.BO[:], z(T, "NC", c), False, True)
-            g.tensor.matmul(T[bm][:, 0:NL], cst(T, "IB"), z(T, "NC", c), True, False)
-            return g.tensor.matmul(T[bm][:, 0:NL], cst(T, "IB"), z(T, "CF", c), False, True)
-        op("T", pc((2 if t + 1 == VIS else 6) * NL), [al("IB"), al("BO"), al("GC"), al("HA"), al("HB"), Z("G1"), Z("G2"), Z("CF"), Z("NC")], [al(bm, 0, 2 * NL)], fc, k)
-        o = c * NL
+        stays(t, c, 2, 3)
+        V(6 * NL, [al("D0" + e), (xb, 0, 6 * NL)], [al(mmn)], lambda g, T, x: g.vector.tensor_tensor_scan(
+            T[mmn][:], T["D0" + e][:], T[xb][:, 0:6 * NL], 0.0, A.add, A.max), k)
+        act(Z("RR"), M6, F.Identity, k, bias=MAGIC)
+        mm([(m1, [("NIF", Z("RR")), ("IB", al("CM")), ("I32", M6)], True)], k)
+        xr, xn, xu, xg = (xb, 0, NL), (xb, NL, 2 * NL), (xb, 2 * NL, 3 * NL), (xb, 7 * NL, 8 * NL)
+        neg = (xn, [("HI", al("C1")), ("NHI", PO)], True)
         if t + 1 < VIS:
-            ns, nl = "NRS%d" % (t + 1), "NRL%d" % (t + 1)
-            V(NL, [al(bm, NL, 2 * NL)], [al(ns, o, o + NL)], lambda g, T, x: g.vector.tensor_scalar(T[ns][:, o:o + NL], T[bm][:, NL:2 * NL], 1024.0, None, A.not_equal), k, bonus="nr")
-            op("G", 0.1, [al(ns, o, o + NL)], [], lambda g, T, x: x["send"](T[nl][:, o:o + NL], T[ns][:, o:o + NL], "aN%d_%d" % (t + 1, c), "next"), k)
-            op("R", MIX["remote"], [al(ns, o, o + NL)], [al(nl, o, o + NL)], None, k, done="aN%d_%d" % (t + 1, c), frm=-1)
-        S(NL, [bk, al("KB", 0, 1)], [Z("W2")], lambda g, T, x: g.scalar.activation(z(T, "W2", c), T[bm][:, 0:NL], F.Exp, bias=T.KB[:, 0:1], scale=-16.0 * LN2), k)
-
-        def fs(g, T, x):
-            g.tensor.matmul(T[bm][:, 0:NL], cst(T, "IB"), T.GC[:], True, False)
-            g.tensor.matmul(T[bm][:, 0:NL], cst(T, "HA"), z(T, "G1", c), False, False)
-            g.tensor.matmul(T[bm][:, 0:NL], cst(T, "HB"), z(T, "G2", c), False, False)
-            return g.tensor.matmul(T[bm][:, 0:NL], T.BOH[:], z(T, "W2", c), False, True)
-        op("T", pc(4 * NL), [al("IB"), al("GC"), al("HA"), al("HB"), al("BOH"), Z("G1"), Z("G2"), Z("W2")], [bk], fs, k)
-        vb = c * 2 * NL
-        r0, r1 = (vb, vb + NL), (vb + NL, vb + 2 * NL)
-        Xn = "X%d_%d" % (t + 1, c)
-
-        def vt(in0, in1, out, alu, R, Wr):
-            V(NL, R, Wr, lambda g, T, x: g.vector.tensor_tensor(out(T), in0(T), in1(T), alu), k)
-
-        def vbs(r):
-            return lambda T: T.VB[:, r[0]:r[1]]
-        V(NL, [Z("XI")], [al("VB", *r0)], lambda g, T, x: g.vector.tensor_copy(T.VB[:, r0[0]:r0[1]], z(T, "XI", c)), k)
-        lS, lG = (lambda T: T[Ln][:, 0:NL]), (lambda T: T[Ln][:, NL:2 * NL])
-        vt(vbs(r0), lS, vbs(r1), A.subtract, [al("VB", *r0), al(Ln, 0, NL)], [al("VB", *r1)])
-        vt(vbs(r0), lG, vbs(r0), A.subtract, [al("VB", *r0), al(Ln, NL, 2 * NL)], [al("VB", *r0)])
-        vt(vbs(r1), lambda T: z(T, "PO", c), vbs(r1), A.mult, [al("VB", *r1), Z("PO")], [al("VB", *r1)])
-        vt(vbs(r1), lS, lambda T: T[Xn][:, 0:NL], A.add, [al("VB", *r1), al(Ln, 0, NL)], [al(Xn, 0, NL)])
-        V(NL, [bk, Z("W2")], [Z("UU")], lambda g, T, x: g.vector.tensor_tensor(z(T, "UU", c), T[bm][:, 0:NL], z(T, "W2", c), A.is_lt), k)
-        vt(vbs(r0), lambda T: z(T, "UU", c), vbs(r0), A.mult, [al("VB", *r0), Z("UU")], [al("VB", *r0)])
-        vt(vbs(r0), lG, lambda T: T[Xn][:, NL:2 * NL], A.add, [al("VB", *r0), al(Ln, NL, 2 * NL)], [al(Xn, NL, 2 * NL)])
+            act(Z("SC"), m1, F.Sign, k, bias=(th, 2, 3), scale=-1.0 / U)
+        act(Z("W2"), m1, F.Exp, k, bias=("KB", 0, 1), scale=17.0 * LN2 / U)
         if t + 1 < VIS:
-            op("G", 0.1, [al(Xn)], [], lambda g, T, x: x["send"](T["L%d_%d" % (t + 1, c)][:], T[Xn][:], "aL%d_%d" % (t + 1, c), "next"), k)
+            mm([neg, (xr, [("NHI", Z("Q2")), ("NHI", al("C45")), ("H32", PO), ("NBH", Z("SC"))], True)], k)
+            zs, zx = ("ZS%d" % (t + 1), o, o + NL), ("ZX%d" % (t + 1), o, o + NL)
+            tt(zs, xr, ("ZF%d" % t, o, o + NL) if t else ("ZI", o, o + NL), A.max, k)
+            op("G", 0.1, [zs], [], lambda g, T, x: x["send"](ap(T, zx), ap(T, zs), "aZ%d_%d" % (t + 1, c), "next"), k)
         else:
-            H = "L%d_%d" % (VIS, c)
-            op("G", 0.1, [al(Xn)], [], lambda g, T, x: x["send"](T[H][:], T[Xn][:], "aL%d_%d" % (VIS, c), "home"), k)
-            op("R", MIX["remote"], [al(Xn)], [al(H)], None, k, done="aL%d_%d" % (VIS, c), frm=2)
-            load("Y", "os%d" % c, [al(H)], [], lambda g, T, x: g.sync.dma_start(T.ys[:, o:o + NL], T[H][:, 0:NL]), 2.0, k)
-            load("S", "og%d" % c, [al(H)], [], lambda g, T, x: g.scalar.dma_start(T.yg[:, o:o + NL], T[H][:, NL:2 * NL]), 2.0, k)
-
-    def zsend(t):
-        u = t + 1
-        op("G", 0.1, [al("ZU%d" % t)], [], lambda g, T, x: x["send"](T["ZR%d" % u][:], T["ZU%d" % t][:], "zr%d" % u, "next"), (t, 5))
-        op("R", MIX["remote"], [al("ZU%d" % t)], [al("ZR%d" % u)], None, (t, 5), done="zr%d" % u, frm=-1)
-        V(L, [al("ZR%d" % u)], [al("ZF%d" % u)], lambda g, T, x: g.vector.tensor_copy(T["ZF%d" % u][:], T["ZR%d" % u][:]), (t, 5))
-        V(2 * L, [al("ZF%d" % u), al("ZI", u * L, u * L + L)], [al("DZ%d" % u)], lambda g, T, x: g.vector.tensor_tensor(
-            T["DZ%d" % u][:], T.ZI[:, u * L:u * L + L], T["ZF%d" % u][:], A.subtract), (t, 5))
+            mm([neg], k)
+        ts(Z("MI"), M6, 1.0 / U, None, A.mult, None, k)
+        ts(Z("AI"), Z("MI"), 6, 4095, A.arith_shift_right, A.bitwise_and, k)
+        mm([(m2, [("KK", Z("Q2")), ("KK", al("C37")), ("KK", PO), ("TB", Z("W2"))], True)], k)
+        tt(Z("T1"), xn, Z("AI"), A.add, k)
+        act(Z("SU"), m2, F.Sign, k, bias=(th, 3, 4))
+        mm([(xu, [("HH", al("C1")), ("NHH", Z("SU"))], True), (xg, [("I32", lG), ("HH", al("C1")), ("HH", Z("SU"))], True)], k)
+        tt(Z("T2"), xu, Z("AI"), A.add, k)
+        xo, lo = ("X%d" % (t + 1), 2 * o, 2 * o + 2 * NL), ("L%d" % (t + 1), 2 * o, 2 * o + 2 * NL)
+        tt(xo, (xb, 6 * NL, 8 * NL), (Z("T1")[0], Z("T1")[1], Z("T2")[2]), A.min, k)
+        op("G", 0.1, [xo], [], lambda g, T, x: x["send"](ap(T, lo), ap(T, xo), "aL%d_%d" % (t + 1, c), "next" if t + 1 < VIS else "home"), k)
+        if t + 1 == VIS:
+            op("R", MIX["remote"], [xo], [lo], None, k, done="aL%d_%d" % (VIS, c), frm=2)
+            load("Y", "os%d" % c, [lo], [], lambda g, T, x: g.sync.dma_start(T.ys[:, o:o + NL], T[lo[0]][:, 2 * o:2 * o + NL]), 2.0, k)
+            load("S", "og%d" % c, [lo], [], lambda g, T, x: g.scalar.dma_start(T.yg[:, o:o + NL], T[lo[0]][:, 2 * o + NL:2 * o + 2 * NL]), 2.0, k)
 
     def thresh(t):
-        n, th = "NRL%d" % t, "TH%d" % t
-        b = "th"
-        V(L, [al(n)], [al("RS", 0, 1)], lambda g, T, x: g.vector.tensor_reduce(T.RS[:, 0:1], T[n][:], AxisListType.X, A.add), (t, 0), bonus=b)
-        op("T", 0.15, [al("ON16"), al("RS", 0, 1)], [al("PB", 0, 1)], lambda g, T, x: g.tensor.matmul(T.PB[:, 0:1], T.ON16[:], T.RS[:, 0:1], True, True), (t, 0), bonus=b)
-        V(1, [al("PB", 0, 1)], [al("THI", 0, 1)], lambda g, T, x: g.vector.tensor_copy(T.THI[:, 0:1], T.PB[:, 0:1]), (t, 0), bonus=b)
-        V(1, [al("THI", 0, 1)], [al("THI", 1, 2)], lambda g, T, x: g.vector.tensor_scalar(T.THI[:, 1:2], T.THI[:, 0:1], 1, None, A.bitwise_and), (t, 0), bonus=b)
-        for j, v in ((0, 12.0), (1, -87.0)):
-            V(1, [al("THI", 1, 2)], [al(th, j, j + 1)], lambda g, T, x, j=j, v=v: g.vector.tensor_scalar(T[th][:, j:j + 1], T.THI[:, 1:2], v, None, A.add), (t, 0), bonus=b)
+        k, b, rs, th = (t, 8), "th", "RS%d" % t, "TH%d" % t
 
-    zsend(0)
+        def f(g, T, x):
+            for c in range(NCH):
+                y = g.tensor.matmul(T.PB[:, 0:1], T.ON32[:], T[rs][:, c:c + 1], c == 0, c == NCH - 1)
+            return y
+        op("T", 0.35, [al("ON32"), al(rs)], [("PB", 0, 1)], f, k, bonus=b, n=768)
+        ts(("THI", 0, 1), ("PB", 0, 1), 0.5, -0.25, A.mult, A.add, k, b)
+        ts(("NP", 0, 1), ("THI", 0, 1), 2.0, ("PB", 0, 1), A.mult, A.subtract, k, b)
+        act((th, 0, 3), ("TH0", 0, 3), F.Identity, k, bias=("NP", 0, 1), bonus=b)
+        act((th, 3, 4), ("NP", 0, 1), F.Identity, k, bias=-TAU[0], scale=TAU[1] - TAU[0], bonus=b)
+
     for t in range(VIS):
+        if t:
+            n0 = len(ops)
         for c in range(NCH):
             walk(t, c)
         if t:
-            if t + 1 < VIS:
-                zsend(t)
+            n1 = len(ops)
             thresh(t)
+            early = [o for o in ops[n0:n1] if any(w[0] in ("ZX%d" % t, "RS%d" % t) for w in o["W"])]
+            ops[n0:] = early + ops[n1:] + [o for o in ops[n0:n1] if not any(w[0] in ("ZX%d" % t, "RS%d" % t) for w in o["W"])]
         for c in range(NCH):
             epilogue(t, c)
     return ops
@@ -421,6 +407,8 @@ def depend(ops):
                 for (m, w2, l2, h2) in acc.get(b, ()):
                     if m != n and (wr or w2) and lo < h2 and l2 < hi:
                         if wr and not w2 and ops[m]["q"] == o["q"] and not ops[m]["done"]:
+                            o["soft"].add(m)
+                        elif o["q"] == "T" and ops[m]["q"] == "T" and b in PSUM:
                             o["soft"].add(m)
                         else:
                             o["hard"].add(m)
@@ -446,20 +434,20 @@ def schedule(ops):
         for m in o["hard"] | o["soft"]:
             succ[m].append(i)
     bot = [0.0] * n
-    hop = MIX["hop"]
+    hop, same = MIX["hop"], MIX["same"]
     for i in range(n - 1, -1, -1):
         bot[i] = ops[i]["cost"] + max([bot[s] + hop for s in succ[i]], default=0.0)
-    own = [0.0] * n
-    for i in range(n - 1, -1, -1):
-        own[i] = ops[i]["cost"] + max([own[s] + hop for s in succ[i] if ops[s]["key"] == ops[i]["key"]], default=0.0)
     pri = []
     for i in range(n):
         b, (t, c) = ops[i]["bonus"], ops[i]["key"]
-        if c >= NCH or t < 0:
-            due = MIX["P"] * (t + 1) - bot[i]
-        else:
-            due = MIX["P"] * (t + 1) + MIX["skew"] * c - MIX["w"] * own[i]
-        pri.append((MIX.get(b, 0.0) if b else 0.0) - due + MIX["noise"] * ((i * 7919 + MIX["seed"] * 104729) % 1009) / 1009.0)
+        p = bot[i]
+        if c < NCH and t >= 0:
+            p -= MIX["skew"][t] * c
+        if b:
+            p += MIX[b][t] if b == "gcov" else MIX[b]
+        if ops[i]["cost"] < 0.5:
+            p += MIX["small"]
+        pri.append(p)
     need = [len(o["hard"] | o["soft"]) for o in ops]
     ready = [0.0] * n
     cand = {}
@@ -475,7 +463,7 @@ def schedule(ops):
                 continue
             f = free.get(q, 0.0) if q != "R" else 0.0
             lo = min(max(f, ready[i]) for i in l)
-            i = max((j for j in l if max(f, ready[j]) <= lo + MIX["slack"]), key=lambda j: (pri[j], -j))
+            i = max((j for j in l if max(f, ready[j]) <= lo + MIX.get("slack" + q, MIX["slack"])), key=lambda j: (pri[j], -j))
             s = max(f, ready[i])
             if best is None or s < best[0]:
                 best = (s, i, q)
@@ -490,7 +478,7 @@ def schedule(ops):
         free[q] = s + (0.1 if o["done"] else o["cost"])
         for j in succ[i]:
             need[j] -= 1
-            ready[j] = max(ready[j], end[i] + (hop if ops[j]["q"] != q else hop / 2) if i in ops[j]["hard"] else s)
+            ready[j] = max(ready[j], end[i] + (hop if ops[j]["q"] != q else same) if i in ops[j]["hard"] else s)
             if not need[j]:
                 cand.setdefault(ops[j]["q"], []).append(j)
     return order, start, end

@@ -9,21 +9,21 @@ NL = L // NCH
 J = 16 * NL
 LN2 = math.log(2.0)
 H = 16384.0
-KG = 2.0 ** 104
 U = 2.0 ** -20
 MAGIC = 768.0
 TAU = (1.5 * 2.0 ** -104, 1.5 * 2.0 ** -121)
-MIX = {'ecv': 2, 'gat': (4, 2, 2), 'g': 1.5, 'pe': 0.42, 'hop': 0.2, 'same': 0.15, 'remote': 3.0, 'slack': 0.2, 'skew': (1.0, 1.0, 1.0), 'small': 4.0, 'gcov': (0.0, -10.0, -20.0), 'top': 60.0, 'th': 10.0, 'idx': 5.0, 'ge': 0.0, 'slackV': 0.1, 'slackS': 0.1}
+LAST = 1.0 - 0.75 * CL
+MIX = {'ecv': 4, 'ecdue': 0.9, 'gat': (4, 4, 4, 5, 4, 4, 5, 4, 4), 'g': 1.7, 'pe': 0.42, 'hop': 0.25, 'same': 0.04, 'remote': 3.0, 'slack': 0.02, 'visit': 33.0, 'due': (0.5, 3.0, 5.5, 2.0, 6.0, 12.5, 0.5, 2.0, 8.0), 'step': (3.5, 3.75, 5.0), 'ex': -1.0, 'parts': 2, 'bw': 0.5, 'late': -500.0, 'gcov': (4.5, 4.5, 4.0, 4.0, 2.0, 4.0, 4.0, 4.0, 4.0), 'top': 60.0, 'th': 30.0, 'idx': 5.0, 'ge': -2.0, 'slackV': 0.3, 'slackS': 0.2, 'g5': 1, 'fv': 1, 'early': 0.0, 's3': (3, 3, 3, 4, 3, 4, 4, 3, 3), 'call': 0.03, 'seed': 1, 'rounds': 1500, 'zs': 2048}
 
-ZB = ["PO", "SR", "MS", "Q2", "SC", "W2", "SU"]
+ZB = ["FB", "PO", "SR", "MS", "Q2", "SC", "W2", "SU"]
 ZF = ["RR", "T1", "T2"]
-ZI_ = ["MI", "AI"]
-SCALED = {"IB": 1.0, "IH": 0.5, "IU": U, "N64": -64.0, "N128": -128.0, "HI": H, "NHI": -H, "HH": H / 2, "NHH": -H / 2, "H32": 32 * H}
+ZI_ = ["MI", "AI", "FI"]
+SCALED = {"IB": 1.0, "IH": 0.5, "IU": U, "N4": -4.0, "N64": -64.0, "N128": -128.0, "HI": H, "NHI": -H, "HH": H / 2, "NHH": -H / 2, "H32": 32 * H}
 BLOCK = {"BO": 1.0, "NBH": -H / 2}
 MATS = list(SCALED) + list(BLOCK) + ["KK", "TB", "E8"]
 SEL = ["I32", "BOA", "BOF", "E8A", "E8F", "NIF", "I14", "I52"]
 CONST = {"C1": 1.0, "C37": -37.0, "C45": -45.0, "CM": MAGIC}
-CONST.update({"O%d" % i: -0.75 * i for i in range(1, CL + 1)})
+CONST.update({"O%d" % i: -0.75 * i if i < CL else LAST - 4.0 for i in range(1, CL + 1)})
 
 SCRATCH = {
     "EVB": ("sbuf", [128, VIS * W], "bfloat16"), "EC": ("sbuf", [128, 2 * W], "bfloat16"), "DT": ("sbuf", [128, 2 * W], "bfloat16"),
@@ -31,24 +31,25 @@ SCRATCH = {
     "TR": ("sbuf", [128, 256], "float32"), "TI": ("sbuf", [128, 256], "int32"), "TA": ("sbuf", [128, 512], "int32"),
     "PL": ("sbuf", [128, 512], "uint16"),
     "DGI": ("sbuf", [128, 1024], "int32"), "DGB": ("sbuf", [128, 1024], "bfloat16"),
-    "SGI": ("sbuf", [128, NCH, 2, NL], "int32"), "ZI": ("sbuf", [128, VIS * L], "int32"), "ZO": ("sbuf", [128, VIS * L], "float32"),
+    "SGI": ("sbuf", [128, NCH, 2, NL], "int32"), "G0I": ("sbuf", [128, L], "int32"),
+    "ZI": ("sbuf", [128, VIS * L], "int32"), "ZO": ("sbuf", [128, VIS * L], "float32"),
     "SG8": ("sbuf", [128, VIS * L], "int32"), "SG8B": ("sbuf", [128, VIS * L], "bfloat16"),
     "ONE": ("sbuf", [128, 128], "float32"), "ON32": ("sbuf", [128, 128], "float32"),
     "SEL": ("sbuf", [128, 128 * len(SEL)], "float32"), "SCN": ("sbuf", [128, 128 * len(MATS)], "bfloat16"),
     "ZK": ("sbuf", [128, 144], "bfloat16"), "CT": ("sbuf", [128, NL * len(CONST)], "bfloat16"),
     "KI": ("sbuf", [128, 2], "int32"), "KB": ("sbuf", [128, 2], "float32"), "THI": ("sbuf", [128, 2], "int32"), "NP": ("sbuf", [128, 2], "float32"),
-    "US": ("sbuf", [128, 2 * L], "uint16"), "ZU": ("sbuf", [128, L], "uint16"),
+    "UA": ("sbuf", [128, 2 * L], "uint16"), "UG": ("sbuf", [128, L], "uint16"),
     "PB": ("psum", [128, 512], "float32"),
 }
 for _t in range(VIS + 1):
-    SCRATCH["L%d" % _t] = ("sbuf", [128, 2 * L], "float32")
+    SCRATCH["LA%d" % _t] = ("sbuf", [128, (3 if _t else 2) * L], "float32")
+    SCRATCH["LG%d" % _t] = ("sbuf", [128, L], "float32")
     if _t:
-        SCRATCH["X%d" % _t] = ("sbuf", [128, 2 * L], "float32")
+        SCRATCH["XA%d" % _t] = ("sbuf", [128, 2 * L], "float32")
+        SCRATCH["XG%d" % _t] = ("sbuf", [128, L], "float32")
     if _t < VIS:
         SCRATCH["TH%d" % _t] = ("sbuf", [128, 4], "float32")
     if 0 < _t < VIS:
-        for _n in ("ZX", "ZS", "ZF"):
-            SCRATCH["%s%d" % (_n, _t)] = ("sbuf", [128, L], "float32")
         SCRATCH["RS%d" % _t] = ("sbuf", [128, 4], "float32")
 SEMAPHORES = ["qV", "qS", "qT", "qG", "lsend"]
 for _c in range(NCH):
@@ -59,13 +60,13 @@ for _c in range(NCH):
     for _n in ("XB", "CB"):
         SCRATCH["%s%d" % (_n, _c)] = ("psum", [128, 512], "float32")
     for _t in range(1, VIS + 1):
-        SEMAPHORES.append("aL%d_%d" % (_t, _c))
-        if _t < VIS:
-            SEMAPHORES.append("aZ%d_%d" % (_t, _c))
+        SEMAPHORES += ["aS%d_%d" % (_t, _c), "aG%d_%d" % (_t, _c)]
 DMAS = ["PTa", "PTb", "PN", "EV0", "EV1", "EV2", "Z0", "Z1", "S0", "G0", "SG", "D0", "D1"] + ["o%s%d" % (x, c) for x in "sg" for c in range(NCH)]
 SEMAPHORES += ["d_" + n for n in DMAS]
 PSUM = {n for n in SCRATCH if SCRATCH[n][0] == "psum"}
+FREE = {n for n in PSUM if n[:2] != "XB"}
 CY = 0.00083
+COSTS = [(1.5, 1.05, 0.2, 0.1, 3.2), (1.1, 1.1, 0.1, 0.05, 3.0), (1.56, 1.0, 0.1, 0.1, 2.5), (1.9, 1.3, 0.15, 0.1, 4.0), (1.3, 1.3, 0.3, 0.2, 4.0)]
 
 
 def vc(n):
@@ -111,7 +112,7 @@ def build():
     ops = []
 
     def op(q, cost, R, Wr, f, key, done=None, frm=None, bonus="", n=0):
-        ops.append({"q": q, "cost": cost, "R": [r[:3] for r in R], "W": [r[:3] for r in Wr], "f": f, "key": key, "done": done, "frm": frm, "bonus": bonus, "n": n})
+        ops.append({"q": q, "cost": cost, "R": R, "W": Wr, "f": f, "key": key, "done": done, "frm": frm, "bonus": bonus, "n": n})
 
     def V(n, R, Wr, f, key, bonus=""):
         op("V", vc(n), R, Wr, f, key, bonus=bonus, n=n)
@@ -170,7 +171,13 @@ def build():
             return y
         op("T", pc(cyc), R, Wr, f, key, bonus=bonus, n=cyc)
 
-    def gather(q, out, win, off, key, in1=None, bonus=""):
+    def gather(q, out, win, off, key, in1=None, bonus="", parts=1):
+        if parts > 1:
+            n = (off[2] - off[1]) // parts
+            for j in range(parts):
+                gather(q, (out[0], out[1] + 16 * n * j, out[1] + 16 * n * (j + 1)), win, (off[0], off[1] + n * j, off[1] + n * (j + 1)), key, None, bonus)
+            return
+
         def f(g, T, x):
             src = ap(T, win).indirect(ap(T, off))
             if in1:
@@ -190,9 +197,9 @@ def build():
     K0 = (-1, 0)
     for y in range(2):
         load("Y", "PT" + "ab"[y], [], [("PT", y, y + 1)], lambda g, T, x, y=y: g.sync.dma_start(T.PT[:, y:16:2, :], T.par[y:8:2, :]), 3.0)
-    load("S", "Z0", [], [al("ZI", 0, L)], lambda g, T, x: g.scalar.dma_start(T.ZI[:, 0:L], T.z[:, 0:L]), 2.4)
-    load("S", "S0", [], [("SGI", 0, 1)], lambda g, T, x: g.scalar.dma_start(T.SGI[:, :, 0, :], T.s0[:]), 2.4)
-    load("S", "G0", [], [("SGI", 1, 2)], lambda g, T, x: g.scalar.dma_start(T.SGI[:, :, 1, :], T.g0[:]), 2.6)
+    load("S", "Z0", [], [("SGI", 0, 1)], lambda g, T, x: g.scalar.dma_start(T.SGI[:, :, 0, :], T.z[:, 0:L]), 2.4)
+    load("S", "S0", [], [("SGI", 1, 2)], lambda g, T, x: g.scalar.dma_start(T.SGI[:, :, 1, :], T.s0[:]), 2.4)
+    load("S", "G0", [], [al("G0I")], lambda g, T, x: g.scalar.dma_start(T.G0I[:], T.g0[:]), 2.6)
     load("Y", "PN", [], [al("PN")], lambda g, T, x: g.sync.dma_start(T.PN[:], T.par[:]), 3.2)
     load("Y", "EV0", [], [al("EVB", 0, W)], lambda g, T, x: g.sync.dma_start(T.EVB[:, 0:W], T.ev[:]), 8.0)
     load("S", "SG", [], [al("SG8")], lambda g, T, x: g.scalar.dma_start(T.SG8[0:8, :], T.sg[:]), 3.0)
@@ -209,10 +216,16 @@ def build():
     op("G", 0.15, [], [("KI", 0, 1)], lambda g, T, x: g.iota(T.KI[:, 0:1], [[0, 1]], 0, 1), K0)
     op("G", 3.6, [al("E8F"), al("BOF"), al("I32"), ("KI", 0, 1)], [al("DT", 0, W // 2)], lambda g, T, x: g.iota(
         T.DT[:, 0:W // 2], [[0, W // 2]], 0, 0, allow_small_or_imprecise_dtypes=True), K0, bonus="top")
-    fill(al("DT", W // 2, 2 * W), 0.0, K0, bonus="top")
+    z1 = 2 * W - MIX["zs"]
+    fill(al("DT", W // 2, z1), 0.0, K0, bonus="top")
+    act(al("DT", z1, 2 * W), al("DT", W // 2, W // 2 + MIX["zs"]), F.Copy, K0, bonus="top")
     ts(("KI", 1, 2), ("KI", 0, 1), 15, None, A.bitwise_and, None, (0, 8))
     ts(("KB", 0, 1), ("KI", 1, 2), -LN2, -172.0 * LN2, A.mult, A.add, (0, 8))
-    fill(al("ZK"), 0.0, K0)
+
+    def const(out, v, key):
+        act(out, ("ONE", 0, size(out)), F.Copy, key, scale=v)
+    const(("ZK", 0, 128), 0.0, K0)
+    const(("ZK", 128, 144), 0.0, K0)
     b0 = al("BOF")[1]
     act(("ZK", 15, 143, 16), ("SEL", b0, b0 + 128, 16), F.Copy, K0)
     for n in SCALED:
@@ -223,19 +236,22 @@ def build():
         act(al(n), al("I32"), F.Copy, K0, scale=v)
     act(al("KK"), al("I52"), F.Copy, K0, scale=2.0 ** 52)
     act(al("E8"), al("E8F"), F.Copy, K0)
-    act(al("BOA"), al("I32"), F.Copy, K0, scale=2.0)
-    tt(al("TB"), al("BOA"), al("BOF"), A.subtract, (0, 8))
+    act(al("BOA"), al("BOF"), F.Copy, K0, scale=-1.0)
+    op("G", 0.4, [al("BOA")], [al("E8A")], lambda g, T, x: g.affine_select(ap(T, al("E8A")), ap(T, al("BOA")), [[-1, 128]], A.not_equal, 1.0, 0, 1), (0, 8))
+    act(al("TB"), al("E8A"), F.Copy, (0, 8))
     for n in CONST:
-        fill(al(n), CONST[n], (0, 8))
-    V(128, [], [al("ON32")], lambda g, T, x: g.vector.memset(T.ON32[:], -1.0 / 32), (0, 8))
+        const(al(n), CONST[n], (0, 8))
+    const(al("ON32"), -1.0 / 32, (0, 8))
     for j, v in enumerate((-11.5, -59.5, 4.5, -TAU[0])):
-        fill(("TH0", j, j + 1), v, (0, 8))
+        const(("TH0", j, j + 1), v, (0, 8))
     for c in range(NCH):
-        fill(("D0%d" % c, 0, 6 * NL, 6), -64.0, (0, 8))
+        const(("D0%d" % c, 0, 6 * NL, 6), -64.0, (0, 8))
+        const(("EE%d" % c, CL, 6 * NL, 6), 0.0, (0, 8))
 
-    cp(al("ZU"), al("ZI", 0, L), K0)
-    V(2 * L, [("SGI", 0, 2)], [al("US")], lambda g, T, x: g.vector.tensor_copy(T.US[:], T.SGI[:]), K0)
-    V(2 * L, [("SGI", 0, 2)], [al("L0")], lambda g, T, x: g.vector.tensor_copy(T.L0[:], T.SGI[:]), K0)
+    V(2 * L, [("SGI", 0, 2)], [al("UA")], lambda g, T, x: g.vector.tensor_copy(T.UA[:], T.SGI[:]), K0)
+    V(2 * L, [("SGI", 0, 2)], [al("LA0")], lambda g, T, x: g.vector.tensor_copy(T.LA0[:], T.SGI[:]), K0)
+    cp(al("UG"), al("G0I"), K0)
+    cp(al("LG0"), al("G0I"), K0)
     V(256, [("PT", 0, 16)], [al("PF")], lambda g, T, x: g.vector.tensor_copy(T.PF[:], T.PT[:]), K0)
     V(256, [al("PF")], [al("TR")], lambda g, T, x: g.vector.transpose(T.TR[:], T.PF[:]), K0)
     for q3 in range(8):
@@ -247,54 +263,65 @@ def build():
         ts(("DGI", d * 512, d * 512 + 512, 2), al("PN"), m, None, A.bitwise_and, None, (0, 5))
         ts(("DGI", d * 512 + 1, d * 512 + 512, 2), al("PN"), 12, m, A.logical_shift_right, A.bitwise_and, (0, 5))
         ts(al("DGB", d * 512, d * 512 + 512), al("DGI", d * 512, d * 512 + 512), 64 * U, None, A.mult, None, (0, 5))
-        load("Y", "D%d" % d, [al("DGB", d * 512, d * 512 + 512)], [al("DT")], lambda g, T, x, d=d: g.sync.dma_start(
+        load("Y", "D%d" % d, [al("DGB", d * 512, d * 512 + 512)], [("DT", d, 2 * W, 2)], lambda g, T, x, d=d: g.sync.dma_start(
             T.DT[d:128:16, :], T.DGB[:, d * 512:d * 512 + 512]), 2.5, (0, 5))
     V(576, [al("SG8")], [al("SG8B")], lambda g, T, x: g.vector.tensor_copy(T.SG8B[0:8, :], T.SG8[0:8, :]), (0, 6))
-    for b in range(4):
+    for b in range(8):
         hf, s = b // 2, b % 2
-        gather("V" if b < MIX["ecv"] else "S", ("EC", hf * W + s, hf * W + W, 2), al("EVB", 0, W), al("PL", s * 256 + hf * 128, s * 256 + hf * 128 + 128), (0, 4))
+        gather("V" if b < MIX["ecv"] else "S", ("EC", hf * 2048 + s, hf * 2048 + 2048, 2), al("EVB", 0, W), al("PL", s * 256 + hf * 64, s * 256 + hf * 64 + 64), (0, 4),
+               bonus=MIX["ecdue"])
     load("Y", "Z1", [al("EC")], [al("ZI", L, VIS * L)], lambda g, T, x: g.sync.dma_start(T.ZI[:, L:VIS * L], T.z[:, L:VIS * L]), 3.0, (0, 9))
     for t in range(1, VIS):
         load("Y", "EV%d" % t, [al("EC")], [al("EVB", t * W, t * W + W)], lambda g, T, x, t=t: g.sync.dma_start(T.EVB[:, t * W:t * W + W], T.ev[:]), 8.0, (0, 9))
         ts(al("ZO", t * L, t * L + L), al("ZI", t * L, t * L + L), float(t * W), None, A.add, None, (t - 1, 9))
 
+    def meets(t, c, out, first, step):
+        e = "%d" % c
+        tt((out + e, first, 6 * NL, step), ("XB" + e, first, 6 * NL, step), ("GE" + e, first, 6 * NL, step), A.is_equal, (t, c))
+
     def stays(t, c, first, step):
         e, n = "%d" % c, 6 // step
-        vv = ("CB" + e, NL, NL + n * NL)
-        tt(("EE" + e, first, 6 * NL, step), ("XB" + e, first, 6 * NL, step), ("GE" + e, first, 6 * NL, step), A.is_equal, (t, c))
-        mm([(vv, [("IB", ("FF" + e, first, 6 * NL, step))] + [("N64", zr("PO", c), (vv[0], NL + j, vv[2], n)) for j in range(n)]
+        v0 = NL * (1, 3, 5)[first - 1]
+        vv = ("CB" + e, v0, v0 + n * NL)
+        mm([(vv, [("IB", ("FF" + e, first, 6 * NL, step))] + [("N64", zr("PO", c), (vv[0], v0 + j, vv[2], n)) for j in range(n)]
              + [("N128", ("EE" + e, first, 6 * NL, step))], True)], (t, c))
         act(("D0" + e, first, 6 * NL, step), vv, F.Sign, (t, c), bias=("TH%d" % t, 1, 2), scale=-1.0)
+
+    def lanes(t, c):
+        o = c * NL * (3 if t else 2)
+        return [("LA%d" % t, o + j * NL, o + j * NL + NL) for j in range(3)] + [("LG%d" % t, c * NL, c * NL + NL)]
+
+    def join(a, b):
+        return (a[0], a[1], b[2])
 
     def walk(t, c):
         k = (t, c)
         o, e = c * NL, "%d" % c
-        ex, cm, dg, ix, xb, cb, ff, ee = "EX" + e, "CM" + e, "DG" + e, "IDX" + e, "XB" + e, "CB" + e, "FF" + e, "EE" + e
-        lS, lG = ("L%d" % t, 2 * o, 2 * o + NL), ("L%d" % t, 2 * o + NL, 2 * o + 2 * NL)
+        ex, cm, dg, ix, xb, cb, ff = "EX" + e, "CM" + e, "DG" + e, "IDX" + e, "XB" + e, "CB" + e, "FF" + e
+        zf, lS, zx, lG = lanes(t, c)
         th = "TH%d" % t
         m1, m2 = (cb, 6 * NL, 7 * NL), (cb, 7 * NL, 8 * NL)
         PO, g5 = zr("PO", c), ("GE" + e, CL, 6 * NL, 6)
+        uz, us, ug = ("UA", 2 * o, 2 * o + NL), ("UA", 2 * o + NL, 2 * o + 2 * NL), ("UG", o, o + NL)
         e8 = al("E8")
         if t:
-            zx, zf = ("ZX%d" % t, o, o + NL), ("ZF%d" % t, o, o + NL)
-            op("R", MIX["remote"], [("ZS%d" % t, o, o + NL)], [zx], None, k, done="aZ%d_%d" % (t, c), frm=-1)
+            op("R", MIX["remote"], [("XA%d" % t, 2 * o, 2 * o + 2 * NL)], [join(lS, zx)], None, k, done="aS%d_%d" % (t, c), frm=-1, bonus="early")
             tt(zf, zx, ("ZO", t * L + o, t * L + o + NL), A.min, k)
-            cp(("ZU", o, o + NL), zf, k)
-            act(zr("SR", c), zx, F.Sign, k, bias=-0.875 * H, acc=("RS%d" % t, c, c + 1))
-            lo = ("L%d" % t, 2 * o, 2 * o + 2 * NL)
-            op("R", MIX["remote"], [("X%d" % t, 2 * o, 2 * o + 2 * NL)], [lo], None, k, done="aL%d_%d" % (t, c), frm=-1)
-            cp(("US", 2 * o, 2 * o + 2 * NL), lo, k)
+            cp(join(uz, us), join(zf, lS), k)
+            act(zr("SR", c), zx, F.Sign, k, bias=-0.875 * H, acc=("RS%d" % t, c, c + 1), bonus="early")
+            op("R", MIX["remote"], [("XG%d" % t, o, o + NL)], [lG], None, k, done="aG%d_%d" % (t, c), frm=-1)
+            cp(ug, lG, k, bonus="ge")
 
         def fp(g, T, x):
             y = g.tensor.matmul(ap(T, m1), T.SCN[0:8, e8[1]:e8[2]], T.SG8B[0:8, t * L + o:t * L + o + NL], True, not t)
             return g.tensor.matmul(ap(T, m1), ap(T, al("IH")), ap(T, zr("SR", c)), False, True) if t else y
         op("T", pc(2 * NL), [e8, al("SG8B")] + ([al("IH"), zr("SR", c)] if t else []), [m1], fp, k, n=2 * NL)
         act(PO, m1, F.Relu, k, bias=-0.5 if t else 0.0)
-        gather("S", al(ex), al("EVB", 0, (t + 1) * W), ("ZU", o, o + NL), k)
-        gather("V", al(cm), al("EVB", 0, W), ("US", 2 * o, 2 * o + NL), k, in1=al(ex))
+        gather("S", al(ex), al("EVB", 0, (t + 1) * W), uz, k, bonus=MIX["ex"], parts=MIX["parts"])
+        gather("V", al(cm), al("EVB", 0, W), us, k, in1=al(ex), bonus=0.0)
 
         def gates():
-            gather("V", al("CG" + e), al("EVB", 0, W), ("US", 2 * o + NL, 2 * o + 2 * NL), k, in1=al(ex), bonus="gcov")
+            gather("V", al("CG" + e), al("EVB", 0, W), ug, k, in1=al(ex), bonus=MIX["gcov"][3 * t + c])
             fold(m1, "CG" + e, k)
             act(zr("MS", c), m1, F.Sign, k, bias=(th, 0, 1))
             mm([(m1, [("BO", zr("MS", c)), ("N64", PO)], True)], k)
@@ -302,73 +329,97 @@ def build():
 
         for i in range(CL + 1):
             xi, fi = (xb, i, 6 * NL, 6), (ff, i + 1, 6 * NL, 6)
-            if i == MIX["gat"][c]:
+            if i == MIX["gat"][3 * t + c]:
                 gates()
             if i:
                 if i < CL:
-                    gather("V", al(cm), al("EC"), al(ix), k, in1=al(ex))
-                gather("S", al(dg), al("DT"), al(ix), k)
+                    gather("V", al(cm), al("EC"), al(ix), k, in1=al(ex), bonus=float(i))
+                gather("S", al(dg), al("DT"), al(ix), k, bonus=float(i), parts=MIX["parts"])
             if i < CL:
                 fold((cb, 0, NL), cm, k)
                 act(fi, (cb, 0, NL), F.Identity, k, bias=16.0, scale=-1.0)
             if i:
                 fold(xi, dg, k, close=False)
-                mm([(xi, [("IB", al("O%d" % i))] + ([("IU", fi)] if i < CL else []), False)], k)
+                mm([(xi, [("IB", al("O%d" % i)), ("IU", fi) if i < CL else ("N4", ("D0" + e, CL, 6 * NL, 6))], False)], k)
             else:
                 mm([(xi, [("I14", lS), ("IU", fi)], True)], k)
             if i < CL:
                 ts(al(ix), xi, 2.0 ** 15, 7.5 / 32 + 0.75 * i * 2.0 ** 15, A.mult, A.add, k, bonus="idx")
+            if i == CL - 1:
+                stays(t, c, 2, 3)
             if i == 0:
-                mm([(m2, [("I14", lG), ("IB", PO)], True), ((xb, 6 * NL, 7 * NL), [("I32", lS), ("HI", PO)], True)], k)
-                act(g5, m2, F.Identity, k, bias=-0.75 * CL)
-            elif i < CL:
-                mm([(m2, [("I32", g5), ("IU", fi)], True)], k, bonus="ge")
-                act(("GE" + e, i, 6 * NL, 6), m2, F.Identity, k, bias=0.75 * (CL - i), bonus="ge")
+                mm([((xb, 6 * NL, 7 * NL), [("I32", lS), ("HI", PO)], True), ((xb, 7 * NL, 8 * NL), [("HI", al("C1")), ("NHI", PO)], True)], k, bonus="ge")
+            if i == MIX["g5"]:
+                mm([(m2, [("I14", lG), ("IB", PO)], True)], k, bonus="ge")
+                act(g5, m2, F.Identity, k, bias=LAST, bonus="ge")
+            if i >= MIX["g5"]:
+                for j in range(1 if i == MIX["g5"] else i, min(i + 1, CL)):
+                    mm([(m2, [("I32", g5), ("IU", (ff, j + 1, 6 * NL, 6))], True)], k, bonus="ge")
+                    act(("GE" + e, j, 6 * NL, 6), m2, F.Identity, k, bias=-0.75 * j - LAST, bonus="ge")
+            if i in (2, 3):
+                meets(t, c, "EE", i, 6)
+            if i == CL - 1:
+                meets(t, c, "EE", 1, 3)
+            if i == MIX["s3"][3 * t + c]:
+                stays(t, c, 3, 6)
             if i == CL - 1:
                 stays(t, c, 1, 3)
-                stays(t, c, 3, 6)
 
     def epilogue(t, c):
         k = (t, c)
         o, e = c * NL, "%d" % c
-        xb, cb, ff, ee, mmn, th = "XB" + e, "CB" + e, "FF" + e, "EE" + e, "MM" + e, "TH%d" % t
-        lG = ("L%d" % t, 2 * o + NL, 2 * o + 2 * NL)
-        m1, m2, vv = (cb, 6 * NL, 7 * NL), (cb, 7 * NL, 8 * NL), (cb, NL, 6 * NL)
+        xb, cb, mmn, th = "XB" + e, "CB" + e, "MM" + e, "TH%d" % t
+        zf, lS, zx, lG = lanes(t, c)
+        m1, m2 = (cb, 6 * NL, 7 * NL), (cb, 7 * NL, 8 * NL)
         PO, M6 = zr("PO", c), (mmn, 5, 6 * NL, 6)
+        last = t + 1 == VIS
+        to = "home" if last else "next"
+        xs, xz, xg = ("XA%d" % (t + 1), 2 * o, 2 * o + NL), ("XA%d" % (t + 1), 2 * o + NL, 2 * o + 2 * NL), ("XG%d" % (t + 1), o, o + NL)
+        _, nS, nz, nG = lanes(t + 1, c)
 
         def Z(n):
             return zr(n, c)
-        stays(t, c, 2, 3)
+
+        def send(dst, src, sem):
+            op("G", 0.1, [src], [], lambda g, T, x: x["send"](ap(T, dst), ap(T, src), sem, to), k)
+
+        def home(dst, src, sem, q, out):
+            op("R", MIX["remote"], [src], [dst], None, k, done=sem, frm=2)
+            load(q, "o%s%d" % (out, c), [dst], [], lambda g, T, x: (g.sync if q == "Y" else g.scalar).dma_start(T["y" + out][:, o:o + NL], ap(T, dst)), 2.0, k)
+        meets(t, c, "D0", CL, 6)
         V(6 * NL, [al("D0" + e), (xb, 0, 6 * NL)], [al(mmn)], lambda g, T, x: g.vector.tensor_tensor_scan(
             T[mmn][:], T["D0" + e][:], T[xb][:, 0:6 * NL], 0.0, A.add, A.max), k)
-        act(Z("RR"), M6, F.Identity, k, bias=MAGIC)
-        mm([(m1, [("NIF", Z("RR")), ("IB", al("CM")), ("I32", M6)], True)], k)
-        xr, xn, xu, xg = (xb, 0, NL), (xb, NL, 2 * NL), (xb, 2 * NL, 3 * NL), (xb, 7 * NL, 8 * NL)
-        neg = (xn, [("HI", al("C1")), ("NHI", PO)], True)
-        if t + 1 < VIS:
-            act(Z("SC"), m1, F.Sign, k, bias=(th, 2, 3), scale=-1.0 / U)
-        act(Z("W2"), m1, F.Exp, k, bias=("KB", 0, 1), scale=17.0 * LN2 / U)
-        if t + 1 < VIS:
-            mm([neg, (xr, [("NHI", Z("Q2")), ("NHI", al("C45")), ("H32", PO), ("NBH", Z("SC"))], True)], k)
-            zs, zx = ("ZS%d" % (t + 1), o, o + NL), ("ZX%d" % (t + 1), o, o + NL)
-            tt(zs, xr, ("ZF%d" % t, o, o + NL) if t else ("ZI", o, o + NL), A.max, k)
-            op("G", 0.1, [zs], [], lambda g, T, x: x["send"](ap(T, zx), ap(T, zs), "aZ%d_%d" % (t + 1, c), "next"), k)
-        else:
-            mm([neg], k)
         ts(Z("MI"), M6, 1.0 / U, None, A.mult, None, k)
+        if MIX["fv"]:
+            ts(Z("FI"), Z("MI"), 63, None, A.bitwise_and, None, k)
+            cp(Z("FB"), Z("FI"), k)
+            fs, fu = Z("FB"), 1.0
+        else:
+            act(Z("RR"), M6, F.Identity, k, bias=MAGIC)
+            mm([(m1, [("NIF", Z("RR")), ("IB", al("CM")), ("I32", M6)], True)], k)
+            fs, fu = m1, 1.0 / U
+        if not last:
+            act(Z("SC"), fs, F.Sign, k, bias=(th, 2, 3), scale=-fu)
+        act(Z("W2"), fs, F.Exp, k, bias=("KB", 0, 1), scale=17.0 * LN2 * fu)
         ts(Z("AI"), Z("MI"), 6, 4095, A.arith_shift_right, A.bitwise_and, k)
+        tt(Z("T1"), (xb, 7 * NL, 8 * NL), Z("AI"), A.add, k)
+        tt(xs, (xb, 6 * NL, 7 * NL), Z("T1"), A.min, k)
+        xr, xu, xn = (xb, 0, NL), (xb, NL, 2 * NL), (xb, 2 * NL, 3 * NL)
+        if not last:
+            mm([(xr, [("NHI", Z("Q2")), ("NHI", al("C45")), ("H32", PO), ("NBH", Z("SC"))], True)], k)
+            tt(xz, xr, zf, A.max, k)
+            send(join(nS, nz), join(xs, xz), "aS%d_%d" % (t + 1, c))
+        else:
+            send(nS, xs, "aS%d_%d" % (t + 1, c))
+            home(nS, xs, "aS%d_%d" % (t + 1, c), "Y", "s")
         mm([(m2, [("KK", Z("Q2")), ("KK", al("C37")), ("KK", PO), ("TB", Z("W2"))], True)], k)
-        tt(Z("T1"), xn, Z("AI"), A.add, k)
         act(Z("SU"), m2, F.Sign, k, bias=(th, 3, 4))
-        mm([(xu, [("HH", al("C1")), ("NHH", Z("SU"))], True), (xg, [("I32", lG), ("HH", al("C1")), ("HH", Z("SU"))], True)], k)
+        mm([(xu, [("HH", al("C1")), ("NHH", Z("SU"))], True), (xn, [("I32", lG), ("HH", al("C1")), ("HH", Z("SU"))], True)], k)
         tt(Z("T2"), xu, Z("AI"), A.add, k)
-        xo, lo = ("X%d" % (t + 1), 2 * o, 2 * o + 2 * NL), ("L%d" % (t + 1), 2 * o, 2 * o + 2 * NL)
-        tt(xo, (xb, 6 * NL, 8 * NL), (Z("T1")[0], Z("T1")[1], Z("T2")[2]), A.min, k)
-        op("G", 0.1, [xo], [], lambda g, T, x: x["send"](ap(T, lo), ap(T, xo), "aL%d_%d" % (t + 1, c), "next" if t + 1 < VIS else "home"), k)
-        if t + 1 == VIS:
-            op("R", MIX["remote"], [xo], [lo], None, k, done="aL%d_%d" % (VIS, c), frm=2)
-            load("Y", "os%d" % c, [lo], [], lambda g, T, x: g.sync.dma_start(T.ys[:, o:o + NL], T[lo[0]][:, 2 * o:2 * o + NL]), 2.0, k)
-            load("S", "og%d" % c, [lo], [], lambda g, T, x: g.scalar.dma_start(T.yg[:, o:o + NL], T[lo[0]][:, 2 * o + NL:2 * o + 2 * NL]), 2.0, k)
+        tt(xg, xn, Z("T2"), A.min, k)
+        send(nG, xg, "aG%d_%d" % (t + 1, c))
+        if last:
+            home(nG, xg, "aG%d_%d" % (t + 1, c), "S", "g")
 
     def thresh(t):
         k, b, rs, th = (t, 8), "th", "RS%d" % t, "TH%d" % t
@@ -384,44 +435,48 @@ def build():
         act((th, 3, 4), ("NP", 0, 1), F.Identity, k, bias=-TAU[0], scale=TAU[1] - TAU[0], bonus=b)
 
     for t in range(VIS):
-        if t:
-            n0 = len(ops)
+        n0 = len(ops)
         for c in range(NCH):
             walk(t, c)
         if t:
             n1 = len(ops)
             thresh(t)
-            early = [o for o in ops[n0:n1] if any(w[0] in ("ZX%d" % t, "RS%d" % t) for w in o["W"])]
-            ops[n0:] = early + ops[n1:] + [o for o in ops[n0:n1] if not any(w[0] in ("ZX%d" % t, "RS%d" % t) for w in o["W"])]
+            ops[n0:] = [o for o in ops[n0:n1] if o["bonus"] == "early"] + ops[n1:] + [o for o in ops[n0:n1] if o["bonus"] != "early"]
         for c in range(NCH):
             epilogue(t, c)
     return ops
 
 
-def depend(ops):
+def columns(lo, hi, step=1):
+    return (1 << hi) - (1 << lo) if step == 1 else sum(1 << j for j in range(lo, hi, step))
+
+
+def depend(ops, free=()):
     acc, bank = {}, {}
     for n, o in enumerate(ops):
         o["hard"], o["soft"] = set(), set()
-        for wr, regs in ((0, o["R"]), (1, o["W"])):
-            for b, lo, hi in regs:
-                for (m, w2, l2, h2) in acc.get(b, ()):
-                    if m != n and (wr or w2) and lo < h2 and l2 < hi:
+        o["bank"] = next((r[0] for r in o["R"] + o["W"] if r[0] in free), None)
+        both = [(wr, [(r[0], columns(*r[1:])) for r in regs]) for wr, regs in ((0, o["R"]), (1, o["W"]))]
+        for wr, regs in both:
+            for b, cols in regs:
+                for (m, w2, c2) in acc.get(b, ()):
+                    if m != n and (wr or w2) and cols & c2:
                         if wr and not w2 and ops[m]["q"] == o["q"] and not ops[m]["done"]:
                             o["soft"].add(m)
                         elif o["q"] == "T" and ops[m]["q"] == "T" and b in PSUM:
                             o["soft"].add(m)
                         else:
                             o["hard"].add(m)
-                if b in PSUM:
+                if b in PSUM and b not in free:
                     for q, m in bank.get(b, {}).items():
                         if m != n:
                             (o["soft"] if q == o["q"] else o["hard"]).add(m)
-        for wr, regs in ((0, o["R"]), (1, o["W"])):
-            for b, lo, hi in regs:
+        for wr, regs in both:
+            for b, cols in regs:
                 if wr:
-                    acc[b] = [a for a in acc.get(b, []) if not (lo <= a[2] and a[3] <= hi and a[0] != n)] + [(n, 1, lo, hi)]
+                    acc[b] = [a for a in acc.get(b, []) if a[2] & ~cols or a[0] == n] + [(n, 1, cols)]
                 else:
-                    acc.setdefault(b, []).append((n, 0, lo, hi))
+                    acc.setdefault(b, []).append((n, 0, cols))
                 if b in PSUM:
                     bank.setdefault(b, {})[o["q"]] = n
     return ops
@@ -440,13 +495,12 @@ def schedule(ops):
     pri = []
     for i in range(n):
         b, (t, c) = ops[i]["bonus"], ops[i]["key"]
-        p = bot[i]
-        if c < NCH and t >= 0:
-            p -= MIX["skew"][t] * c
-        if b:
-            p += MIX[b][t] if b == "gcov" else MIX[b]
-        if ops[i]["cost"] < 0.5:
-            p += MIX["small"]
+        if isinstance(b, float):
+            p = -(MIX["visit"] * t + (MIX["due"][3 * t + c] if c < NCH else 0.0) + MIX["step"][t] * b)
+        elif c < NCH and t >= 0:
+            p = 1000.0 + bot[i] * MIX["bw"] - MIX["due"][3 * t + c] + MIX.get(b, 0.0)
+        else:
+            p = MIX["late"] + bot[i] + MIX.get(b, 0.0) if t >= 0 and c > 7 and not b else 1000.0 + bot[i] + MIX.get(b, 0.0)
         pri.append(p)
     need = [len(o["hard"] | o["soft"]) for o in ops]
     ready = [0.0] * n
@@ -484,12 +538,150 @@ def schedule(ops):
     return order, start, end
 
 
+def prices(ops, costs):
+    gat, slow, hop, same, far = costs
+    cost = []
+    for o in ops:
+        q, n = o["q"], o["n"]
+        if q in "VS" and not o["done"]:
+            cost.append(0.055 + -n * CY * gat * slow if n < 0 else max(64, n) * CY * slow + MIX["call"])
+        else:
+            cost.append(n * MIX["pe"] * 1e-3 * slow + 0.03 if q == "T" else far if q == "R" else o["cost"])
+    return cost, [0.0 if o["q"] == "R" else 0.1 if o["done"] else c for o, c in zip(ops, cost)]
+
+
+def replay(ops, order, costs, price):
+    hop, same = costs[2], costs[3]
+    cost, hold = price
+    free, end, user = {}, [0.0] * len(ops), {}
+    for i in order:
+        o = ops[i]
+        q, b = o["q"], o["bank"]
+        s = free.get(q, 0.0)
+        for m in o["hard"]:
+            e = end[m] + (same if ops[m]["q"] == q else hop)
+            if e > s:
+                s = e
+        if b:
+            u = user.setdefault(b, {})
+            for q2, e in u.items():
+                if q2 != q and e + hop > s:
+                    s = e + hop
+            u[q] = s + cost[i]
+        end[i] = s + cost[i]
+        if q != "R":
+            free[q] = s + hold[i]
+    return max(end)
+
+
+def pack(ops, lst, hold, pred, base, hop):
+    st, busy = [0.0] * len(ops), {}
+    for j in lst:
+        s = base[j]
+        for i, d in pred[j]:
+            if st[i] + d > s:
+                s = st[i] + d
+        h, q, b = hold[j], ops[j]["q"], ops[j]["bank"]
+        if h:
+            Q, B = busy.setdefault(q, []), busy.setdefault(b, []) if b else []
+            while True:
+                k = len(Q)
+                while k and Q[k - 1][1] > s + 1e-9:
+                    k -= 1
+                while k < len(Q) and Q[k][0] < s + h - 1e-9:
+                    s = Q[k][1]
+                    k += 1
+                late = [e + hop for a, e, q2 in B if q2 != q and a - hop < s + h - 1e-9 and e + hop > s + 1e-9]
+                if not late:
+                    break
+                s = max(late)
+            Q.insert(k, (s, s + h))
+            B.append((s, s + h, q))
+        st[j] = s
+    return st
+
+
+def ordered(key, pred):
+    seen, out = [False] * len(key), []
+    for j in sorted(range(len(key)), key=lambda i: key[i]):
+        stack = [j]
+        while stack:
+            y = stack[-1]
+            if seen[y]:
+                stack.pop()
+                continue
+            m = [i for i, d in pred[y] if not seen[i]]
+            if m:
+                stack += m
+            else:
+                seen[y] = True
+                out.append(y)
+                stack.pop()
+    return out
+
+
+def refine(ops, st, rounds):
+    n = len(ops)
+    hop, same = COSTS[0][2], COSTS[0][3]
+    price = [prices(ops, c) for c in COSTS]
+    cost, hold = price[0]
+    pred, back = [[] for _ in ops], [[] for _ in ops]
+    for j, o in enumerate(ops):
+        for i in o["hard"] | o["soft"]:
+            d = cost[i] + (same if ops[i]["q"] == o["q"] else hop) if i in o["hard"] else hold[i]
+            pred[j].append((i, d))
+            back[i].append((j, d - hold[i] + hold[j]))
+    zero, rest = [0.0] * n, [cost[i] - hold[i] for i in range(n)]
+    seed, best = [MIX["seed"]], None
+    big = [i for i in range(n) if ops[i]["n"] < 0]
+
+    def draw():
+        seed[0] = (seed[0] * 1103515245 + 12345) % 2147483648
+        return seed[0] / 2147483648.0
+    for r in range(rounds):
+        if r > 2:
+            mid, wide, amp, kind = draw() * max(best[1]), 3.0 + 17.0 * draw(), 0.1 + draw(), draw()
+            if kind < 0.4:
+                st = [s + amp * (2.0 * draw() - 1.0) if abs(s - mid) < wide else s for s in best[1]]
+            elif kind < 0.7:
+                c, amp = int(NCH * draw()), 8.0 * (draw() - 0.5)
+                st = [s + amp if abs(s - mid) < wide and o["key"][1] == c else s for s, o in zip(best[1], ops)]
+            else:
+                st = list(best[1])
+                for _ in range(1 + int(3 * draw())):
+                    st[big[int(len(big) * draw())]] += 10.0 * (draw() - 0.5)
+        rs = pack(ops, ordered([-st[i] - hold[i] for i in range(n)], back), hold, back, rest, hop)
+        st = pack(ops, ordered([-rs[i] - hold[i] for i in range(n)], pred), hold, pred, zero, hop)
+        order = ordered(st, pred)
+        v = sum(math.log(replay(ops, order, c, p)) for c, p in zip(COSTS, price))
+        if best is None or v < best[0]:
+            best = (v, st, order)
+    return best[2]
+
+
+PLAN = {}
+
+
+def plan(rounds=None):
+    start = schedule(depend(build()))[1]
+    ops = depend(build(), FREE)
+    order = refine(ops, start, rounds or MIX["rounds"])
+    user = {}
+    for i in order:
+        b, q = ops[i]["bank"], ops[i]["q"]
+        if b:
+            ops[i]["hard"] |= {m for q2, m in user.setdefault(b, {}).items() if q2 != q}
+            user[b][q] = i
+    return ops, order
+
+
 def rank_program(g, core, T, topo):
     rank = T.rank_of(core)
     if rank is None:
         return
-    ops = depend(build())
-    order, _, _ = schedule(ops)
+    if not PLAN:
+        PLAN["ops"], PLAN["order"] = plan()
+    ops, order = PLAN["ops"], PLAN["order"]
     place = {i: n for n, i in enumerate(order)}
     cores = T.cores
     to = {"next": cores[(rank + 1) % NR], "home": cores[(rank - 2) % NR]}

@@ -13,7 +13,7 @@ U = 2.0 ** -20
 MAGIC = 768.0
 TAU = (1.5 * 2.0 ** -104, 1.5 * 2.0 ** -121)
 LAST = 1.0 - 0.75 * CL
-MIX = {'ecv': 4, 'ecdue': 0.9, 'gat': (4, 4, 4, 5, 4, 4, 5, 4, 4), 'g': 1.7, 'pe': 0.42, 'hop': 0.25, 'same': 0.04, 'remote': 3.0, 'slack': 0.02, 'visit': 33.0, 'due': (0.5, 3.0, 5.5, 2.0, 6.0, 12.5, 0.5, 2.0, 8.0), 'step': (3.5, 3.75, 5.0), 'ex': -1.0, 'parts': 2, 'bw': 0.5, 'late': -500.0, 'gcov': (4.5, 4.5, 4.0, 4.0, 2.0, 4.0, 4.0, 4.0, 4.0), 'top': 60.0, 'th': 30.0, 'idx': 5.0, 'ge': -2.0, 'slackV': 0.3, 'slackS': 0.2, 'g5': 1, 'fv': 1, 'early': 0.0, 's3': (3, 3, 3, 4, 3, 4, 4, 3, 3), 'call': 0.03, 'seed': 1, 'rounds': 1500, 'zs': 2048}
+MIX = {'ecv': 4, 'ecdue': 0.78, 'gat': (4, 5, 5, 5, 4, 4, 5, 4, 4), 'g': 1.71, 'pe': 0.42, 'hop': 0.16, 'same': 0.04, 'remote': 3.2, 'slack': 0.02, 'visit': 35.6, 'due': (-0.7, 5.0, 8, 0.0, 8.0, 13.2, 0, 7.7, 16.7), 'step': (3.2, 4.18, 5.05), 'ex': -1.0, 'split': {(1, 2, 5): 'S', (2, 1, 5): 'SV', (2, 2, 5): 'SV', (0, 1, 0): 'S', (1, 0, 3): 'S', (2, 0, 5): 'S', (0, 2, 3): 'S', (2, 2, 0): 'S', (1, 1, 0): 'S', (2, 2, 4): 'S', (1, 2, 0): 'S', (0, 1, 1): 'S'}, 'bw': 0.1, 'late': -500.0, 'gcov': (4.5, 3.5, 4.0, 2.8, 3.0, 4.0, 4.0, 5.7, 4.0), 'top': 60.0, 'th': 26.9, 'idx': -2.7, 'ge': -8.3, 'slackV': 0.24, 'slackS': 0.1, 'g5': 1, 'fv': (1, 1, 1, 1, 1, 0, 1, 1, 1), 'early': 2.2, 's3': (4, 3, 3, 4, 4, 4, 4, 3, 4), 'call': 0.03, 'seed': 1, 'rounds': 2500, 'zs': 4096}
 
 ZB = ["FB", "PO", "SR", "MS", "Q2", "SC", "W2", "SU"]
 ZF = ["RR", "T1", "T2"]
@@ -28,16 +28,17 @@ CONST.update({"O%d" % i: -0.75 * i if i < CL else LAST - 4.0 for i in range(1, C
 SCRATCH = {
     "EVB": ("sbuf", [128, VIS * W], "bfloat16"), "EC": ("sbuf", [128, 2 * W], "bfloat16"), "DT": ("sbuf", [128, 2 * W], "bfloat16"),
     "PN": ("sbuf", [128, 256], "int32"), "PT": ("sbuf", [128, 16, 16], "int32"), "PF": ("sbuf", [128, 256], "float32"),
-    "TR": ("sbuf", [128, 256], "float32"), "TI": ("sbuf", [128, 256], "int32"), "TA": ("sbuf", [128, 512], "int32"),
+    "TR": ("sbuf", [128, 256], "float32"), "TI": ("sbuf", [128, 256], "int32"), "TA": ("sbuf", [128, 2, 256], "int32"),
+    "ZR": ("sbuf", [128, 128], "bfloat16"),
     "PL": ("sbuf", [128, 512], "uint16"),
     "DGI": ("sbuf", [128, 1024], "int32"), "DGB": ("sbuf", [128, 1024], "bfloat16"),
     "SGI": ("sbuf", [128, NCH, 2, NL], "int32"), "G0I": ("sbuf", [128, L], "int32"),
-    "ZI": ("sbuf", [128, VIS * L], "int32"), "ZO": ("sbuf", [128, VIS * L], "float32"),
+    "ZI": ("sbuf", [128, VIS * L], "int32"), "ZO": ("psum", [128, 512], "float32"),
     "SG8": ("sbuf", [128, VIS * L], "int32"), "SG8B": ("sbuf", [128, VIS * L], "bfloat16"),
     "ONE": ("sbuf", [128, 128], "float32"), "ON32": ("sbuf", [128, 128], "float32"),
     "SEL": ("sbuf", [128, 128 * len(SEL)], "float32"), "SCN": ("sbuf", [128, 128 * len(MATS)], "bfloat16"),
     "ZK": ("sbuf", [128, 144], "bfloat16"), "CT": ("sbuf", [128, NL * len(CONST)], "bfloat16"),
-    "KI": ("sbuf", [128, 2], "int32"), "KB": ("sbuf", [128, 2], "float32"), "THI": ("sbuf", [128, 2], "int32"), "NP": ("sbuf", [128, 2], "float32"),
+    "KI": ("sbuf", [128, 2], "int32"), "KB": ("sbuf", [128, 2], "float32"), "KW": ("sbuf", [128, 2], "float32"), "THI": ("sbuf", [128, 2], "int32"), "NP": ("sbuf", [128, 2], "float32"),
     "UA": ("sbuf", [128, 2 * L], "uint16"), "UG": ("sbuf", [128, L], "uint16"),
     "PB": ("psum", [128, 512], "float32"),
 }
@@ -60,13 +61,14 @@ for _c in range(NCH):
     for _n in ("XB", "CB"):
         SCRATCH["%s%d" % (_n, _c)] = ("psum", [128, 512], "float32")
     for _t in range(1, VIS + 1):
-        SEMAPHORES += ["aS%d_%d" % (_t, _c), "aG%d_%d" % (_t, _c)]
+        SEMAPHORES += ["aS%d_%d" % (_t, _c)] + ["aG%d_%d" % (_t, _c)] * (_t < VIS)
 DMAS = ["PTa", "PTb", "PN", "EV0", "EV1", "EV2", "Z0", "Z1", "S0", "G0", "SG", "D0", "D1"] + ["o%s%d" % (x, c) for x in "sg" for c in range(NCH)]
 SEMAPHORES += ["d_" + n for n in DMAS]
 PSUM = {n for n in SCRATCH if SCRATCH[n][0] == "psum"}
 FREE = {n for n in PSUM if n[:2] != "XB"}
 CY = 0.00083
-COSTS = [(1.5, 1.05, 0.2, 0.1, 3.2), (1.1, 1.1, 0.1, 0.05, 3.0), (1.56, 1.0, 0.1, 0.1, 2.5), (1.9, 1.3, 0.15, 0.1, 4.0), (1.3, 1.3, 0.3, 0.2, 4.0)]
+COSTS = [(1.5, 1.05, 0.2, 0.1, 2.8, 0.3, 2.0, 7.5), (1.1, 1.1, 0.1, 0.05, 2.5, 0.2, 1.0, 6.5), (1.56, 1.0, 0.1, 0.1, 2.0, 0.5, 1.5, 7.0),
+         (1.9, 1.3, 0.15, 0.1, 3.5, 0.3, 3.0, 8.5), (1.3, 1.3, 0.3, 0.2, 3.5, 0.6, 2.0, 8.0)]
 
 
 def vc(n):
@@ -111,8 +113,8 @@ def ap(T, r):
 def build():
     ops = []
 
-    def op(q, cost, R, Wr, f, key, done=None, frm=None, bonus="", n=0):
-        ops.append({"q": q, "cost": cost, "R": R, "W": Wr, "f": f, "key": key, "done": done, "frm": frm, "bonus": bonus, "n": n})
+    def op(q, cost, R, Wr, f, key, done=None, frm=None, bonus="", n=0, send=None):
+        ops.append({"q": q, "cost": cost, "R": R, "W": Wr, "f": f, "key": key, "done": done, "frm": frm, "bonus": bonus, "n": n, "send": send})
 
     def V(n, R, Wr, f, key, bonus=""):
         op("V", vc(n), R, Wr, f, key, bonus=bonus, n=n)
@@ -147,13 +149,13 @@ def build():
         V(size(out) // 2, [], [out], lambda g, T, x: g.vector.memset(ap(T, out), v), key, bonus)
 
     def act(out, a, fn, key, bias=0.0, scale=1.0, acc=None, bonus=""):
-        R = [a] + [s for s in (bias,) if isinstance(s, tuple)]
+        R = [a] + [s for s in (bias, scale) if isinstance(s, tuple)]
 
         def f(g, T, x):
-            b = ap(T, bias) if isinstance(bias, tuple) else bias
+            b, m = [ap(T, s) if isinstance(s, tuple) else s for s in (bias, scale)]
             if acc:
-                return g.scalar.activation(ap(T, out), ap(T, a), fn, bias=b, scale=scale, accum_out=ap(T, acc))
-            return g.scalar.activation(ap(T, out), ap(T, a), fn, bias=b, scale=scale)
+                return g.scalar.activation(ap(T, out), ap(T, a), fn, bias=b, scale=m, accum_out=ap(T, acc))
+            return g.scalar.activation(ap(T, out), ap(T, a), fn, bias=b, scale=m)
         S(size(out), R, [out] + ([acc] if acc else []), f, key, bonus)
 
     def mm(groups, key, bonus="", close=True):
@@ -171,11 +173,11 @@ def build():
             return y
         op("T", pc(cyc), R, Wr, f, key, bonus=bonus, n=cyc)
 
-    def gather(q, out, win, off, key, in1=None, bonus="", parts=1):
-        if parts > 1:
-            n = (off[2] - off[1]) // parts
-            for j in range(parts):
-                gather(q, (out[0], out[1] + 16 * n * j, out[1] + 16 * n * (j + 1)), win, (off[0], off[1] + n * j, off[1] + n * (j + 1)), key, None, bonus)
+    def gather(q, out, win, off, key, in1=None, bonus=""):
+        if len(q) > 1:
+            n = (off[2] - off[1]) // len(q)
+            for j in range(len(q)):
+                gather(q[j], (out[0], out[1] + 16 * n * j, out[1] + 16 * n * (j + 1)), win, (off[0], off[1] + n * j, off[1] + n * (j + 1)), key, None, bonus)
             return
 
         def f(g, T, x):
@@ -216,20 +218,33 @@ def build():
     op("G", 0.15, [], [("KI", 0, 1)], lambda g, T, x: g.iota(T.KI[:, 0:1], [[0, 1]], 0, 1), K0)
     op("G", 3.6, [al("E8F"), al("BOF"), al("I32"), ("KI", 0, 1)], [al("DT", 0, W // 2)], lambda g, T, x: g.iota(
         T.DT[:, 0:W // 2], [[0, W // 2]], 0, 0, allow_small_or_imprecise_dtypes=True), K0, bonus="top")
-    z1 = 2 * W - MIX["zs"]
-    fill(al("DT", W // 2, z1), 0.0, K0, bonus="top")
-    act(al("DT", z1, 2 * W), al("DT", W // 2, W // 2 + MIX["zs"]), F.Copy, K0, bonus="top")
+    z0, z1 = W // 2, W // 2 + MIX["zs"]
+    fill(al("ZR"), 0.0, K0, bonus="top")
+    fill(al("DT", z0, z1), 0.0, K0, bonus="top")
+    for a in range(z1, 2 * W, z1 - z0):
+        n = min(z1 - z0, 2 * W - a)
+        act(al("DT", a, a + n), al("DT", z0, z0 + n), F.Copy, K0, bonus="top")
     ts(("KI", 1, 2), ("KI", 0, 1), 15, None, A.bitwise_and, None, (0, 8))
-    ts(("KB", 0, 1), ("KI", 1, 2), -LN2, -172.0 * LN2, A.mult, A.add, (0, 8))
+    cp(("KB", 0, 1), ("KI", 1, 2), (0, 8))
+    act(("KW", 0, 1), ("KB", 0, 1), F.Exp, (0, 8), scale=-LN2)
+    ops[-1]["n"] = 1600
 
     def const(out, v, key):
         act(out, ("ONE", 0, size(out)), F.Copy, key, scale=v)
+
+    def late(out, v, step):
+        n = size(out)
+        op("G", 0.17 + 2 * n * CY, [al("ZR")], [out], lambda g, T, x: g.affine_select(
+            ap(T, out), T.ZR[:, 0:n], [[-step, n]], A.not_equal, v, 0, step), (0, 8))
     const(("ZK", 0, 128), 0.0, K0)
     const(("ZK", 128, 144), 0.0, K0)
     b0 = al("BOF")[1]
     act(("ZK", 15, 143, 16), ("SEL", b0, b0 + 128, 16), F.Copy, K0)
     for n in SCALED:
-        act(al(n), al("I32"), F.Copy, K0, scale=SCALED[n])
+        if n in ("IB", "IU"):
+            act(al(n), al("I32"), F.Copy, K0, scale=SCALED[n])
+        else:
+            late(al(n), SCALED[n], 1)
     for n in BLOCK:
         act(al(n), al("BOF"), F.Copy, K0, scale=BLOCK[n])
     for n, v in (("NIF", -1.0), ("I14", 64 * U), ("I52", 2.0 ** 52)):
@@ -238,15 +253,15 @@ def build():
     act(al("E8"), al("E8F"), F.Copy, K0)
     act(al("BOA"), al("BOF"), F.Copy, K0, scale=-1.0)
     op("G", 0.4, [al("BOA")], [al("E8A")], lambda g, T, x: g.affine_select(ap(T, al("E8A")), ap(T, al("BOA")), [[-1, 128]], A.not_equal, 1.0, 0, 1), (0, 8))
-    act(al("TB"), al("E8A"), F.Copy, (0, 8))
+    act(al("TB"), al("E8A"), F.Copy, (0, 8), scale=("KW", 0, 1))
     for n in CONST:
-        const(al(n), CONST[n], (0, 8))
+        late(al(n), CONST[n], 0)
     const(al("ON32"), -1.0 / 32, (0, 8))
     for j, v in enumerate((-11.5, -59.5, 4.5, -TAU[0])):
         const(("TH0", j, j + 1), v, (0, 8))
     for c in range(NCH):
-        const(("D0%d" % c, 0, 6 * NL, 6), -64.0, (0, 8))
-        const(("EE%d" % c, CL, 6 * NL, 6), 0.0, (0, 8))
+        late(("D0%d" % c, 0, 6 * NL, 6), -64.0, 0)
+        late(("EE%d" % c, CL, 6 * NL, 6), 0.0, 0)
 
     V(2 * L, [("SGI", 0, 2)], [al("UA")], lambda g, T, x: g.vector.tensor_copy(T.UA[:], T.SGI[:]), K0)
     V(2 * L, [("SGI", 0, 2)], [al("LA0")], lambda g, T, x: g.vector.tensor_copy(T.LA0[:], T.SGI[:]), K0)
@@ -254,11 +269,11 @@ def build():
     cp(al("LG0"), al("G0I"), K0)
     V(256, [("PT", 0, 16)], [al("PF")], lambda g, T, x: g.vector.tensor_copy(T.PF[:], T.PT[:]), K0)
     V(256, [al("PF")], [al("TR")], lambda g, T, x: g.vector.transpose(T.TR[:], T.PF[:]), K0)
+    cp(al("TI"), al("TR"), K0)
+    V(256, [al("TI")], [("TA", 0, 1)], lambda g, T, x: g.vector.tensor_scalar(T.TA[:, 0, :], T.TI[:], 4095, None, A.bitwise_and), K0)
+    V(256, [al("TI")], [("TA", 1, 2)], lambda g, T, x: g.vector.tensor_scalar(T.TA[:, 1, :], T.TI[:], 12, None, A.logical_shift_right), K0)
     for q3 in range(8):
-        V(32, [al("TR")], [("TI", q3, q3 + 1)], lambda g, T, x, q3=q3: g.vector.tensor_copy(T.TI[:, q3:256:8], T.TR[:, q3 * 32:q3 * 32 + 32]), K0)
-    ts(al("TA", 0, 256), al("TI"), 4095, None, A.bitwise_and, None, K0)
-    ts(al("TA", 256, 512), al("TI"), 12, None, A.logical_shift_right, None, K0)
-    cp(al("PL"), al("TA"), K0)
+        V(64, [("TA", 0, 2)], [("PL", q3, 512, 8)], lambda g, T, x, q3=q3: g.vector.tensor_copy(T.PL[:, q3:512:8], T.TA[:, :, q3 * 32:q3 * 32 + 32]), K0)
     for d, m in enumerate((4032, 63)):
         ts(("DGI", d * 512, d * 512 + 512, 2), al("PN"), m, None, A.bitwise_and, None, (0, 5))
         ts(("DGI", d * 512 + 1, d * 512 + 512, 2), al("PN"), 12, m, A.logical_shift_right, A.bitwise_and, (0, 5))
@@ -273,7 +288,7 @@ def build():
     load("Y", "Z1", [al("EC")], [al("ZI", L, VIS * L)], lambda g, T, x: g.sync.dma_start(T.ZI[:, L:VIS * L], T.z[:, L:VIS * L]), 3.0, (0, 9))
     for t in range(1, VIS):
         load("Y", "EV%d" % t, [al("EC")], [al("EVB", t * W, t * W + W)], lambda g, T, x, t=t: g.sync.dma_start(T.EVB[:, t * W:t * W + W], T.ev[:]), 8.0, (0, 9))
-        ts(al("ZO", t * L, t * L + L), al("ZI", t * L, t * L + L), float(t * W), None, A.add, None, (t - 1, 9))
+        ts(al("ZO", t * L - L, t * L), al("ZI", t * L, t * L + L), float(t * W), None, A.add, None, (t - 1, 9))
 
     def meets(t, c, out, first, step):
         e = "%d" % c
@@ -305,11 +320,11 @@ def build():
         uz, us, ug = ("UA", 2 * o, 2 * o + NL), ("UA", 2 * o + NL, 2 * o + 2 * NL), ("UG", o, o + NL)
         e8 = al("E8")
         if t:
-            op("R", MIX["remote"], [("XA%d" % t, 2 * o, 2 * o + 2 * NL)], [join(lS, zx)], None, k, done="aS%d_%d" % (t, c), frm=-1, bonus="early")
-            tt(zf, zx, ("ZO", t * L + o, t * L + o + NL), A.min, k)
+            op("R", MIX["remote"], [("aS%d_%d" % (t, c), 0, 1)], [join(lS, zx)], None, k, done="aS%d_%d" % (t, c), frm=-1, bonus="early")
+            tt(zf, zx, ("ZO", t * L - L + o, t * L - L + o + NL), A.min, k)
             cp(join(uz, us), join(zf, lS), k)
             act(zr("SR", c), zx, F.Sign, k, bias=-0.875 * H, acc=("RS%d" % t, c, c + 1), bonus="early")
-            op("R", MIX["remote"], [("XG%d" % t, o, o + NL)], [lG], None, k, done="aG%d_%d" % (t, c), frm=-1)
+            op("R", MIX["remote"], [("aG%d_%d" % (t, c), 0, 1)], [lG], None, k, done="aG%d_%d" % (t, c), frm=-1)
             cp(ug, lG, k, bonus="ge")
 
         def fp(g, T, x):
@@ -317,7 +332,7 @@ def build():
             return g.tensor.matmul(ap(T, m1), ap(T, al("IH")), ap(T, zr("SR", c)), False, True) if t else y
         op("T", pc(2 * NL), [e8, al("SG8B")] + ([al("IH"), zr("SR", c)] if t else []), [m1], fp, k, n=2 * NL)
         act(PO, m1, F.Relu, k, bias=-0.5 if t else 0.0)
-        gather("S", al(ex), al("EVB", 0, (t + 1) * W), uz, k, bonus=MIX["ex"], parts=MIX["parts"])
+        gather(MIX["split"].get((t, c, 0), "SS"), al(ex), al("EVB", 0, (t + 1) * W), uz, k, bonus=MIX["ex"])
         gather("V", al(cm), al("EVB", 0, W), us, k, in1=al(ex), bonus=0.0)
 
         def gates():
@@ -334,7 +349,7 @@ def build():
             if i:
                 if i < CL:
                     gather("V", al(cm), al("EC"), al(ix), k, in1=al(ex), bonus=float(i))
-                gather("S", al(dg), al("DT"), al(ix), k, bonus=float(i), parts=MIX["parts"])
+                gather(MIX["split"].get((t, c, i), "SS"), al(dg), al("DT"), al(ix), k, bonus=float(i))
             if i < CL:
                 fold((cb, 0, NL), cm, k)
                 act(fi, (cb, 0, NL), F.Identity, k, bias=16.0, scale=-1.0)
@@ -381,16 +396,17 @@ def build():
             return zr(n, c)
 
         def send(dst, src, sem):
-            op("G", 0.1, [src], [], lambda g, T, x: x["send"](ap(T, dst), ap(T, src), sem, to), k)
+            op("G", 0.3, [src], [(sem, 0, 1)], lambda g, T, x: x["send"](ap(T, dst), ap(T, src), sem, to), k, send=sem)
 
-        def home(dst, src, sem, q, out):
-            op("R", MIX["remote"], [src], [dst], None, k, done=sem, frm=2)
+        def store(dst, q, out):
             load(q, "o%s%d" % (out, c), [dst], [], lambda g, T, x: (g.sync if q == "Y" else g.scalar).dma_start(T["y" + out][:, o:o + NL], ap(T, dst)), 2.0, k)
+        if last:
+            xg = xz
         meets(t, c, "D0", CL, 6)
         V(6 * NL, [al("D0" + e), (xb, 0, 6 * NL)], [al(mmn)], lambda g, T, x: g.vector.tensor_tensor_scan(
             T[mmn][:], T["D0" + e][:], T[xb][:, 0:6 * NL], 0.0, A.add, A.max), k)
         ts(Z("MI"), M6, 1.0 / U, None, A.mult, None, k)
-        if MIX["fv"]:
+        if MIX["fv"][3 * t + c]:
             ts(Z("FI"), Z("MI"), 63, None, A.bitwise_and, None, k)
             cp(Z("FB"), Z("FI"), k)
             fs, fu = Z("FB"), 1.0
@@ -400,7 +416,7 @@ def build():
             fs, fu = m1, 1.0 / U
         if not last:
             act(Z("SC"), fs, F.Sign, k, bias=(th, 2, 3), scale=-fu)
-        act(Z("W2"), fs, F.Exp, k, bias=("KB", 0, 1), scale=17.0 * LN2 * fu)
+        act(Z("W2"), fs, F.Exp, k, bias=-172.0 * LN2, scale=17.0 * LN2 * fu)
         ts(Z("AI"), Z("MI"), 6, 4095, A.arith_shift_right, A.bitwise_and, k)
         tt(Z("T1"), (xb, 7 * NL, 8 * NL), Z("AI"), A.add, k)
         tt(xs, (xb, 6 * NL, 7 * NL), Z("T1"), A.min, k)
@@ -409,17 +425,19 @@ def build():
             mm([(xr, [("NHI", Z("Q2")), ("NHI", al("C45")), ("H32", PO), ("NBH", Z("SC"))], True)], k)
             tt(xz, xr, zf, A.max, k)
             send(join(nS, nz), join(xs, xz), "aS%d_%d" % (t + 1, c))
-        else:
-            send(nS, xs, "aS%d_%d" % (t + 1, c))
-            home(nS, xs, "aS%d_%d" % (t + 1, c), "Y", "s")
         mm([(m2, [("KK", Z("Q2")), ("KK", al("C37")), ("KK", PO), ("TB", Z("W2"))], True)], k)
         act(Z("SU"), m2, F.Sign, k, bias=(th, 3, 4))
         mm([(xu, [("HH", al("C1")), ("NHH", Z("SU"))], True), (xn, [("I32", lG), ("HH", al("C1")), ("HH", Z("SU"))], True)], k)
         tt(Z("T2"), xu, Z("AI"), A.add, k)
         tt(xg, xn, Z("T2"), A.min, k)
-        send(nG, xg, "aG%d_%d" % (t + 1, c))
-        if last:
-            home(nG, xg, "aG%d_%d" % (t + 1, c), "S", "g")
+        if not last:
+            send(nG, xg, "aG%d_%d" % (t + 1, c))
+        else:
+            sem = "aS%d_%d" % (t + 1, c)
+            send(join(nS, nz), join(xs, xg), sem)
+            op("R", MIX["remote"], [(sem, 0, 1)], [join(nS, nz)], None, k, done=sem, frm=2)
+            store(nS, "Y", "s")
+            store(nz, "S", "g")
 
     def thresh(t):
         k, b, rs, th = (t, 8), "th", "RS%d" % t, "TH%d" % t
@@ -448,7 +466,10 @@ def build():
 
 
 def columns(lo, hi, step=1):
-    return (1 << hi) - (1 << lo) if step == 1 else sum(1 << j for j in range(lo, hi, step))
+    if step == 1:
+        return (1 << hi) - (1 << lo)
+    n = len(range(lo, hi, step))
+    return ((1 << step * n) - 1) // ((1 << step) - 1) << lo
 
 
 def depend(ops, free=()):
@@ -456,6 +477,8 @@ def depend(ops, free=()):
     for n, o in enumerate(ops):
         o["hard"], o["soft"] = set(), set()
         o["bank"] = next((r[0] for r in o["R"] + o["W"] if r[0] in free), None)
+        if o["done"] == "d_EV0":
+            o["soft"] |= {m for m in range(n) if ops[m]["q"] == o["q"]}
         both = [(wr, [(r[0], columns(*r[1:])) for r in regs]) for wr, regs in ((0, o["R"]), (1, o["W"]))]
         for wr, regs in both:
             for b, cols in regs:
@@ -539,14 +562,18 @@ def schedule(ops):
 
 
 def prices(ops, costs):
-    gat, slow, hop, same, far = costs
+    gat, slow, hop, same, far, issue, first, table = costs
     cost = []
     for o in ops:
         q, n = o["q"], o["n"]
         if q in "VS" and not o["done"]:
             cost.append(0.055 + -n * CY * gat * slow if n < 0 else max(64, n) * CY * slow + MIX["call"])
+        elif o["send"]:
+            cost.append(issue + (first if o["send"] == "aS1_0" else 0.0))
+        elif o["done"] == "d_EV0":
+            cost.append(table)
         else:
-            cost.append(n * MIX["pe"] * 1e-3 * slow + 0.03 if q == "T" else far if q == "R" else o["cost"])
+            cost.append(n * MIX["pe"] * 1e-3 * slow + 0.03 if q == "T" else far if q == "R" else o["cost"] * (slow if q == "G" else 1.0))
     return cost, [0.0 if o["q"] == "R" else 0.1 if o["done"] else c for o, c in zip(ops, cost)]
 
 
@@ -721,7 +748,7 @@ def rank_program(g, core, T, topo):
             ins.then_inc(T.sem[o["done"]], 16)
             tok[i] = (o["done"], 16)
             sems[o["done"]] = 16
-        elif o["W"]:
+        elif o["W"] and not o["send"]:
             count[q] += 1
             ins.then_inc(T.sem["q" + q], 1)
             tok[i] = ("q" + q, count[q])

import math
from concourse.mybir import AluOpType, ActivationFunctionType

A = AluOpType
F = ActivationFunctionType
NR, W, L, VIS, CL = 8, 4096, 192, 3, 5
NCH = 3
NL = L // NCH
J = 16 * NL
LN2 = math.log(2.0)
H = 16384.0
U = 2.0 ** -20
MAGIC = 768.0
TAU = (1.5 * 2.0 ** -104, 1.5 * 2.0 ** -121)
LAST = 1.0 - 0.75 * CL
MIX = {'ecv': 4, 'ecdue': 0.78, 'gat': (4, 5, 5, 5, 4, 4, 5, 4, 4), 'g': 1.71, 'pe': 0.42, 'hop': 0.16, 'same': 0.04, 'remote': 3.2, 'slack': 0.02, 'visit': 35.6, 'due': (-0.7, 5.0, 8, 0.0, 8.0, 13.2, 0, 7.7, 16.7), 'step': (3.2, 4.18, 5.05), 'ex': -1.0, 'split': {(1, 2, 5): 'S', (2, 1, 5): 'SV', (2, 2, 5): 'SV', (0, 1, 0): 'S', (1, 0, 3): 'S', (2, 0, 5): 'S', (0, 2, 3): 'S', (2, 2, 0): 'S', (1, 1, 0): 'S', (2, 2, 4): 'S', (1, 2, 0): 'S', (0, 1, 1): 'S'}, 'bw': 0.1, 'late': -500.0, 'gcov': (4.5, 3.5, 4.0, 2.8, 3.0, 4.0, 4.0, 5.7, 4.0), 'top': 60.0, 'th': 26.9, 'idx': -2.7, 'ge': -8.3, 'slackV': 0.24, 'slackS': 0.1, 'g5': 1, 'fv': (1, 1, 1, 1, 1, 0, 1, 1, 1), 'early': 2.2, 's3': (4, 3, 3, 4, 4, 4, 4, 3, 4), 'call': 0.03, 'seed': 1, 'rounds': 2500, 'zs': 4096}

ZB = ["FB", "PO", "SR", "MS", "Q2", "SC", "W2", "SU"]
ZF = ["RR", "T1", "T2"]
ZI_ = ["MI", "AI", "FI"]
SCALED = {"IB": 1.0, "IH": 0.5, "IU": U, "N4": -4.0, "N64": -64.0, "N128": -128.0, "HI": H, "NHI": -H, "HH": H / 2, "NHH": -H / 2, "H32": 32 * H}
BLOCK = {"BO": 1.0, "NBH": -H / 2}
MATS = list(SCALED) + list(BLOCK) + ["KK", "TB", "E8"]
SEL = ["I32", "BOA", "BOF", "E8A", "E8F", "NIF", "I14", "I52"]
CONST = {"C1": 1.0, "C37": -37.0, "C45": -45.0, "CM": MAGIC}
CONST.update({"O%d" % i: -0.75 * i if i < CL else LAST - 4.0 for i in range(1, CL + 1)})

SCRATCH = {
    "EVB": ("sbuf", [128, VIS * W], "bfloat16"), "EC": ("sbuf", [128, 2 * W], "bfloat16"), "DT": ("sbuf", [128, 2 * W], "bfloat16"),
    "PN": ("sbuf", [128, 256], "int32"), "PT": ("sbuf", [128, 16, 16], "int32"), "PF": ("sbuf", [128, 256], "float32"),
    "TR": ("sbuf", [128, 256], "float32"), "TI": ("sbuf", [128, 256], "int32"), "TA": ("sbuf", [128, 2, 256], "int32"),
    "ZR": ("sbuf", [128, 128], "bfloat16"),
    "PL": ("sbuf", [128, 512], "uint16"),
    "DGI": ("sbuf", [128, 1024], "int32"), "DGB": ("sbuf", [128, 1024], "bfloat16"),
    "SGI": ("sbuf", [128, NCH, 2, NL], "int32"), "G0I": ("sbuf", [128, L], "int32"),
    "ZI": ("sbuf", [128, VIS * L], "int32"), "ZO": ("psum", [128, 512], "float32"),
    "SG8": ("sbuf", [128, VIS * L], "int32"), "SG8B": ("sbuf", [128, VIS * L], "bfloat16"),
    "ONE": ("sbuf", [128, 128], "float32"), "ON32": ("sbuf", [128, 128], "float32"),
    "SEL": ("sbuf", [128, 128 * len(SEL)], "float32"), "SCN": ("sbuf", [128, 128 * len(MATS)], "bfloat16"),
    "ZK": ("sbuf", [128, 144], "bfloat16"), "CT": ("sbuf", [128, NL * len(CONST)], "bfloat16"),
    "KI": ("sbuf", [128, 2], "int32"), "KB": ("sbuf", [128, 2], "float32"), "KW": ("sbuf", [128, 2], "float32"), "THI": ("sbuf", [128, 2], "int32"), "NP": ("sbuf", [128, 2], "float32"),
    "UA": ("sbuf", [128, 2 * L], "uint16"), "UG": ("sbuf", [128, L], "uint16"),
    "PB": ("psum", [128, 512], "float32"),
}
for _t in range(VIS + 1):
    SCRATCH["LA%d" % _t] = ("sbuf", [128, (3 if _t else 2) * L], "float32")
    SCRATCH["LG%d" % _t] = ("sbuf", [128, L], "float32")
    if _t:
        SCRATCH["XA%d" % _t] = ("sbuf", [128, 2 * L], "float32")
        SCRATCH["XG%d" % _t] = ("sbuf", [128, L], "float32")
    if _t < VIS:
        SCRATCH["TH%d" % _t] = ("sbuf", [128, 4], "float32")
    if 0 < _t < VIS:
        SCRATCH["RS%d" % _t] = ("sbuf", [128, 4], "float32")
SEMAPHORES = ["qV", "qS", "qT", "qG", "lsend"]
for _c in range(NCH):
    for _n, _k, _d in (("IDX", NL, "uint16"), ("EX", J, "bfloat16"), ("CG", J, "bfloat16"), ("CM", J, "bfloat16"), ("DG", J, "bfloat16"),
                       ("FF", 6 * NL, "bfloat16"), ("EE", 6 * NL, "bfloat16"), ("D0", 6 * NL, "bfloat16"), ("MM", 6 * NL, "float32"), ("GE", 6 * NL, "float32"),
                       ("SB", NL * len(ZB), "bfloat16"), ("SF", NL * len(ZF), "float32"), ("SI", NL * len(ZI_), "int32")):
        SCRATCH["%s%d" % (_n, _c)] = ("sbuf", [128, _k], _d)
    for _n in ("XB", "CB"):
        SCRATCH["%s%d" % (_n, _c)] = ("psum", [128, 512], "float32")
    for _t in range(1, VIS + 1):
        SEMAPHORES += ["aS%d_%d" % (_t, _c)] + ["aG%d_%d" % (_t, _c)] * (_t < VIS)
DMAS = ["PTa", "PTb", "PN", "EV0", "EV1", "EV2", "Z0", "Z1", "S0", "G0", "SG", "D0", "D1"] + ["o%s%d" % (x, c) for x in "sg" for c in range(NCH)]
SEMAPHORES += ["d_" + n for n in DMAS]
PSUM = {n for n in SCRATCH if SCRATCH[n][0] == "psum"}
FREE = {n for n in PSUM if n[:2] != "XB"}
CY = 0.00083
COSTS = [(1.5, 1.05, 0.2, 0.1, 2.8, 0.3, 2.0, 7.5), (1.1, 1.1, 0.1, 0.05, 2.5, 0.2, 1.0, 6.5), (1.56, 1.0, 0.1, 0.1, 2.0, 0.5, 1.5, 7.0),
         (1.9, 1.3, 0.15, 0.1, 3.5, 0.3, 3.0, 8.5), (1.3, 1.3, 0.3, 0.2, 3.5, 0.6, 2.0, 8.0)]


def vc(n):
    return max(64, n) * CY + 0.03


def sc(n):
    return max(64, n) * CY + 0.04


def ga(n):
    return 0.055 + n * CY * MIX["g"]


def pc(cycles):
    return cycles * MIX["pe"] * 1e-3 + 0.03


def named(n):
    for b, l, k in (("SCN", MATS, 128), ("SEL", SEL, 128), ("CT", list(CONST), NL)):
        if n in l:
            return (b, l.index(n) * k, l.index(n) * k + k)
    return None


def al(n, lo=0, hi=None):
    if lo == 0 and hi is None and named(n) and n not in SCRATCH:
        return named(n)
    return (n, lo, math.prod(SCRATCH[n][1][1:]) if hi is None else hi)


def zr(n, c):
    for b, l in (("SB", ZB), ("SF", ZF), ("SI", ZI_)):
        if n in l:
            return ("%s%d" % (b, c), l.index(n) * NL, l.index(n) * NL + NL)


def ap(T, r):
    return T[r[0]][:, r[1]:r[2]] if len(r) == 3 else T[r[0]][:, r[1]:r[2]:r[3]]


def build():
    ops = []

    def op(q, cost, R, Wr, f, key, done=None, frm=None, bonus="", n=0, send=None):
        ops.append({"q": q, "cost": cost, "R": R, "W": Wr, "f": f, "key": key, "done": done, "frm": frm, "bonus": bonus, "n": n, "send": send})

    def V(n, R, Wr, f, key, bonus=""):
        op("V", vc(n), R, Wr, f, key, bonus=bonus, n=n)

    def S(n, R, Wr, f, key, bonus=""):
        op("S", sc(n), R, Wr, f, key, bonus=bonus, n=n)

    def load(q, sem, R, Wr, f, cost, key=(-1, 0)):
        op(q, cost, R, Wr, f, key, done="d_" + sem)

    def size(r):
        return len(range(*r[1:]))

    def tt(out, a, b, alu, key, bonus=""):
        n = size(out) * (1 if a[0] in PSUM or b[0] in PSUM else 2)
        V(n, [a, b], [out], lambda g, T, x: g.vector.tensor_tensor(ap(T, out), ap(T, a), ap(T, b), alu), key, bonus)

    def ts(out, a, s1, s2, o0, o1, key, bonus=""):
        R = [a] + [s for s in (s1, s2) if isinstance(s, tuple)]

        def f(g, T, x):
            v1, v2 = [ap(T, s) if isinstance(s, tuple) else s for s in (s1, s2)]
            if o1 is None:
                return g.vector.tensor_scalar(ap(T, out), ap(T, a), v1, None, o0)
            return g.vector.tensor_scalar(ap(T, out), ap(T, a), v1, v2, o0, o1)
        V(size(out), R, [out], f, key, bonus)

    def cp(out, a, key, bonus=""):
        V(size(out), [a], [out], lambda g, T, x: g.vector.tensor_copy(ap(T, out), ap(T, a)), key, bonus)

    def fill(out, v, key, bonus=""):
        V(size(out) // 2, [], [out], lambda g, T, x: g.vector.memset(ap(T, out), v), key, bonus)

    def act(out, a, fn, key, bias=0.0, scale=1.0, acc=None, bonus=""):
        R = [a] + [s for s in (bias, scale) if isinstance(s, tuple)]

        def f(g, T, x):
            b, m = [ap(T, s) if isinstance(s, tuple) else s for s in (bias, scale)]
            if acc:
                return g.scalar.activation(ap(T, out), ap(T, a), fn, bias=b, scale=m, accum_out=ap(T, acc))
            return g.scalar.activation(ap(T, out), ap(T, a), fn, bias=b, scale=m)
        S(size(out), R, [out] + ([acc] if acc else []), f, key, bonus)

    def mm(groups, key, bonus="", close=True):
        R, Wr, cyc = [], [], 0
        for out, terms, first in groups:
            Wr.append(out)
            for t in terms:
                R += [al(t[0]), t[1]]
                cyc += max(64, size(t[1])) * (4 if t[0] in SEL else 1)

        def f(g, T, x):
            for out, terms, first in groups:
                for n, t in enumerate(terms):
                    y = g.tensor.matmul(ap(T, t[2] if len(t) > 2 else out), ap(T, al(t[0])), ap(T, t[1]), first and n == 0, close and n == len(terms) - 1)
            return y
        op("T", pc(cyc), R, Wr, f, key, bonus=bonus, n=cyc)

    def gather(q, out, win, off, key, in1=None, bonus=""):
        if len(q) > 1:
            n = (off[2] - off[1]) // len(q)
            for j in range(len(q)):
                gather(q[j], (out[0], out[1] + 16 * n * j, out[1] + 16 * n * (j + 1)), win, (off[0], off[1] + n * j, off[1] + n * (j + 1)), key, None, bonus)
            return

        def f(g, T, x):
            src = ap(T, win).indirect(ap(T, off))
            if in1:
                return g.vector.tensor_tensor(ap(T, out), src, ap(T, in1), A.is_ge)
            if q == "V":
                return g.vector.tensor_copy(ap(T, out), src)
            return g.scalar.activation(ap(T, out), src, F.Copy)
        op(q, ga(size(out)), [win, off] + ([in1] if in1 else []), [out], f, key, bonus=bonus, n=-size(out))

    def fold(out, src, key, close=True):
        def f(g, T, x):
            for r in range(16):
                y = g.tensor.matmul(ap(T, out), T.ZK[:, 15 - r:143 - r], T[src][:, r:J:16], r == 0, close and r == 15)
            return y
        op("T", pc(J), [al("ZK"), al(src)], [out], f, key, n=J)

    K0 = (-1, 0)
    for y in range(2):
        load("Y", "PT" + "ab"[y], [], [("PT", y, y + 1)], lambda g, T, x, y=y: g.sync.dma_start(T.PT[:, y:16:2, :], T.par[y:8:2, :]), 3.0)
    load("S", "Z0", [], [("SGI", 0, 1)], lambda g, T, x: g.scalar.dma_start(T.SGI[:, :, 0, :], T.z[:, 0:L]), 2.4)
    load("S", "S0", [], [("SGI", 1, 2)], lambda g, T, x: g.scalar.dma_start(T.SGI[:, :, 1, :], T.s0[:]), 2.4)
    load("S", "G0", [], [al("G0I")], lambda g, T, x: g.scalar.dma_start(T.G0I[:], T.g0[:]), 2.6)
    load("Y", "PN", [], [al("PN")], lambda g, T, x: g.sync.dma_start(T.PN[:], T.par[:]), 3.2)
    load("Y", "EV0", [], [al("EVB", 0, W)], lambda g, T, x: g.sync.dma_start(T.EVB[:, 0:W], T.ev[:]), 8.0)
    load("S", "SG", [], [al("SG8")], lambda g, T, x: g.scalar.dma_start(T.SG8[0:8, :], T.sg[:]), 3.0)

    V(128, [], [al("ONE")], lambda g, T, x: g.vector.memset(T.ONE[:], 1.0), K0, bonus="top")

    def asel(o, i, pat, cmp, base, ch):
        op("G", 0.4, [al(i)], [al(o)], lambda g, T, x: g.affine_select(ap(T, al(o)), ap(T, al(i)), pat, cmp, 0.0, base, ch), K0, bonus="top")
    asel("BOA", "ONE", [[-16, 8], [0, 16]], A.is_ge, 0, 1)
    asel("BOF", "BOA", [[16, 8], [0, 16]], A.is_ge, 15, -1)
    asel("I32", "ONE", [[-1, 128]], A.is_equal, 0, 1)
    asel("E8A", "ONE", [[1, 128]], A.is_ge, 0, -16)
    asel("E8F", "E8A", [[-1, 128]], A.is_ge, 15, 16)
    op("G", 0.15, [], [("KI", 0, 1)], lambda g, T, x: g.iota(T.KI[:, 0:1], [[0, 1]], 0, 1), K0)
    op("G", 3.6, [al("E8F"), al("BOF"), al("I32"), ("KI", 0, 1)], [al("DT", 0, W // 2)], lambda g, T, x: g.iota(
        T.DT[:, 0:W // 2], [[0, W // 2]], 0, 0, allow_small_or_imprecise_dtypes=True), K0, bonus="top")
    z0, z1 = W // 2, W // 2 + MIX["zs"]
    fill(al("ZR"), 0.0, K0, bonus="top")
    fill(al("DT", z0, z1), 0.0, K0, bonus="top")
    for a in range(z1, 2 * W, z1 - z0):
        n = min(z1 - z0, 2 * W - a)
        act(al("DT", a, a + n), al("DT", z0, z0 + n), F.Copy, K0, bonus="top")
    ts(("KI", 1, 2), ("KI", 0, 1), 15, None, A.bitwise_and, None, (0, 8))
    cp(("KB", 0, 1), ("KI", 1, 2), (0, 8))
    act(("KW", 0, 1), ("KB", 0, 1), F.Exp, (0, 8), scale=-LN2)
    ops[-1]["n"] = 1600

    def const(out, v, key):
        act(out, ("ONE", 0, size(out)), F.Copy, key, scale=v)

    def late(out, v, step):
        n = size(out)
        op("G", 0.17 + 2 * n * CY, [al("ZR")], [out], lambda g, T, x: g.affine_select(
            ap(T, out), T.ZR[:, 0:n], [[-step, n]], A.not_equal, v, 0, step), (0, 8))
    const(("ZK", 0, 128), 0.0, K0)
    const(("ZK", 128, 144), 0.0, K0)
    b0 = al("BOF")[1]
    act(("ZK", 15, 143, 16), ("SEL", b0, b0 + 128, 16), F.Copy, K0)
    for n in SCALED:
        if n in ("IB", "IU"):
            act(al(n), al("I32"), F.Copy, K0, scale=SCALED[n])
        else:
            late(al(n), SCALED[n], 1)
    for n in BLOCK:
        act(al(n), al("BOF"), F.Copy, K0, scale=BLOCK[n])
    for n, v in (("NIF", -1.0), ("I14", 64 * U), ("I52", 2.0 ** 52)):
        act(al(n), al("I32"), F.Copy, K0, scale=v)
    act(al("KK"), al("I52"), F.Copy, K0, scale=2.0 ** 52)
    act(al("E8"), al("E8F"), F.Copy, K0)
    act(al("BOA"), al("BOF"), F.Copy, K0, scale=-1.0)
    op("G", 0.4, [al("BOA")], [al("E8A")], lambda g, T, x: g.affine_select(ap(T, al("E8A")), ap(T, al("BOA")), [[-1, 128]], A.not_equal, 1.0, 0, 1), (0, 8))
    act(al("TB"), al("E8A"), F.Copy, (0, 8), scale=("KW", 0, 1))
    for n in CONST:
        late(al(n), CONST[n], 0)
    const(al("ON32"), -1.0 / 32, (0, 8))
    for j, v in enumerate((-11.5, -59.5, 4.5, -TAU[0])):
        const(("TH0", j, j + 1), v, (0, 8))
    for c in range(NCH):
        late(("D0%d" % c, 0, 6 * NL, 6), -64.0, 0)
        late(("EE%d" % c, CL, 6 * NL, 6), 0.0, 0)

    V(2 * L, [("SGI", 0, 2)], [al("UA")], lambda g, T, x: g.vector.tensor_copy(T.UA[:], T.SGI[:]), K0)
    V(2 * L, [("SGI", 0, 2)], [al("LA0")], lambda g, T, x: g.vector.tensor_copy(T.LA0[:], T.SGI[:]), K0)
    cp(al("UG"), al("G0I"), K0)
    cp(al("LG0"), al("G0I"), K0)
    V(256, [("PT", 0, 16)], [al("PF")], lambda g, T, x: g.vector.tensor_copy(T.PF[:], T.PT[:]), K0)
    V(256, [al("PF")], [al("TR")], lambda g, T, x: g.vector.transpose(T.TR[:], T.PF[:]), K0)
    cp(al("TI"), al("TR"), K0)
    V(256, [al("TI")], [("TA", 0, 1)], lambda g, T, x: g.vector.tensor_scalar(T.TA[:, 0, :], T.TI[:], 4095, None, A.bitwise_and), K0)
    V(256, [al("TI")], [("TA", 1, 2)], lambda g, T, x: g.vector.tensor_scalar(T.TA[:, 1, :], T.TI[:], 12, None, A.logical_shift_right), K0)
    for q3 in range(8):
        V(64, [("TA", 0, 2)], [("PL", q3, 512, 8)], lambda g, T, x, q3=q3: g.vector.tensor_copy(T.PL[:, q3:512:8], T.TA[:, :, q3 * 32:q3 * 32 + 32]), K0)
    for d, m in enumerate((4032, 63)):
        ts(("DGI", d * 512, d * 512 + 512, 2), al("PN"), m, None, A.bitwise_and, None, (0, 5))
        ts(("DGI", d * 512 + 1, d * 512 + 512, 2), al("PN"), 12, m, A.logical_shift_right, A.bitwise_and, (0, 5))
        ts(al("DGB", d * 512, d * 512 + 512), al("DGI", d * 512, d * 512 + 512), 64 * U, None, A.mult, None, (0, 5))
        load("Y", "D%d" % d, [al("DGB", d * 512, d * 512 + 512)], [("DT", d, 2 * W, 2)], lambda g, T, x, d=d: g.sync.dma_start(
            T.DT[d:128:16, :], T.DGB[:, d * 512:d * 512 + 512]), 2.5, (0, 5))
    V(576, [al("SG8")], [al("SG8B")], lambda g, T, x: g.vector.tensor_copy(T.SG8B[0:8, :], T.SG8[0:8, :]), (0, 6))
    for b in range(8):
        hf, s = b // 2, b % 2
        gather("V" if b < MIX["ecv"] else "S", ("EC", hf * 2048 + s, hf * 2048 + 2048, 2), al("EVB", 0, W), al("PL", s * 256 + hf * 64, s * 256 + hf * 64 + 64), (0, 4),
               bonus=MIX["ecdue"])
    load("Y", "Z1", [al("EC")], [al("ZI", L, VIS * L)], lambda g, T, x: g.sync.dma_start(T.ZI[:, L:VIS * L], T.z[:, L:VIS * L]), 3.0, (0, 9))
    for t in range(1, VIS):
        load("Y", "EV%d" % t, [al("EC")], [al("EVB", t * W, t * W + W)], lambda g, T, x, t=t: g.sync.dma_start(T.EVB[:, t * W:t * W + W], T.ev[:]), 8.0, (0, 9))
        ts(al("ZO", t * L - L, t * L), al("ZI", t * L, t * L + L), float(t * W), None, A.add, None, (t - 1, 9))

    def meets(t, c, out, first, step):
        e = "%d" % c
        tt((out + e, first, 6 * NL, step), ("XB" + e, first, 6 * NL, step), ("GE" + e, first, 6 * NL, step), A.is_equal, (t, c))

    def stays(t, c, first, step):
        e, n = "%d" % c, 6 // step
        v0 = NL * (1, 3, 5)[first - 1]
        vv = ("CB" + e, v0, v0 + n * NL)
        mm([(vv, [("IB", ("FF" + e, first, 6 * NL, step))] + [("N64", zr("PO", c), (vv[0], v0 + j, vv[2], n)) for j in range(n)]
             + [("N128", ("EE" + e, first, 6 * NL, step))], True)], (t, c))
        act(("D0" + e, first, 6 * NL, step), vv, F.Sign, (t, c), bias=("TH%d" % t, 1, 2), scale=-1.0)

    def lanes(t, c):
        o = c * NL * (3 if t else 2)
        return [("LA%d" % t, o + j * NL, o + j * NL + NL) for j in range(3)] + [("LG%d" % t, c * NL, c * NL + NL)]

    def join(a, b):
        return (a[0], a[1], b[2])

    def walk(t, c):
        k = (t, c)
        o, e = c * NL, "%d" % c
        ex, cm, dg, ix, xb, cb, ff = "EX" + e, "CM" + e, "DG" + e, "IDX" + e, "XB" + e, "CB" + e, "FF" + e
        zf, lS, zx, lG = lanes(t, c)
        th = "TH%d" % t
        m1, m2 = (cb, 6 * NL, 7 * NL), (cb, 7 * NL, 8 * NL)
        PO, g5 = zr("PO", c), ("GE" + e, CL, 6 * NL, 6)
        uz, us, ug = ("UA", 2 * o, 2 * o + NL), ("UA", 2 * o + NL, 2 * o + 2 * NL), ("UG", o, o + NL)
        e8 = al("E8")
        if t:
            op("R", MIX["remote"], [("aS%d_%d" % (t, c), 0, 1)], [join(lS, zx)], None, k, done="aS%d_%d" % (t, c), frm=-1, bonus="early")
            tt(zf, zx, ("ZO", t * L - L + o, t * L - L + o + NL), A.min, k)
            cp(join(uz, us), join(zf, lS), k)
            act(zr("SR", c), zx, F.Sign, k, bias=-0.875 * H, acc=("RS%d" % t, c, c + 1), bonus="early")
            op("R", MIX["remote"], [("aG%d_%d" % (t, c), 0, 1)], [lG], None, k, done="aG%d_%d" % (t, c), frm=-1)
            cp(ug, lG, k, bonus="ge")

        def fp(g, T, x):
            y = g.tensor.matmul(ap(T, m1), T.SCN[0:8, e8[1]:e8[2]], T.SG8B[0:8, t * L + o:t * L + o + NL], True, not t)
            return g.tensor.matmul(ap(T, m1), ap(T, al("IH")), ap(T, zr("SR", c)), False, True) if t else y
        op("T", pc(2 * NL), [e8, al("SG8B")] + ([al("IH"), zr("SR", c)] if t else []), [m1], fp, k, n=2 * NL)
        act(PO, m1, F.Relu, k, bias=-0.5 if t else 0.0)
        gather(MIX["split"].get((t, c, 0), "SS"), al(ex), al("EVB", 0, (t + 1) * W), uz, k, bonus=MIX["ex"])
        gather("V", al(cm), al("EVB", 0, W), us, k, in1=al(ex), bonus=0.0)

        def gates():
            gather("V", al("CG" + e), al("EVB", 0, W), ug, k, in1=al(ex), bonus=MIX["gcov"][3 * t + c])
            fold(m1, "CG" + e, k)
            act(zr("MS", c), m1, F.Sign, k, bias=(th, 0, 1))
            mm([(m1, [("BO", zr("MS", c)), ("N64", PO)], True)], k)
            act(zr("Q2", c), m1, F.Abs, k, bias=21.0)

        for i in range(CL + 1):
            xi, fi = (xb, i, 6 * NL, 6), (ff, i + 1, 6 * NL, 6)
            if i == MIX["gat"][3 * t + c]:
                gates()
            if i:
                if i < CL:
                    gather("V", al(cm), al("EC"), al(ix), k, in1=al(ex), bonus=float(i))
                gather(MIX["split"].get((t, c, i), "SS"), al(dg), al("DT"), al(ix), k, bonus=float(i))
            if i < CL:
                fold((cb, 0, NL), cm, k)
                act(fi, (cb, 0, NL), F.Identity, k, bias=16.0, scale=-1.0)
            if i:
                fold(xi, dg, k, close=False)
                mm([(xi, [("IB", al("O%d" % i)), ("IU", fi) if i < CL else ("N4", ("D0" + e, CL, 6 * NL, 6))], False)], k)
            else:
                mm([(xi, [("I14", lS), ("IU", fi)], True)], k)
            if i < CL:
                ts(al(ix), xi, 2.0 ** 15, 7.5 / 32 + 0.75 * i * 2.0 ** 15, A.mult, A.add, k, bonus="idx")
            if i == CL - 1:
                stays(t, c, 2, 3)
            if i == 0:
                mm([((xb, 6 * NL, 7 * NL), [("I32", lS), ("HI", PO)], True), ((xb, 7 * NL, 8 * NL), [("HI", al("C1")), ("NHI", PO)], True)], k, bonus="ge")
            if i == MIX["g5"]:
                mm([(m2, [("I14", lG), ("IB", PO)], True)], k, bonus="ge")
                act(g5, m2, F.Identity, k, bias=LAST, bonus="ge")
            if i >= MIX["g5"]:
                for j in range(1 if i == MIX["g5"] else i, min(i + 1, CL)):
                    mm([(m2, [("I32", g5), ("IU", (ff, j + 1, 6 * NL, 6))], True)], k, bonus="ge")
                    act(("GE" + e, j, 6 * NL, 6), m2, F.Identity, k, bias=-0.75 * j - LAST, bonus="ge")
            if i in (2, 3):
                meets(t, c, "EE", i, 6)
            if i == CL - 1:
                meets(t, c, "EE", 1, 3)
            if i == MIX["s3"][3 * t + c]:
                stays(t, c, 3, 6)
            if i == CL - 1:
                stays(t, c, 1, 3)

    def epilogue(t, c):
        k = (t, c)
        o, e = c * NL, "%d" % c
        xb, cb, mmn, th = "XB" + e, "CB" + e, "MM" + e, "TH%d" % t
        zf, lS, zx, lG = lanes(t, c)
        m1, m2 = (cb, 6 * NL, 7 * NL), (cb, 7 * NL, 8 * NL)
        PO, M6 = zr("PO", c), (mmn, 5, 6 * NL, 6)
        last = t + 1 == VIS
        to = "home" if last else "next"
        xs, xz, xg = ("XA%d" % (t + 1), 2 * o, 2 * o + NL), ("XA%d" % (t + 1), 2 * o + NL, 2 * o + 2 * NL), ("XG%d" % (t + 1), o, o + NL)
        _, nS, nz, nG = lanes(t + 1, c)

        def Z(n):
            return zr(n, c)

        def send(dst, src, sem):
            op("G", 0.3, [src], [(sem, 0, 1)], lambda g, T, x: x["send"](ap(T, dst), ap(T, src), sem, to), k, send=sem)

        def store(dst, q, out):
            load(q, "o%s%d" % (out, c), [dst], [], lambda g, T, x: (g.sync if q == "Y" else g.scalar).dma_start(T["y" + out][:, o:o + NL], ap(T, dst)), 2.0, k)
        if last:
            xg = xz
        meets(t, c, "D0", CL, 6)
        V(6 * NL, [al("D0" + e), (xb, 0, 6 * NL)], [al(mmn)], lambda g, T, x: g.vector.tensor_tensor_scan(
            T[mmn][:], T["D0" + e][:], T[xb][:, 0:6 * NL], 0.0, A.add, A.max), k)
        ts(Z("MI"), M6, 1.0 / U, None, A.mult, None, k)
        if MIX["fv"][3 * t + c]:
            ts(Z("FI"), Z("MI"), 63, None, A.bitwise_and, None, k)
            cp(Z("FB"), Z("FI"), k)
            fs, fu = Z("FB"), 1.0
        else:
            act(Z("RR"), M6, F.Identity, k, bias=MAGIC)
            mm([(m1, [("NIF", Z("RR")), ("IB", al("CM")), ("I32", M6)], True)], k)
            fs, fu = m1, 1.0 / U
        if not last:
            act(Z("SC"), fs, F.Sign, k, bias=(th, 2, 3), scale=-fu)
        act(Z("W2"), fs, F.Exp, k, bias=-172.0 * LN2, scale=17.0 * LN2 * fu)
        ts(Z("AI"), Z("MI"), 6, 4095, A.arith_shift_right, A.bitwise_and, k)
        tt(Z("T1"), (xb, 7 * NL, 8 * NL), Z("AI"), A.add, k)
        tt(xs, (xb, 6 * NL, 7 * NL), Z("T1"), A.min, k)
        xr, xu, xn = (xb, 0, NL), (xb, NL, 2 * NL), (xb, 2 * NL, 3 * NL)
        if not last:
            mm([(xr, [("NHI", Z("Q2")), ("NHI", al("C45")), ("H32", PO), ("NBH", Z("SC"))], True)], k)
            tt(xz, xr, zf, A.max, k)
            send(join(nS, nz), join(xs, xz), "aS%d_%d" % (t + 1, c))
        mm([(m2, [("KK", Z("Q2")), ("KK", al("C37")), ("KK", PO), ("TB", Z("W2"))], True)], k)
        act(Z("SU"), m2, F.Sign, k, bias=(th, 3, 4))
        mm([(xu, [("HH", al("C1")), ("NHH", Z("SU"))], True), (xn, [("I32", lG), ("HH", al("C1")), ("HH", Z("SU"))], True)], k)
        tt(Z("T2"), xu, Z("AI"), A.add, k)
        tt(xg, xn, Z("T2"), A.min, k)
        if not last:
            send(nG, xg, "aG%d_%d" % (t + 1, c))
        else:
            sem = "aS%d_%d" % (t + 1, c)
            send(join(nS, nz), join(xs, xg), sem)
            op("R", MIX["remote"], [(sem, 0, 1)], [join(nS, nz)], None, k, done=sem, frm=2)
            store(nS, "Y", "s")
            store(nz, "S", "g")

    def thresh(t):
        k, b, rs, th = (t, 8), "th", "RS%d" % t, "TH%d" % t

        def f(g, T, x):
            for c in range(NCH):
                y = g.tensor.matmul(T.PB[:, 0:1], T.ON32[:], T[rs][:, c:c + 1], c == 0, c == NCH - 1)
            return y
        op("T", 0.35, [al("ON32"), al(rs)], [("PB", 0, 1)], f, k, bonus=b, n=768)
        ts(("THI", 0, 1), ("PB", 0, 1), 0.5, -0.25, A.mult, A.add, k, b)
        ts(("NP", 0, 1), ("THI", 0, 1), 2.0, ("PB", 0, 1), A.mult, A.subtract, k, b)
        act((th, 0, 3), ("TH0", 0, 3), F.Identity, k, bias=("NP", 0, 1), bonus=b)
        act((th, 3, 4), ("NP", 0, 1), F.Identity, k, bias=-TAU[0], scale=TAU[1] - TAU[0], bonus=b)

    for t in range(VIS):
        n0 = len(ops)
        for c in range(NCH):
            walk(t, c)
        if t:
            n1 = len(ops)
            thresh(t)
            ops[n0:] = [o for o in ops[n0:n1] if o["bonus"] == "early"] + ops[n1:] + [o for o in ops[n0:n1] if o["bonus"] != "early"]
        for c in range(NCH):
            epilogue(t, c)
    return ops


def columns(lo, hi, step=1):
    if step == 1:
        return (1 << hi) - (1 << lo)
    n = len(range(lo, hi, step))
    return ((1 << step * n) - 1) // ((1 << step) - 1) << lo


def depend(ops, free=()):
    acc, bank = {}, {}
    for n, o in enumerate(ops):
        o["hard"], o["soft"] = set(), set()
        o["bank"] = next((r[0] for r in o["R"] + o["W"] if r[0] in free), None)
        if o["done"] == "d_EV0":
            o["soft"] |= {m for m in range(n) if ops[m]["q"] == o["q"]}
        both = [(wr, [(r[0], columns(*r[1:])) for r in regs]) for wr, regs in ((0, o["R"]), (1, o["W"]))]
        for wr, regs in both:
            for b, cols in regs:
                for (m, w2, c2) in acc.get(b, ()):
                    if m != n and (wr or w2) and cols & c2:
                        if wr and not w2 and ops[m]["q"] == o["q"] and not ops[m]["done"]:
                            o["soft"].add(m)
                        elif o["q"] == "T" and ops[m]["q"] == "T" and b in PSUM:
                            o["soft"].add(m)
                        else:
                            o["hard"].add(m)
                if b in PSUM and b not in free:
                    for q, m in bank.get(b, {}).items():
                        if m != n:
                            (o["soft"] if q == o["q"] else o["hard"]).add(m)
        for wr, regs in both:
            for b, cols in regs:
                if wr:
                    acc[b] = [a for a in acc.get(b, []) if a[2] & ~cols or a[0] == n] + [(n, 1, cols)]
                else:
                    acc.setdefault(b, []).append((n, 0, cols))
                if b in PSUM:
                    bank.setdefault(b, {})[o["q"]] = n
    return ops


def schedule(ops):
    n = len(ops)
    succ = [[] for _ in range(n)]
    for i, o in enumerate(ops):
        for m in o["hard"] | o["soft"]:
            succ[m].append(i)
    bot = [0.0] * n
    hop, same = MIX["hop"], MIX["same"]
    for i in range(n - 1, -1, -1):
        bot[i] = ops[i]["cost"] + max([bot[s] + hop for s in succ[i]], default=0.0)
    pri = []
    for i in range(n):
        b, (t, c) = ops[i]["bonus"], ops[i]["key"]
        if isinstance(b, float):
            p = -(MIX["visit"] * t + (MIX["due"][3 * t + c] if c < NCH else 0.0) + MIX["step"][t] * b)
        elif c < NCH and t >= 0:
            p = 1000.0 + bot[i] * MIX["bw"] - MIX["due"][3 * t + c] + MIX.get(b, 0.0)
        else:
            p = MIX["late"] + bot[i] + MIX.get(b, 0.0) if t >= 0 and c > 7 and not b else 1000.0 + bot[i] + MIX.get(b, 0.0)
        pri.append(p)
    need = [len(o["hard"] | o["soft"]) for o in ops]
    ready = [0.0] * n
    cand = {}
    for i in range(n):
        if not need[i]:
            cand.setdefault(ops[i]["q"], []).append(i)
    free, order, end = {}, [], [0.0] * n
    start = [0.0] * n
    while True:
        best = None
        for q, l in cand.items():
            if not l:
                continue
            f = free.get(q, 0.0) if q != "R" else 0.0
            lo = min(max(f, ready[i]) for i in l)
            i = max((j for j in l if max(f, ready[j]) <= lo + MIX.get("slack" + q, MIX["slack"])), key=lambda j: (pri[j], -j))
            s = max(f, ready[i])
            if best is None or s < best[0]:
                best = (s, i, q)
        if best is None:
            break
        s, i, q = best
        o = ops[i]
        cand[q].remove(i)
        order.append(i)
        start[i] = s
        end[i] = s + o["cost"]
        free[q] = s + (0.1 if o["done"] else o["cost"])
        for j in succ[i]:
            need[j] -= 1
            ready[j] = max(ready[j], end[i] + (hop if ops[j]["q"] != q else same) if i in ops[j]["hard"] else s)
            if not need[j]:
                cand.setdefault(ops[j]["q"], []).append(j)
    return order, start, end


def prices(ops, costs):
    gat, slow, hop, same, far, issue, first, table = costs
    cost = []
    for o in ops:
        q, n = o["q"], o["n"]
        if q in "VS" and not o["done"]:
            cost.append(0.055 + -n * CY * gat * slow if n < 0 else max(64, n) * CY * slow + MIX["call"])
        elif o["send"]:
            cost.append(issue + (first if o["send"] == "aS1_0" else 0.0))
        elif o["done"] == "d_EV0":
            cost.append(table)
        else:
            cost.append(n * MIX["pe"] * 1e-3 * slow + 0.03 if q == "T" else far if q == "R" else o["cost"] * (slow if q == "G" else 1.0))
    return cost, [0.0 if o["q"] == "R" else 0.1 if o["done"] else c for o, c in zip(ops, cost)]


def replay(ops, order, costs, price):
    hop, same = costs[2], costs[3]
    cost, hold = price
    free, end, user = {}, [0.0] * len(ops), {}
    for i in order:
        o = ops[i]
        q, b = o["q"], o["bank"]
        s = free.get(q, 0.0)
        for m in o["hard"]:
            e = end[m] + (same if ops[m]["q"] == q else hop)
            if e > s:
                s = e
        if b:
            u = user.setdefault(b, {})
            for q2, e in u.items():
                if q2 != q and e + hop > s:
                    s = e + hop
            u[q] = s + cost[i]
        end[i] = s + cost[i]
        if q != "R":
            free[q] = s + hold[i]
    return max(end)


def pack(ops, lst, hold, pred, base, hop):
    st, busy = [0.0] * len(ops), {}
    for j in lst:
        s = base[j]
        for i, d in pred[j]:
            if st[i] + d > s:
                s = st[i] + d
        h, q, b = hold[j], ops[j]["q"], ops[j]["bank"]
        if h:
            Q, B = busy.setdefault(q, []), busy.setdefault(b, []) if b else []
            while True:
                k = len(Q)
                while k and Q[k - 1][1] > s + 1e-9:
                    k -= 1
                while k < len(Q) and Q[k][0] < s + h - 1e-9:
                    s = Q[k][1]
                    k += 1
                late = [e + hop for a, e, q2 in B if q2 != q and a - hop < s + h - 1e-9 and e + hop > s + 1e-9]
                if not late:
                    break
                s = max(late)
            Q.insert(k, (s, s + h))
            B.append((s, s + h, q))
        st[j] = s
    return st


def ordered(key, pred):
    seen, out = [False] * len(key), []
    for j in sorted(range(len(key)), key=lambda i: key[i]):
        stack = [j]
        while stack:
            y = stack[-1]
            if seen[y]:
                stack.pop()
                continue
            m = [i for i, d in pred[y] if not seen[i]]
            if m:
                stack += m
            else:
                seen[y] = True
                out.append(y)
                stack.pop()
    return out


def refine(ops, st, rounds):
    n = len(ops)
    hop, same = COSTS[0][2], COSTS[0][3]
    price = [prices(ops, c) for c in COSTS]
    cost, hold = price[0]
    pred, back = [[] for _ in ops], [[] for _ in ops]
    for j, o in enumerate(ops):
        for i in o["hard"] | o["soft"]:
            d = cost[i] + (same if ops[i]["q"] == o["q"] else hop) if i in o["hard"] else hold[i]
            pred[j].append((i, d))
            back[i].append((j, d - hold[i] + hold[j]))
    zero, rest = [0.0] * n, [cost[i] - hold[i] for i in range(n)]
    seed, best = [MIX["seed"]], None
    big = [i for i in range(n) if ops[i]["n"] < 0]

    def draw():
        seed[0] = (seed[0] * 1103515245 + 12345) % 2147483648
        return seed[0] / 2147483648.0
    for r in range(rounds):
        if r > 2:
            mid, wide, amp, kind = draw() * max(best[1]), 3.0 + 17.0 * draw(), 0.1 + draw(), draw()
            if kind < 0.4:
                st = [s + amp * (2.0 * draw() - 1.0) if abs(s - mid) < wide else s for s in best[1]]
            elif kind < 0.7:
                c, amp = int(NCH * draw()), 8.0 * (draw() - 0.5)
                st = [s + amp if abs(s - mid) < wide and o["key"][1] == c else s for s, o in zip(best[1], ops)]
            else:
                st = list(best[1])
                for _ in range(1 + int(3 * draw())):
                    st[big[int(len(big) * draw())]] += 10.0 * (draw() - 0.5)
        rs = pack(ops, ordered([-st[i] - hold[i] for i in range(n)], back), hold, back, rest, hop)
        st = pack(ops, ordered([-rs[i] - hold[i] for i in range(n)], pred), hold, pred, zero, hop)
        order = ordered(st, pred)
        v = sum(math.log(replay(ops, order, c, p)) for c, p in zip(COSTS, price))
        if best is None or v < best[0]:
            best = (v, st, order)
    return best[2]


PLAN = {}


def plan(rounds=None):
    start = schedule(depend(build()))[1]
    ops = depend(build(), FREE)
    order = refine(ops, start, rounds or MIX["rounds"])
    user = {}
    for i in order:
        b, q = ops[i]["bank"], ops[i]["q"]
        if b:
            ops[i]["hard"] |= {m for q2, m in user.setdefault(b, {}).items() if q2 != q}
            user[b][q] = i
    return ops, order


def rank_program(g, core, T, topo):
    rank = T.rank_of(core)
    if rank is None:
        return
    if not PLAN:
        PLAN["ops"], PLAN["order"] = plan()
    ops, order = PLAN["ops"], PLAN["order"]
    place = {i: n for n, i in enumerate(order)}
    cores = T.cores
    to = {"next": cores[(rank + 1) % NR], "home": cores[(rank - 2) % NR]}
    sent = [0]

    def send(out, src, sem, where):
        dst = to[where]
        rid, pid, _ = topo.addr(dst)
        sent[0] += len(topo.engines(core, dst))
        return g.remote_dma(out_ap=out, in_ap=src, remote_sem=T.sem[sem], local_sem=T.sem["lsend"], pid=pid, routing_id=rid, dma_engine_mask=topo.mask(core, dst))

    x = {"send": send}
    eng = {"V": g.vector, "S": g.scalar, "T": g.tensor, "G": g, "Y": g.sync}
    count = {q: 0 for q in eng}
    know = {q: {} for q in eng}
    tok, clock, sems = {}, {}, {}
    for i in order:
        o = ops[i]
        q = o["q"]
        if q == "R":
            src = cores[(rank + o["frm"]) % NR]
            tok[i] = (o["done"], len(topo.engines(src, core)))
            clock[i] = {}
            sems[o["done"]] = tok[i][1]
            continue
        for m in sorted((m for m in o["hard"] if m in tok), key=lambda m: -place[m]):
            s, v = tok[m]
            if know[q].get(s, 0) < v:
                eng[q].wait_ge(T.sem[s], v)
                know[q][s] = v
                for a, b in clock[m].items():
                    if know[q].get(a, 0) < b:
                        know[q][a] = b
        ins = o["f"](g, T, x)
        clock[i] = dict(know[q])
        if o["done"]:
            ins.then_inc(T.sem[o["done"]], 16)
            tok[i] = (o["done"], 16)
            sems[o["done"]] = 16
        elif o["W"] and not o["send"]:
            count[q] += 1
            ins.then_inc(T.sem["q" + q], 1)
            tok[i] = ("q" + q, count[q])
            sems["q" + q] = count[q]
    for s, v in sems.items():
        if know["G"].get(s, 0) < v:
            g.wait_ge(T.sem[s], v)
    g.wait_ge(T.sem["lsend"], sent[0])
